import numpy as np
import ml_dtypes


def mxq(x, axis, fmt="e4m3"):
    dtype, down = {"e4m3": (ml_dtypes.float8_e4m3fn, 7), "e5m2": (ml_dtypes.float8_e5m2, 14)}[fmt]
    v = np.moveaxis(np.asarray(x, np.float32).astype(ml_dtypes.bfloat16).astype(np.float64), axis, -1)
    blocks = v.reshape(v.shape[:-1] + (-1, 32))
    amax = np.abs(blocks).max(-1, keepdims=True)
    byte = np.maximum(np.where(amax > 0, np.frexp(amax)[1] - 1 + 127, 0) - down, 1)
    scale = np.exp2(byte - 127.0)
    codes = (blocks / scale).astype(np.float32).astype(dtype).astype(np.float64)
    return np.moveaxis((codes * scale).reshape(v.shape), -1, axis)


WIDE = False


def mx_kscale(k):
    if not WIDE:
        return np.ones(k)
    levels = np.array([24, -24, 12, -12, 0])
    if k % 512:
        return np.exp2(np.random.permutation(np.resize(levels, k // 32))).repeat(32)
    a = np.empty((k // 512, 16))
    for p in range(k // 512):
        a[p, :8] = np.random.permutation(np.resize(levels, 8))
        for g in range(8):
            far = levels[np.abs(levels - a[p, g]) >= 10]
            a[p, g + 8] = far[np.random.randint(len(far))]
    return np.exp2(a.ravel()).repeat(32)


def f64(x):
    return np.asarray(x).astype(np.float64)


def striped(idx):
    return np.tile(idx.reshape(-1, 16).T, (8, 1)).astype(np.uint16)


def unstriped(offs):
    return offs[:16].T.reshape(-1).astype(np.int64)


E2M1 = np.array([0.0, 0.5, 1.0, 1.5, 2.0, 3.0, 4.0, 6.0, -0.0, -0.5, -1.0, -1.5, -2.0, -3.0, -4.0, -6.0])


def pack_weight(w, fmt):
    k, n = w.shape
    w = f64(np.asarray(w, np.float32).astype(ml_dtypes.bfloat16)).reshape(k // 32, 32, n)
    amax = np.abs(w).max(1)
    if fmt == "e4m3":
        byte = np.frexp(amax)[1] - 1 + 127 - 7
    else:
        mant, ex = np.frexp(amax / 6.0)
        byte = np.where(mant > 0.5, ex, ex - 1) + 127
    byte = np.clip(np.where(amax > 0, byte, 1), 1, 254)
    scaled = (w * np.exp2(127.0 - byte)[:, None, :]).reshape(k, n).astype(np.float32)
    by_word = np.ascontiguousarray(scaled.reshape(k // 512, 128, 4, n).transpose(0, 1, 3, 2))
    if fmt == "e4m3":
        words = by_word.astype(ml_dtypes.float8_e4m3fn).view(np.uint8)
    else:
        c = by_word.astype(ml_dtypes.float4_e2m1fn).view(np.uint8) & 0xF
        words = (c[..., 0::2] | (c[..., 1::2] << 4)).reshape(k // 512, 128, 2 * n)
    return np.ascontiguousarray(words), np.ascontiguousarray(byte.astype(np.uint8).reshape(k // 512, 16, n))


def unpack_weight(words, scales, fmt):
    g, _, n = scales.shape
    words = np.ascontiguousarray(words).reshape(g, 128, n, -1)
    if fmt == "e4m3":
        vals = words.view(ml_dtypes.float8_e4m3fn).astype(np.float64)
    else:
        nib = np.empty((g, 128, n, 4), np.uint8)
        nib[..., 0::2] = words & 0xF
        nib[..., 1::2] = words >> 4
        vals = E2M1[nib]
    vals = vals * np.repeat(np.exp2(scales.astype(np.float64) - 127.0), 8, axis=1)[..., None]
    return vals.transpose(0, 1, 3, 2).reshape(g * 512, n)


def sigm(f):
    return 1.0 / (1.0 + np.exp(-np.maximum(f, -700.0)))


K, N, T, J = 512, 512, 2048, 1024


def setup_inputs():
    n = np.random.standard_normal
    s = mx_kscale(K)[:, None]
    p_tab = pack_weight(n((K, T)) * s, "e4m3")
    p_wa = pack_weight(n((K, N)) / np.sqrt(2 * K) / s, "e4m3")
    p_wb = pack_weight(n((K, N)) / np.sqrt(2 * K) / s, "e4m3")
    p_wc = pack_weight(n((K, N)) / np.sqrt(K) / s, "e2m1")
    return {
        "tab_words": p_tab[0],
        "tab_scales": p_tab[1],
        "wa_words": p_wa[0],
        "wa_scales": p_wa[1],
        "wb_words": p_wb[0],
        "wb_scales": p_wb[1],
        "wc_words": p_wc[0],
        "wc_scales": p_wc[1],
        "wo": (n((K, N)) / np.sqrt(K) / s).astype(np.float32),
        "wgo": np.tile(np.random.uniform(0.5, 2.0, J), (128, 1)).astype(np.float32),
        "offs": striped(np.random.permutation(T)[:J]),
        "offs2": striped(np.random.permutation(T)[:J]),
    }


def reference(tab_words, tab_scales, wa_words, wa_scales, wb_words, wb_scales, wc_words, wc_scales, wo, wgo, offs, offs2):
    idx = unstriped(offs)
    idx2 = unstriped(offs2)
    tab_ = unpack_weight(tab_words, tab_scales, "e4m3")[:, idx]
    tabb_ = unpack_weight(tab_words, tab_scales, "e4m3")[:, idx2]
    wa_ = unpack_weight(wa_words, wa_scales, "e4m3")
    wb_ = unpack_weight(wb_words, wb_scales, "e4m3")
    za = wa_.T @ tabb_ + wb_.T @ tab_
    eta = sigm(za)
    wc_ = unpack_weight(wc_words, wc_scales, "e2m1")
    ms = wc_.T @ tab_
    wo_ = mxq(f64(wo), 0, "e4m3")
    ow = wo_.T @ tabb_
    out = np.zeros((N, T))
    out[:, idx2] = f64(wgo)[0] * (np.maximum(ow + eta * ms, 0.0))
    return out

@@ -1,0 +1,176 @@
+from contextlib import ExitStack
+
+import concourse.mybir as mybir
+
+K, N, T, J = 512, 512, 2048, 1024
+FLOPS = 4 * 2 * K * N * J
+
+F32 = mybir.dt.float32
+BF16 = mybir.dt.bfloat16
+I32 = mybir.dt.int32
+U32 = mybir.dt.uint32
+U16 = mybir.dt.uint16
+U8 = mybir.dt.uint8
+FP8X4 = mybir.dt.float8_e4m3fn_x4
+FP4X4 = mybir.dt.float4_e2m1fn_x4
+ACT = mybir.ActivationFunctionType
+ALU = mybir.AluOpType
+
+P = 128
+PACK = 4
+LANES = 16
+N_TILES = N // P
+QUARTER = J // 4
+HALF = J // 2
+
+
+def tile_list_rgg_ownrelu_kernel(
+    tc, tab_words, tab_scales, wa_words, wa_scales, wb_words, wb_scales, wc_words, wc_scales, wo, wgo, offs, offs2, out
+):
+    nc = tc.nc
+    with ExitStack() as ctx:
+        keep = ctx.enter_context(tc.tile_pool(name="keep", bufs=1))
+        work = ctx.enter_context(tc.tile_pool(name="work", bufs=3))
+        psum = ctx.enter_context(tc.psum_pool(name="psum", bufs=1))
+
+        src_list = keep.tile([P, J // LANES], U16, name="src_list")
+        dst_list = keep.tile([P, J // LANES], U16, name="dst_list")
+        table_words = keep.tile([P, T], I32, name="table_words", align_bytes=64)
+        table_scales = keep.tile([P, T // 4], I32, name="table_scales", align_bytes=64)
+        wa_codes = keep.tile([P, N], I32, name="wa_codes", align_bytes=64)
+        wb_codes = keep.tile([P, N], I32, name="wb_codes", align_bytes=64)
+        wc_codes = keep.tile([P, 2 * N], U8, name="wc_codes", align_bytes=64)
+        w_scales = keep.tile([P, 3 * N // 4], I32, name="w_scales", align_bytes=64)
+        wo_raw = keep.tile([P, PACK, N], F32, name="wo_raw")
+        wo_grouped = keep.tile([P, N, PACK], BF16, name="wo_grouped", align_bytes=64)
+        wo_codes = keep.tile([P, N], U32, name="wo_codes", align_bytes=64)
+        wo_scales = keep.tile([P, N], U8, name="wo_scales", align_bytes=64)
+        edge_w = keep.tile([P, J], F32, name="edge_w")
+        src_words = keep.tile([P, J], U32, name="src_words", align_bytes=64)
+        dst_words = keep.tile([P, J], U32, name="dst_words", align_bytes=64)
+        src_scales = keep.tile([P, J], U8, name="src_scales", align_bytes=64)
+        dst_scales = keep.tile([P, J], U8, name="dst_scales", align_bytes=64)
+        rows_out = [keep.tile([P, T], F32, name="rows_out%d" % b) for b in range(2)]
+        warm = keep.tile([P, 2], F32, name="warm")
+
+        nc.gpsimd.memset(table_scales[:], 0)
+        nc.gpsimd.memset(w_scales[:], 0)
+        nc.vector.memset(warm[:, 0:1], 0.0)
+        nc.scalar.activation(warm[:, 1:2], warm[:, 0:1], ACT.Sigmoid)
+
+        def load_scales(queue, plane, scales):
+            for r in range(4):
+                queue.dma_start(plane[r:P:32, :], scales[0, r:16:4, :].bitcast(I32))
+
+        def load_words(tile_i32, words):
+            nc.sync.dma_start(tile_i32, words[0].rearrange("p c i -> p (c i)").bitcast(I32))
+
+        wo_view = wo.rearrange("(p i) n -> p i n", i=PACK)
+
+        nc.sync.dma_start(dst_list[:], offs2)
+        nc.sync.dma_start(src_list[:], offs)
+        load_scales(nc.sync, table_scales, tab_scales)
+        load_words(table_words[:], tab_words)
+        load_words(wa_codes[:], wa_words)
+        load_words(wb_codes[:], wb_words)
+        nc.sync.dma_start(wc_codes[:].bitcast(I32), wc_words[0].bitcast(I32))
+        for w, (queue, scales) in enumerate(((nc.sync, wa_scales), (nc.sync, wb_scales), (nc.gpsimd, wc_scales))):
+            load_scales(queue, w_scales[:, w * N // 4 : (w + 1) * N // 4], scales)
+        nc.sync.dma_start(wo_raw[:, :, 0:P], wo_view[:, :, 0:P])
+        nc.sync.dma_start(edge_w[:, 0:HALF], wgo[:, 0:HALF])
+        nc.sync.dma_start(wo_raw[:, :, P:N], wo_view[:, :, P:N])
+        nc.sync.dma_start(edge_w[:, HALF:J], wgo[:, HALF:J])
+
+        nc.vector.memset(rows_out[0][:], 0.0)
+        for c in range(0, T, HALF):
+            nc.gpsimd.memset(rows_out[1][:, c : c + HALF], 0.0)
+
+        w_scale_bytes = w_scales[:].bitcast(U8)
+
+        def list_cols(j0, j1):
+            return slice(j0 // LANES, j1 // LANES)
+
+        def gather_scales(j0, j1):
+            for picked, lst in ((dst_scales, dst_list), (src_scales, src_list)):
+                nc.vector.tensor_copy(picked[:, j0:j1], table_scales[:].bitcast(U8).indirect(lst[:, list_cols(j0, j1)]))
+
+        def gather_words(j0, j1):
+            for picked, lst in ((dst_words, dst_list), (src_words, src_list)):
+                nc.vector.tensor_copy(picked[:, j0:j1], table_words[:].bitcast(U32).indirect(lst[:, list_cols(j0, j1)]))
+
+        def quantize_wo(n0, n1):
+            nc.scalar.copy(wo_grouped[:, n0:n1, :], wo_raw[:, :, n0:n1].rearrange("p i n -> p n i"))
+            nc.vector.quantize_mx(
+                out=wo_codes[:, n0:n1].bitcast(FP8X4),
+                scales=wo_scales[:, n0:n1],
+                in_=wo_grouped[:, n0:n1, :].rearrange("p n i -> p (n i)"),
+            )
+
+        def gate(nt, j0, j1):
+            width = j1 - j0
+            cols = slice(nt * P, (nt + 1) * P)
+            za = psum.tile([P, HALF], F32, name="za", bufs=3)
+            nc.tensor.matmul_mx(
+                out=za[:, 0:width], lhsT=wa_codes[:, cols].bitcast(FP8X4), lhsT_scale=w_scale_bytes[:, cols],
+                rhs=dst_words[:, j0:j1].bitcast(FP8X4), rhs_scale=dst_scales[:, j0:j1], start=True, stop=False,
+            )
+            nc.tensor.matmul_mx(
+                out=za[:, 0:width], lhsT=wb_codes[:, cols].bitcast(FP8X4),
+                lhsT_scale=w_scale_bytes[:, N + nt * P : N + (nt + 1) * P],
+                rhs=src_words[:, j0:j1].bitcast(FP8X4), rhs_scale=src_scales[:, j0:j1], start=False, stop=True,
+            )
+            ms = psum.tile([P, HALF], F32, name="ms", bufs=3)
+            nc.tensor.matmul_mx(
+                out=ms[:, 0:width], lhsT=wc_codes[:, 2 * nt * P : 2 * (nt + 1) * P].bitcast(FP4X4),
+                lhsT_scale=w_scale_bytes[:, 2 * N + nt * P : 2 * N + (nt + 1) * P],
+                rhs=src_words[:, j0:j1].bitcast(FP8X4), rhs_scale=src_scales[:, j0:j1], start=True, stop=True,
+            )
+            eta = work.tile([P, HALF], F32, name="eta")
+            nc.scalar.activation(eta[:, 0:width], za[:, 0:width], ACT.Sigmoid)
+            message = work.tile([P, HALF], F32, name="message")
+            nc.scalar.copy(message[:, 0:width], ms[:, 0:width])
+            gated = work.tile([P, HALF], F32, name="gated")
+            nc.gpsimd.tensor_tensor(gated[:, 0:width], eta[:, 0:width], message[:, 0:width], ALU.mult)
+            return gated
+
+        def finish(nt, j0, j1, gated, fuse_weight):
+            width = j1 - j0
+            cols = slice(nt * P, (nt + 1) * P)
+            ow = psum.tile([P, HALF], F32, name="ow", bufs=2)
+            nc.tensor.matmul_mx(
+                out=ow[:, 0:width], lhsT=wo_codes[:, cols].bitcast(FP8X4), lhsT_scale=wo_scales[:, cols],
+                rhs=dst_words[:, j0:j1].bitcast(FP8X4), rhs_scale=dst_scales[:, j0:j1], start=True, stop=True,
+            )
+            own = work.tile([P, HALF], F32, name="own")
+            nc.scalar.copy(own[:, 0:width], ow[:, 0:width])
+            total = work.tile([P, HALF], F32, name="total")
+            nc.gpsimd.tensor_tensor(total[:, 0:width], gated[:, 0:width], own[:, 0:width], ALU.add)
+            relu = work.tile([P, HALF], F32, name="relu")
+            nc.scalar.activation(relu[:, 0:width], total[:, 0:width], ACT.Relu)
+            window = rows_out[nt % 2][:].indirect(dst_list[:, list_cols(j0, j1)])
+            if fuse_weight:
+                nc.vector.tensor_tensor(window, relu[:, 0:width], edge_w[:, j0:j1], ALU.mult)
+            else:
+                weighted = work.tile([P, HALF], F32, name="weighted")
+                nc.gpsimd.tensor_tensor(weighted[:, 0:width], relu[:, 0:width], edge_w[:, j0:j1], ALU.mult)
+                nc.vector.tensor_copy(window, weighted[:, 0:width])
+            if j1 == J:
+                nc.sync.dma_start(out[cols, :], rows_out[nt % 2][:])
+
+        gather_scales(0, HALF)
+        gather_words(0, QUARTER)
+        quantize_wo(0, P)
+        gather_words(QUARTER, HALF)
+        gather_scales(HALF, 3 * QUARTER)
+        gather_words(HALF, 3 * QUARTER)
+        gather_scales(3 * QUARTER, J)
+        gather_words(3 * QUARTER, J)
+
+        units = [(0, q * QUARTER, (q + 1) * QUARTER) for q in range(4)]
+        units += [(nt, h * HALF, (h + 1) * HALF) for nt in range(1, N_TILES) for h in range(2)]
+        for u, (nt, j0, j1) in enumerate(units):
+            gated = gate(nt, j0, j1)
+            finish(nt, j0, j1, gated, u == len(units) - 1)
+            if u == 1:
+                quantize_wo(P, 2 * P)
+                quantize_wo(2 * P, N)

@@ -58,9 +58,9 @@ def tile_list_rgg_ownrelu_kernel(
         nc.vector.memset(warm[:, 0:1], 0.0)
         nc.scalar.activation(warm[:, 1:2], warm[:, 0:1], ACT.Sigmoid)
 
-        def load_scales(queue, plane, scales):
+        def load_scales(plane, scales):
             for r in range(4):
-                queue.dma_start(plane[r:P:32, :], scales[0, r:16:4, :].bitcast(I32))
+                nc.sync.dma_start(plane[r:P:32, :], scales[0, r:16:4, :].bitcast(I32))
 
         def load_words(tile_i32, words):
             nc.sync.dma_start(tile_i32, words[0].rearrange("p c i -> p (c i)").bitcast(I32))
@@ -69,21 +69,19 @@ def tile_list_rgg_ownrelu_kernel(
 
         nc.sync.dma_start(dst_list[:], offs2)
         nc.sync.dma_start(src_list[:], offs)
-        load_scales(nc.sync, table_scales, tab_scales)
+        load_scales(table_scales, tab_scales)
         load_words(table_words[:], tab_words)
+        for w, scales in enumerate((wa_scales, wb_scales, wc_scales)):
+            load_scales(w_scales[:, w * N // 4 : (w + 1) * N // 4], scales)
         load_words(wa_codes[:], wa_words)
         load_words(wb_codes[:], wb_words)
         nc.sync.dma_start(wc_codes[:].bitcast(I32), wc_words[0].bitcast(I32))
-        for w, (queue, scales) in enumerate(((nc.sync, wa_scales), (nc.sync, wb_scales), (nc.gpsimd, wc_scales))):
-            load_scales(queue, w_scales[:, w * N // 4 : (w + 1) * N // 4], scales)
         nc.sync.dma_start(wo_raw[:, :, 0:P], wo_view[:, :, 0:P])
-        nc.sync.dma_start(edge_w[:, 0:HALF], wgo[:, 0:HALF])
+        nc.sync.dma_start(edge_w[:], wgo)
         nc.sync.dma_start(wo_raw[:, :, P:N], wo_view[:, :, P:N])
-        nc.sync.dma_start(edge_w[:, HALF:J], wgo[:, HALF:J])
 
-        nc.vector.memset(rows_out[0][:], 0.0)
-        for c in range(0, T, HALF):
-            nc.gpsimd.memset(rows_out[1][:, c : c + HALF], 0.0)
+        for b in range(2):
+            nc.gpsimd.memset(rows_out[b][:], 0.0)
 
         w_scale_bytes = w_scales[:].bitcast(U8)
 
@@ -127,10 +125,8 @@ def tile_list_rgg_ownrelu_kernel(
             )
             eta = work.tile([P, HALF], F32, name="eta")
             nc.scalar.activation(eta[:, 0:width], za[:, 0:width], ACT.Sigmoid)
-            message = work.tile([P, HALF], F32, name="message")
-            nc.scalar.copy(message[:, 0:width], ms[:, 0:width])
             gated = work.tile([P, HALF], F32, name="gated")
-            nc.gpsimd.tensor_tensor(gated[:, 0:width], eta[:, 0:width], message[:, 0:width], ALU.mult)
+            nc.vector.tensor_tensor(gated[:, 0:width], ms[:, 0:width], eta[:, 0:width], ALU.mult)
             return gated
 
         def finish(nt, j0, j1, gated, fuse_weight):
@@ -141,36 +137,30 @@ def tile_list_rgg_ownrelu_kernel(
                 out=ow[:, 0:width], lhsT=wo_codes[:, cols].bitcast(FP8X4), lhsT_scale=wo_scales[:, cols],
                 rhs=dst_words[:, j0:j1].bitcast(FP8X4), rhs_scale=dst_scales[:, j0:j1], start=True, stop=True,
             )
-            own = work.tile([P, HALF], F32, name="own")
-            nc.scalar.copy(own[:, 0:width], ow[:, 0:width])
             total = work.tile([P, HALF], F32, name="total")
-            nc.gpsimd.tensor_tensor(total[:, 0:width], gated[:, 0:width], own[:, 0:width], ALU.add)
-            relu = work.tile([P, HALF], F32, name="relu")
-            nc.scalar.activation(relu[:, 0:width], total[:, 0:width], ACT.Relu)
+            nc.vector.tensor_tensor(total[:, 0:width], ow[:, 0:width], gated[:, 0:width], ALU.add)
             window = rows_out[nt % 2][:].indirect(dst_list[:, list_cols(j0, j1)])
             if fuse_weight:
+                relu = work.tile([P, HALF], F32, name="relu")
+                nc.scalar.activation(relu[:, 0:width], total[:, 0:width], ACT.Relu)
                 nc.vector.tensor_tensor(window, relu[:, 0:width], edge_w[:, j0:j1], ALU.mult)
             else:
                 weighted = work.tile([P, HALF], F32, name="weighted")
-                nc.gpsimd.tensor_tensor(weighted[:, 0:width], relu[:, 0:width], edge_w[:, j0:j1], ALU.mult)
+                nc.vector.scalar_tensor_tensor(weighted[:, 0:width], total[:, 0:width], 0.0, edge_w[:, j0:j1], ALU.max, ALU.mult)
                 nc.vector.tensor_copy(window, weighted[:, 0:width])
             if j1 == J:
                 nc.sync.dma_start(out[cols, :], rows_out[nt % 2][:])
 
         gather_scales(0, HALF)
-        gather_words(0, QUARTER)
+        gather_words(0, HALF)
+        gather_scales(HALF, J)
         quantize_wo(0, P)
-        gather_words(QUARTER, HALF)
-        gather_scales(HALF, 3 * QUARTER)
-        gather_words(HALF, 3 * QUARTER)
-        gather_scales(3 * QUARTER, J)
-        gather_words(3 * QUARTER, J)
+        gather_words(HALF, J)
 
-        units = [(0, q * QUARTER, (q + 1) * QUARTER) for q in range(4)]
-        units += [(nt, h * HALF, (h + 1) * HALF) for nt in range(1, N_TILES) for h in range(2)]
+        units = [(nt, h * HALF, (h + 1) * HALF) for nt in range(N_TILES) for h in range(2)]
         for u, (nt, j0, j1) in enumerate(units):
             gated = gate(nt, j0, j1)
-            finish(nt, j0, j1, gated, u == len(units) - 1)
-            if u == 1:
+            finish(nt, j0, j1, gated, False)
+            if u == 0:
                 quantize_wo(P, 2 * P)
                 quantize_wo(2 * P, N)

@@ -22,6 +22,7 @@ LANES = 16
 N_TILES = N // P
 QUARTER = J // 4
 HALF = J // 2
+G_GATES = 2
 
 
 def tile_list_rgg_ownrelu_kernel(
@@ -30,7 +31,7 @@ def tile_list_rgg_ownrelu_kernel(
     nc = tc.nc
     with ExitStack() as ctx:
         keep = ctx.enter_context(tc.tile_pool(name="keep", bufs=1))
-        work = ctx.enter_context(tc.tile_pool(name="work", bufs=3))
+        work = ctx.enter_context(tc.tile_pool(name="work", bufs=9))
         psum = ctx.enter_context(tc.psum_pool(name="psum", bufs=1))
 
         src_list = keep.tile([P, J // LANES], U16, name="src_list")
@@ -53,36 +54,40 @@ def tile_list_rgg_ownrelu_kernel(
         rows_out = [keep.tile([P, T], F32, name="rows_out%d" % b) for b in range(2)]
         warm = keep.tile([P, 2], F32, name="warm")
 
-        nc.gpsimd.memset(table_scales[:], 0)
-        nc.gpsimd.memset(w_scales[:], 0)
-        nc.vector.memset(warm[:, 0:1], 0.0)
+        nc.gpsimd.memset(warm[:, 0:1], 0.0)
         nc.scalar.activation(warm[:, 1:2], warm[:, 0:1], ACT.Sigmoid)
 
-        def load_scales(plane, scales):
-            for r in range(4):
-                nc.sync.dma_start(plane[r:P:32, :], scales[0, r:16:4, :].bitcast(I32))
+        def load_scales(plane, scales, quadrants):
+            rows = scales[0].bitcast(I32)
+            for q in quadrants:
+                quadrant_rows = rows[4 * q : 4 * (q + 1), :].unsqueeze(0).broadcast_to([8, 4, rows.shape[1]])
+                nc.sync.dma_start(plane[32 * q : 32 * (q + 1), :], quadrant_rows)
 
         def load_words(tile_i32, words):
             nc.sync.dma_start(tile_i32, words[0].rearrange("p c i -> p (c i)").bitcast(I32))
 
-        wo_view = wo.rearrange("(p i) n -> p i n", i=PACK)
-
         nc.sync.dma_start(dst_list[:], offs2)
-        nc.sync.dma_start(src_list[:], offs)
-        load_scales(table_scales, tab_scales)
+        load_scales(table_scales, tab_scales, range(4))
         load_words(table_words[:], tab_words)
-        for w, scales in enumerate((wa_scales, wb_scales, wc_scales)):
-            load_scales(w_scales[:, w * N // 4 : (w + 1) * N // 4], scales)
-        load_words(wa_codes[:], wa_words)
+        nc.sync.dma_start(src_list[:], offs)
+        wo_rows = wo.rearrange("(p i) n -> p i n", i=PACK)
+        nc.sync.dma_start(wo_raw[:, :, 0:P], wo_rows[:, :, 0:P])
+        load_scales(w_scales[:, N // 2 : 3 * N // 4], wc_scales, range(4))
+        load_scales(w_scales[:, N // 4 : N // 2], wb_scales, range(2))
         load_words(wb_codes[:], wb_words)
-        nc.sync.dma_start(wc_codes[:].bitcast(I32), wc_words[0].bitcast(I32))
-        nc.sync.dma_start(wo_raw[:, :, 0:P], wo_view[:, :, 0:P])
+        load_words(wa_codes[:], wa_words)
+        load_scales(w_scales[:, N // 4 : N // 2], wb_scales, range(2, 4))
+        load_scales(w_scales[:, 0 : N // 4], wa_scales, range(4))
         nc.sync.dma_start(edge_w[:], wgo)
-        nc.sync.dma_start(wo_raw[:, :, P:N], wo_view[:, :, P:N])
+        nc.sync.dma_start(wo_raw[:, :, P:N], wo_rows[:, :, P:N])
 
-        for b in range(2):
-            nc.gpsimd.memset(rows_out[b][:], 0.0)
+        nc.vector.memset(rows_out[0][:], 0.0)
+        for c in range(0, T, HALF):
+            nc.gpsimd.memset(rows_out[1][:, c : c + HALF], 0.0)
+        nc.gpsimd.dma_start(wc_codes[:].bitcast(I32), wc_words[0].bitcast(I32))
 
+        gate_banks = [psum.tile([P, HALF], F32, name="gate_bank%d" % b) for b in range(4)]
+        message_banks = [psum.tile([P, HALF], F32, name="message_bank%d" % b) for b in range(4)]
         w_scale_bytes = w_scales[:].bitcast(U8)
 
         def list_cols(j0, j1):
@@ -104,52 +109,61 @@ def tile_list_rgg_ownrelu_kernel(
                 in_=wo_grouped[:, n0:n1, :].rearrange("p n i -> p (n i)"),
             )
 
-        def gate(nt, j0, j1):
-            width = j1 - j0
+        def gate(nt, j0, za, ms, message):
+            j1 = j0 + HALF
             cols = slice(nt * P, (nt + 1) * P)
-            za = psum.tile([P, HALF], F32, name="za", bufs=3)
             nc.tensor.matmul_mx(
-                out=za[:, 0:width], lhsT=wa_codes[:, cols].bitcast(FP8X4), lhsT_scale=w_scale_bytes[:, cols],
+                out=za[:], lhsT=wa_codes[:, cols].bitcast(FP8X4), lhsT_scale=w_scale_bytes[:, cols],
                 rhs=dst_words[:, j0:j1].bitcast(FP8X4), rhs_scale=dst_scales[:, j0:j1], start=True, stop=False,
             )
             nc.tensor.matmul_mx(
-                out=za[:, 0:width], lhsT=wb_codes[:, cols].bitcast(FP8X4),
+                out=za[:], lhsT=wb_codes[:, cols].bitcast(FP8X4),
                 lhsT_scale=w_scale_bytes[:, N + nt * P : N + (nt + 1) * P],
                 rhs=src_words[:, j0:j1].bitcast(FP8X4), rhs_scale=src_scales[:, j0:j1], start=False, stop=True,
             )
-            ms = psum.tile([P, HALF], F32, name="ms", bufs=3)
             nc.tensor.matmul_mx(
-                out=ms[:, 0:width], lhsT=wc_codes[:, 2 * nt * P : 2 * (nt + 1) * P].bitcast(FP4X4),
+                out=ms[:], lhsT=wc_codes[:, 2 * nt * P : 2 * (nt + 1) * P].bitcast(FP4X4),
                 lhsT_scale=w_scale_bytes[:, 2 * N + nt * P : 2 * N + (nt + 1) * P],
                 rhs=src_words[:, j0:j1].bitcast(FP8X4), rhs_scale=src_scales[:, j0:j1], start=True, stop=True,
             )
             eta = work.tile([P, HALF], F32, name="eta")
-            nc.scalar.activation(eta[:, 0:width], za[:, 0:width], ACT.Sigmoid)
+            nc.scalar.activation(eta[:], za[:], ACT.Sigmoid)
             gated = work.tile([P, HALF], F32, name="gated")
-            nc.vector.tensor_tensor(gated[:, 0:width], ms[:, 0:width], eta[:, 0:width], ALU.mult)
+            if message is None:
+                nc.vector.tensor_tensor(gated[:], ms[:], eta[:], ALU.mult)
+            else:
+                nc.scalar.copy(message[:], ms[:])
+                nc.gpsimd.tensor_tensor(gated[:], message[:], eta[:], ALU.mult)
             return gated
 
-        def finish(nt, j0, j1, gated, fuse_weight):
+        def finish(nt, j0, j1, ow, gated, fuse_weight):
             width = j1 - j0
             cols = slice(nt * P, (nt + 1) * P)
-            ow = psum.tile([P, HALF], F32, name="ow", bufs=2)
             nc.tensor.matmul_mx(
-                out=ow[:, 0:width], lhsT=wo_codes[:, cols].bitcast(FP8X4), lhsT_scale=wo_scales[:, cols],
+                out=ow, lhsT=wo_codes[:, cols].bitcast(FP8X4), lhsT_scale=wo_scales[:, cols],
                 rhs=dst_words[:, j0:j1].bitcast(FP8X4), rhs_scale=dst_scales[:, j0:j1], start=True, stop=True,
             )
+            own = work.tile([P, HALF], F32, name="own")
+            nc.scalar.copy(own[:, 0:width], ow)
             total = work.tile([P, HALF], F32, name="total")
-            nc.vector.tensor_tensor(total[:, 0:width], ow[:, 0:width], gated[:, 0:width], ALU.add)
+            nc.gpsimd.tensor_tensor(total[:, 0:width], gated, own[:, 0:width], ALU.add)
+            relu = work.tile([P, HALF], F32, name="relu")
+            nc.scalar.activation(relu[:, 0:width], total[:, 0:width], ACT.Relu)
+            relus.append(relu)
+            if fuse_weight:
+                return relu[:, 0:width]
+            weighted = work.tile([P, HALF], F32, name="weighted")
+            nc.gpsimd.tensor_tensor(weighted[:, 0:width], relu[:, 0:width], edge_w[:, j0:j1], ALU.mult)
+            return weighted[:, 0:width]
+
+        def scatter(nt, j0, j1, values, fuse_weight):
             window = rows_out[nt % 2][:].indirect(dst_list[:, list_cols(j0, j1)])
             if fuse_weight:
-                relu = work.tile([P, HALF], F32, name="relu")
-                nc.scalar.activation(relu[:, 0:width], total[:, 0:width], ACT.Relu)
-                nc.vector.tensor_tensor(window, relu[:, 0:width], edge_w[:, j0:j1], ALU.mult)
+                nc.vector.tensor_tensor(window, values, edge_w[:, j0:j1], ALU.mult)
             else:
-                weighted = work.tile([P, HALF], F32, name="weighted")
-                nc.vector.scalar_tensor_tensor(weighted[:, 0:width], total[:, 0:width], 0.0, edge_w[:, j0:j1], ALU.max, ALU.mult)
-                nc.vector.tensor_copy(window, weighted[:, 0:width])
+                nc.vector.tensor_copy(window, values)
             if j1 == J:
-                nc.sync.dma_start(out[cols, :], rows_out[nt % 2][:])
+                nc.sync.dma_start(out[nt * P : (nt + 1) * P, :], rows_out[nt % 2][:])
 
         gather_scales(0, HALF)
         gather_words(0, HALF)
@@ -157,10 +171,32 @@ def tile_list_rgg_ownrelu_kernel(
         quantize_wo(0, P)
         gather_words(HALF, J)
 
-        units = [(nt, h * HALF, (h + 1) * HALF) for nt in range(N_TILES) for h in range(2)]
-        for u, (nt, j0, j1) in enumerate(units):
-            gated = gate(nt, j0, j1)
-            finish(nt, j0, j1, gated, False)
-            if u == 0:
-                quantize_wo(P, 2 * P)
-                quantize_wo(2 * P, N)
+        pieces = []
+        relus = []
+
+        def piece(nt, j0, j1, bank, gated):
+            last = nt == N_TILES - 1 and j1 == J
+            values = finish(nt, j0, j1, gate_banks[bank][:, 0 : j1 - j0], gated, last)
+            pieces.append((nt, j0, j1, values, last))
+
+        g00 = gate(0, 0, gate_banks[0], message_banks[0], None)
+        g10 = gate(1, 0, gate_banks[1], message_banks[1], None)
+        piece(0, 0, QUARTER, 0, g00[:, 0:QUARTER])
+        piece(0, QUARTER, HALF, 1, g00[:, QUARTER:HALF])
+        g01 = gate(0, HALF, gate_banks[2], message_banks[0], None)
+        g20 = gate(2, 0, gate_banks[3], message_banks[2], None)
+        piece(0, HALF, J, 0, g01[:])
+        quantize_wo(P, 2 * P)
+        piece(1, 0, HALF, 1, g10[:])
+        g11 = gate(1, HALF, gate_banks[2], message_banks[1], None)
+        piece(1, HALF, J, 3, g11[:])
+        quantize_wo(2 * P, N)
+        piece(2, 0, HALF, 0, g20[:])
+        g21 = gate(2, HALF, gate_banks[1], message_banks[2], relus[2])
+        piece(2, HALF, J, 2, g21[:])
+        g30 = gate(3, 0, gate_banks[3], message_banks[3], relus[3])
+        piece(3, 0, HALF, 0, g30[:])
+        g31 = gate(3, HALF, gate_banks[1], message_banks[3], relus[4])
+        piece(3, HALF, J, 2, g31[:])
+        for args in pieces:
+            scatter(*args)

@@ -1,6 +1,7 @@
 from contextlib import ExitStack
 
 import concourse.mybir as mybir
+from concourse.masks import make_identity
 
 K, N, T, J = 512, 512, 2048, 1024
 FLOPS = 4 * 2 * K * N * J
@@ -19,10 +20,9 @@ ALU = mybir.AluOpType
 P = 128
 PACK = 4
 LANES = 16
-N_TILES = N // P
-QUARTER = J // 4
 HALF = J // 2
-G_GATES = 2
+E_TILES = HALF // P
+OUT_TILES = 2
 
 
 def tile_list_rgg_ownrelu_kernel(
@@ -31,172 +31,183 @@ def tile_list_rgg_ownrelu_kernel(
     nc = tc.nc
     with ExitStack() as ctx:
         keep = ctx.enter_context(tc.tile_pool(name="keep", bufs=1))
-        work = ctx.enter_context(tc.tile_pool(name="work", bufs=9))
-        psum = ctx.enter_context(tc.psum_pool(name="psum", bufs=1))
+        shared = ctx.enter_context(tc.tile_pool(name="shared", bufs=1))
+        work = ctx.enter_context(tc.tile_pool(name="work", bufs=8))
+        psum = ctx.enter_context(tc.psum_pool(name="psum", bufs=2))
 
         src_list = keep.tile([P, J // LANES], U16, name="src_list")
         dst_list = keep.tile([P, J // LANES], U16, name="dst_list")
         table_words = keep.tile([P, T], I32, name="table_words", align_bytes=64)
-        table_scales = keep.tile([P, T // 4], I32, name="table_scales", align_bytes=64)
+        table_scales = keep.tile([P, T // 4], I32, name="table_scales", tag="table_scales", align_bytes=64)
         wa_codes = keep.tile([P, N], I32, name="wa_codes", align_bytes=64)
         wb_codes = keep.tile([P, N], I32, name="wb_codes", align_bytes=64)
         wc_codes = keep.tile([P, 2 * N], U8, name="wc_codes", align_bytes=64)
-        w_scales = keep.tile([P, 3 * N // 4], I32, name="w_scales", align_bytes=64)
-        wo_raw = keep.tile([P, PACK, N], F32, name="wo_raw")
-        wo_grouped = keep.tile([P, N, PACK], BF16, name="wo_grouped", align_bytes=64)
+        wa_plane = keep.tile([P, N // 4], I32, name="wa_plane", align_bytes=64)
+        wb_plane = keep.tile([P, N // 4], I32, name="wb_plane", align_bytes=64)
+        wc_plane = keep.tile([P, N // 4], I32, name="wc_plane", align_bytes=64)
+        wo_raw = [
+            keep.tile([P, PACK, P], F32, name="wo_raw0"),
+            keep.tile([P, PACK, P], F32, name="wo_raw1"),
+            keep.tile([P, PACK, 2 * P], F32, name="wo_raw2"),
+        ]
         wo_codes = keep.tile([P, N], U32, name="wo_codes", align_bytes=64)
         wo_scales = keep.tile([P, N], U8, name="wo_scales", align_bytes=64)
-        edge_w = keep.tile([P, J], F32, name="edge_w")
-        src_words = keep.tile([P, J], U32, name="src_words", align_bytes=64)
-        dst_words = keep.tile([P, J], U32, name="dst_words", align_bytes=64)
-        src_scales = keep.tile([P, J], U8, name="src_scales", align_bytes=64)
-        dst_scales = keep.tile([P, J], U8, name="dst_scales", align_bytes=64)
-        rows_out = [keep.tile([P, T], F32, name="rows_out%d" % b) for b in range(2)]
+        edge_w = [keep.tile([P, HALF], F32, name="edge_w%d" % h) for h in range(2)]
+        src_words = []
+        dst_words = [keep.tile([P, HALF], U32, name="dst_words0", align_bytes=64)]
+        src_scales = [keep.tile([P, HALF], U8, name="src_scales0", align_bytes=64)]
+        dst_scales = [keep.tile([P, HALF], U8, name="dst_scales%d" % h, align_bytes=64) for h in range(2)]
+        rows_out = [keep.tile([P, T], F32, name="rows_out%d" % b) for b in range(OUT_TILES - 1)]
+        identity = keep.tile([P, P], F32, name="identity")
         warm = keep.tile([P, 2], F32, name="warm")
 
         nc.gpsimd.memset(warm[:, 0:1], 0.0)
         nc.scalar.activation(warm[:, 1:2], warm[:, 0:1], ACT.Sigmoid)
 
-        def load_scales(plane, scales, quadrants):
+        def load_scales(plane, scales, quadrants, queue):
             rows = scales[0].bitcast(I32)
             for q in quadrants:
                 quadrant_rows = rows[4 * q : 4 * (q + 1), :].unsqueeze(0).broadcast_to([8, 4, rows.shape[1]])
-                nc.sync.dma_start(plane[32 * q : 32 * (q + 1), :], quadrant_rows)
+                queue.dma_start(plane[32 * q : 32 * (q + 1), :], quadrant_rows)
 
         def load_words(tile_i32, words):
             nc.sync.dma_start(tile_i32, words[0].rearrange("p c i -> p (c i)").bitcast(I32))
 
-        nc.sync.dma_start(dst_list[:], offs2)
-        load_scales(table_scales, tab_scales, range(4))
-        load_words(table_words[:], tab_words)
-        nc.sync.dma_start(src_list[:], offs)
         wo_rows = wo.rearrange("(p i) n -> p i n", i=PACK)
-        nc.sync.dma_start(wo_raw[:, :, 0:P], wo_rows[:, :, 0:P])
-        load_scales(w_scales[:, N // 2 : 3 * N // 4], wc_scales, range(4))
-        load_scales(w_scales[:, N // 4 : N // 2], wb_scales, range(2))
-        load_words(wb_codes[:], wb_words)
+        nc.sync.dma_start(dst_list[:], offs2)
+        load_scales(table_scales, tab_scales, range(4), nc.sync)
+        nc.sync.dma_start(src_list[:], offs)
+        load_scales(wa_plane, wa_scales, range(1), nc.sync)
+        load_words(table_words[:], tab_words)
+        load_scales(wc_plane, wc_scales, range(4), nc.gpsimd)
+        nc.sync.dma_start(wo_raw[0][:], wo_rows[:, :, 0:P])
+        load_scales(wa_plane, wa_scales, range(1, 4), nc.sync)
+        nc.sync.dma_start(wc_codes[:].bitcast(I32), wc_words[0].bitcast(I32))
         load_words(wa_codes[:], wa_words)
-        load_scales(w_scales[:, N // 4 : N // 2], wb_scales, range(2, 4))
-        load_scales(w_scales[:, 0 : N // 4], wa_scales, range(4))
-        nc.sync.dma_start(edge_w[:], wgo)
-        nc.sync.dma_start(wo_raw[:, :, P:N], wo_rows[:, :, P:N])
+        load_words(wb_codes[:], wb_words)
+        load_scales(wb_plane, wb_scales, range(4), nc.sync)
+        nc.sync.dma_start(wo_raw[1][:], wo_rows[:, :, P : 2 * P])
+        nc.sync.dma_start(edge_w[0][:], wgo[:, 0:HALF])
+        nc.sync.dma_start(wo_raw[2][:], wo_rows[:, :, 2 * P : N])
+        nc.sync.dma_start(edge_w[1][:], wgo[:, HALF:J])
 
+        make_identity(nc, identity[:])
         nc.vector.memset(rows_out[0][:], 0.0)
-        for c in range(0, T, HALF):
-            nc.gpsimd.memset(rows_out[1][:, c : c + HALF], 0.0)
-        nc.gpsimd.dma_start(wc_codes[:].bitcast(I32), wc_words[0].bitcast(I32))
 
-        gate_banks = [psum.tile([P, HALF], F32, name="gate_bank%d" % b) for b in range(4)]
-        message_banks = [psum.tile([P, HALF], F32, name="message_bank%d" % b) for b in range(4)]
-        w_scale_bytes = w_scales[:].bitcast(U8)
+        def list_cols(h):
+            return slice(h * HALF // LANES, (h + 1) * HALF // LANES)
 
-        def list_cols(j0, j1):
-            return slice(j0 // LANES, j1 // LANES)
+        def gather_scales(picked, lst, h):
+            nc.vector.tensor_copy(picked[h][:], table_scales[:].bitcast(U8).indirect(lst[:, list_cols(h)]))
 
-        def gather_scales(j0, j1):
-            for picked, lst in ((dst_scales, dst_list), (src_scales, src_list)):
-                nc.vector.tensor_copy(picked[:, j0:j1], table_scales[:].bitcast(U8).indirect(lst[:, list_cols(j0, j1)]))
+        def gather_words(picked, lst, h):
+            nc.vector.tensor_copy(picked[h][:], table_words[:].bitcast(U32).indirect(lst[:, list_cols(h)]))
 
-        def gather_words(j0, j1):
-            for picked, lst in ((dst_words, dst_list), (src_words, src_list)):
-                nc.vector.tensor_copy(picked[:, j0:j1], table_words[:].bitcast(U32).indirect(lst[:, list_cols(j0, j1)]))
-
-        def quantize_wo(n0, n1):
-            nc.scalar.copy(wo_grouped[:, n0:n1, :], wo_raw[:, :, n0:n1].rearrange("p i n -> p n i"))
+        def quantize_wo(n0, raw, grouped):
+            n1 = n0 + raw.shape[2]
+            nc.scalar.copy(grouped, raw[:].rearrange("p i n -> p n i"))
             nc.vector.quantize_mx(
                 out=wo_codes[:, n0:n1].bitcast(FP8X4),
                 scales=wo_scales[:, n0:n1],
-                in_=wo_grouped[:, n0:n1, :].rearrange("p n i -> p (n i)"),
+                in_=grouped.rearrange("p n i -> p (n i)"),
             )
 
-        def gate(nt, j0, za, ms, message):
-            j1 = j0 + HALF
+        def product(bank, e, words, scales, w_codes, w_scales, start, stop):
+            edges = slice(e * P, (e + 1) * P)
+            nc.tensor.matmul_mx(
+                out=bank[:, edges], lhsT=words[:, edges].bitcast(FP8X4), lhsT_scale=scales[:, edges],
+                rhs=w_codes, rhs_scale=w_scales, start=start, stop=stop,
+            )
+
+        def gate_products(u, nt, h):
             cols = slice(nt * P, (nt + 1) * P)
-            nc.tensor.matmul_mx(
-                out=za[:], lhsT=wa_codes[:, cols].bitcast(FP8X4), lhsT_scale=w_scale_bytes[:, cols],
-                rhs=dst_words[:, j0:j1].bitcast(FP8X4), rhs_scale=dst_scales[:, j0:j1], start=True, stop=False,
-            )
-            nc.tensor.matmul_mx(
-                out=za[:], lhsT=wb_codes[:, cols].bitcast(FP8X4),
-                lhsT_scale=w_scale_bytes[:, N + nt * P : N + (nt + 1) * P],
-                rhs=src_words[:, j0:j1].bitcast(FP8X4), rhs_scale=src_scales[:, j0:j1], start=False, stop=True,
-            )
-            nc.tensor.matmul_mx(
-                out=ms[:], lhsT=wc_codes[:, 2 * nt * P : 2 * (nt + 1) * P].bitcast(FP4X4),
-                lhsT_scale=w_scale_bytes[:, 2 * N + nt * P : 2 * N + (nt + 1) * P],
-                rhs=src_words[:, j0:j1].bitcast(FP8X4), rhs_scale=src_scales[:, j0:j1], start=True, stop=True,
-            )
-            eta = work.tile([P, HALF], F32, name="eta")
+            za = psum.tile([P, HALF], F32, name="za%d" % u, tag="sum_bank%d" % (u % 3), bufs=1)
+            ms = psum.tile([P, HALF], F32, name="ms", bufs=3)
+            for e in range(E_TILES):
+                product(ms, e, src_words[h], src_scales[h], wc_codes[:, 2 * nt * P : 2 * (nt + 1) * P].bitcast(FP4X4),
+                        wc_plane[:].bitcast(U8)[:, cols], True, True)
+            for e in range(E_TILES):
+                product(za, e, dst_words[h], dst_scales[h], wa_codes[:, cols].bitcast(FP8X4),
+                        wa_plane[:].bitcast(U8)[:, cols], True, False)
+                product(za, e, src_words[h], src_scales[h], wb_codes[:, cols].bitcast(FP8X4),
+                        wb_plane[:].bitcast(U8)[:, cols], False, True)
+            eta = keep.tile([P, HALF], F32, name="eta%d" % u, tag="eta%d" % u, align_bytes=64)
             nc.scalar.activation(eta[:], za[:], ACT.Sigmoid)
-            gated = work.tile([P, HALF], F32, name="gated")
-            if message is None:
-                nc.vector.tensor_tensor(gated[:], ms[:], eta[:], ALU.mult)
-            else:
-                nc.scalar.copy(message[:], ms[:])
-                nc.gpsimd.tensor_tensor(gated[:], message[:], eta[:], ALU.mult)
+            return ms, eta
+
+        def own_product(nt, h):
+            cols = slice(nt * P, (nt + 1) * P)
+            ow = psum.tile([P, HALF], F32, name="ow")
+            for e in range(E_TILES):
+                product(ow, e, dst_words[h], dst_scales[h], wo_codes[:, cols].bitcast(FP8X4), wo_scales[:, cols], True, True)
+            own = work.tile([P, HALF], F32, name="own")
+            nc.scalar.copy(own[:], ow[:])
+            return own
+
+        def gate(u, ms, eta):
+            gated = keep.tile([P, HALF], F32, name="gated%d" % u, tag="gated%d" % u, align_bytes=64)
+            nc.vector.tensor_tensor(gated[:], ms[:], eta[:], ALU.mult)
             return gated
 
-        def finish(nt, j0, j1, ow, gated, fuse_weight):
-            width = j1 - j0
-            cols = slice(nt * P, (nt + 1) * P)
-            nc.tensor.matmul_mx(
-                out=ow, lhsT=wo_codes[:, cols].bitcast(FP8X4), lhsT_scale=wo_scales[:, cols],
-                rhs=dst_words[:, j0:j1].bitcast(FP8X4), rhs_scale=dst_scales[:, j0:j1], start=True, stop=True,
-            )
-            own = work.tile([P, HALF], F32, name="own")
-            nc.scalar.copy(own[:, 0:width], ow)
-            total = work.tile([P, HALF], F32, name="total")
-            nc.gpsimd.tensor_tensor(total[:, 0:width], gated, own[:, 0:width], ALU.add)
+        def turn_own(u, own):
+            total = psum.tile([P, HALF], F32, name="total%d" % u, tag="sum_bank%d" % ((u + 1) % 3 if u else 0), bufs=1)
+            for e in range(E_TILES):
+                edges = slice(e * P, (e + 1) * P)
+                nc.tensor.matmul(total[:, edges], own[:, edges], identity[:], start=e == 0, stop=False, is_transpose=True)
+            return total
+
+        def add_gated(total, gated):
+            for e in range(E_TILES):
+                edges = slice(e * P, (e + 1) * P)
+                nc.tensor.matmul(total[:, edges], gated[:, edges], identity[:], start=False, stop=e == E_TILES - 1, is_transpose=True)
             relu = work.tile([P, HALF], F32, name="relu")
-            nc.scalar.activation(relu[:, 0:width], total[:, 0:width], ACT.Relu)
-            relus.append(relu)
-            if fuse_weight:
-                return relu[:, 0:width]
-            weighted = work.tile([P, HALF], F32, name="weighted")
-            nc.gpsimd.tensor_tensor(weighted[:, 0:width], relu[:, 0:width], edge_w[:, j0:j1], ALU.mult)
-            return weighted[:, 0:width]
+            nc.scalar.activation(relu[:], total[:], ACT.Relu)
+            return relu
 
-        def scatter(nt, j0, j1, values, fuse_weight):
-            window = rows_out[nt % 2][:].indirect(dst_list[:, list_cols(j0, j1)])
-            if fuse_weight:
-                nc.vector.tensor_tensor(window, values, edge_w[:, j0:j1], ALU.mult)
-            else:
-                nc.vector.tensor_copy(window, values)
-            if j1 == J:
-                nc.sync.dma_start(out[nt * P : (nt + 1) * P, :], rows_out[nt % 2][:])
+        def scatter(nt, h, relu):
+            rows = rows_out[nt % OUT_TILES]
+            nc.vector.tensor_tensor(
+                rows[:].indirect(dst_list[:, list_cols(h)]), relu[:], edge_w[h][:], ALU.mult
+            )
+            if h == 1:
+                nc.sync.dma_start(out[nt * P : (nt + 1) * P, :], rows[:])
 
-        gather_scales(0, HALF)
-        gather_words(0, HALF)
-        gather_scales(HALF, J)
-        quantize_wo(0, P)
-        gather_words(HALF, J)
+        gather_scales(dst_scales, dst_list, 0)
+        gather_scales(src_scales, src_list, 0)
+        gather_scales(dst_scales, dst_list, 1)
+        gather_words(dst_words, dst_list, 0)
+        grouped_head = shared.tile([P, 2 * P + 32, PACK], BF16, name="grouped_head", offset=1920, align_bytes=64)
+        quantize_wo(0, wo_raw[0], grouped_head[:, 0:P, :])
+        src_words.append(shared.tile([P, HALF], U32, name="src_words0", offset=4096, align_bytes=64))
+        gather_words(src_words, src_list, 0)
+        dst_words.append(shared.tile([P, HALF], U32, name="dst_words1", offset=0, align_bytes=64))
+        gather_words(dst_words, dst_list, 1)
+        src_words.append(shared.tile([P, HALF], U32, name="src_words1", offset=2048, align_bytes=64))
+        gather_words(src_words, src_list, 1)
 
-        pieces = []
+        units = [(0, 0), (1, 0), (0, 1), (1, 1), (2, 0), (2, 1), (3, 0), (3, 1)]
+        gated = []
         relus = []
 
-        def piece(nt, j0, j1, bank, gated):
-            last = nt == N_TILES - 1 and j1 == J
-            values = finish(nt, j0, j1, gate_banks[bank][:, 0 : j1 - j0], gated, last)
-            pieces.append((nt, j0, j1, values, last))
+        def finish(u, own):
+            relus.append(add_gated(turn_own(u, own), gated[u]))
 
-        g00 = gate(0, 0, gate_banks[0], message_banks[0], None)
-        g10 = gate(1, 0, gate_banks[1], message_banks[1], None)
-        piece(0, 0, QUARTER, 0, g00[:, 0:QUARTER])
-        piece(0, QUARTER, HALF, 1, g00[:, QUARTER:HALF])
-        g01 = gate(0, HALF, gate_banks[2], message_banks[0], None)
-        g20 = gate(2, 0, gate_banks[3], message_banks[2], None)
-        piece(0, HALF, J, 0, g01[:])
-        quantize_wo(P, 2 * P)
-        piece(1, 0, HALF, 1, g10[:])
-        g11 = gate(1, HALF, gate_banks[2], message_banks[1], None)
-        piece(1, HALF, J, 3, g11[:])
-        quantize_wo(2 * P, N)
-        piece(2, 0, HALF, 0, g20[:])
-        g21 = gate(2, HALF, gate_banks[1], message_banks[2], relus[2])
-        piece(2, HALF, J, 2, g21[:])
-        g30 = gate(3, 0, gate_banks[3], message_banks[3], relus[3])
-        piece(3, 0, HALF, 0, g30[:])
-        g31 = gate(3, HALF, gate_banks[1], message_banks[3], relus[4])
-        piece(3, HALF, J, 2, g31[:])
-        for args in pieces:
-            scatter(*args)
+        gated.append(gate(0, *gate_products(0, *units[0])))
+        grouped_second = keep.tile([P, P, PACK], BF16, name="grouped_second", align_bytes=64)
+        quantize_wo(P, wo_raw[1], grouped_second[:])
+        src_scales.append(keep.tile([P, HALF], U8, name="src_scales1", tag="eta0", align_bytes=64))
+        gather_scales(src_scales, src_list, 1)
+        rows_out.append(keep.tile([P, T], F32, name="rows_out1", tag="table_scales", align_bytes=64))
+        nc.gpsimd.memset(rows_out[1][:], 0.0)
+        finish(0, own_product(*units[0]))
+        for u in range(1, len(units) + 1):
+            if u >= 2:
+                own = own_product(*units[u - 1])
+            if u < len(units):
+                gated.append(gate(u, *gate_products(u, *units[u])))
+            if u >= 2:
+                finish(u - 1, own)
+            scatter(*units[u - 1], relus[u - 1])
+            if u == 2:
+                grouped_rest = keep.tile([P, 2 * P, PACK], BF16, name="grouped_rest", tag="gated1", align_bytes=64)
+                quantize_wo(2 * P, wo_raw[2], grouped_rest[:])

@@ -1,7 +1,6 @@
 from contextlib import ExitStack
 
 import concourse.mybir as mybir
-from concourse.masks import make_identity
 
 K, N, T, J = 512, 512, 2048, 1024
 FLOPS = 4 * 2 * K * N * J
@@ -23,6 +22,7 @@ LANES = 16
 HALF = J // 2
 E_TILES = HALF // P
 OUT_TILES = 2
+WC_ROW, WA_ROW, WB_ROW = 0, 4, 8
 
 
 def tile_list_rgg_ownrelu_kernel(
@@ -31,28 +31,17 @@ def tile_list_rgg_ownrelu_kernel(
     nc = tc.nc
     with ExitStack() as ctx:
         keep = ctx.enter_context(tc.tile_pool(name="keep", bufs=1))
+        loads = ctx.enter_context(tc.tile_pool(name="loads", bufs=1))
         shared = ctx.enter_context(tc.tile_pool(name="shared", bufs=1))
         work = ctx.enter_context(tc.tile_pool(name="work", bufs=8))
         psum = ctx.enter_context(tc.psum_pool(name="psum", bufs=2))
 
         src_list = keep.tile([P, J // LANES], U16, name="src_list")
         dst_list = keep.tile([P, J // LANES], U16, name="dst_list")
-        table_words = keep.tile([P, T], I32, name="table_words", align_bytes=64)
         table_scales = keep.tile([P, T // 4], I32, name="table_scales", tag="table_scales", align_bytes=64)
-        wa_codes = keep.tile([P, N], I32, name="wa_codes", align_bytes=64)
-        wb_codes = keep.tile([P, N], I32, name="wb_codes", align_bytes=64)
-        wc_codes = keep.tile([P, 2 * N], U8, name="wc_codes", align_bytes=64)
-        wa_plane = keep.tile([P, N // 4], I32, name="wa_plane", align_bytes=64)
-        wb_plane = keep.tile([P, N // 4], I32, name="wb_plane", align_bytes=64)
-        wc_plane = keep.tile([P, N // 4], I32, name="wc_plane", align_bytes=64)
-        wo_raw = [
-            keep.tile([P, PACK, P], F32, name="wo_raw0"),
-            keep.tile([P, PACK, P], F32, name="wo_raw1"),
-            keep.tile([P, PACK, 2 * P], F32, name="wo_raw2"),
-        ]
+        w_planes = keep.tile([P, N // 4], I32, name="w_planes", align_bytes=64)
         wo_codes = keep.tile([P, N], U32, name="wo_codes", align_bytes=64)
         wo_scales = keep.tile([P, N], U8, name="wo_scales", align_bytes=64)
-        edge_w = [keep.tile([P, HALF], F32, name="edge_w%d" % h) for h in range(2)]
         src_words = []
         dst_words = [keep.tile([P, HALF], U32, name="dst_words0", align_bytes=64)]
         src_scales = [keep.tile([P, HALF], U8, name="src_scales0", align_bytes=64)]
@@ -61,38 +50,54 @@ def tile_list_rgg_ownrelu_kernel(
         identity = keep.tile([P, P], F32, name="identity")
         warm = keep.tile([P, 2], F32, name="warm")
 
+        nc.gpsimd.memset(table_scales[:], 0)
+        zeros = loads.tile([P, 25 * 256], F32, name="zeros", offset=0, align_bytes=64)
+        nc.gpsimd.memset(zeros[:, 0:P], 0.0)
+        nc.gpsimd.affine_select(
+            out=identity[:], in_=zeros[:, 0:P], compare_op=ALU.not_equal, fill=1.0, base=0,
+            pattern=[[-1, P]], channel_multiplier=1,
+        )
+        nc.gpsimd.memset(w_planes[:], 0)
         nc.gpsimd.memset(warm[:, 0:1], 0.0)
         nc.scalar.activation(warm[:, 1:2], warm[:, 0:1], ACT.Sigmoid)
+        nc.vector.memset(rows_out[0][:, 0 : T - 1], 0.0)
+        nc.vector.memset(rows_out[0][:, T - 1 : T], 0.0)
 
-        def load_scales(plane, scales, quadrants, queue):
+        table_words = loads.tile([P, T], I32, name="table_words", offset=0, align_bytes=64)
+        wa_codes = loads.tile([P, N], I32, name="wa_codes", offset=8 * 1024, align_bytes=64)
+        wb_codes = loads.tile([P, N], I32, name="wb_codes", offset=10 * 1024, align_bytes=64)
+        wc_codes = loads.tile([P, 2 * N], U8, name="wc_codes", offset=12 * 1024, align_bytes=64)
+        wo_raw = [
+            loads.tile([P, PACK, P], F32, name="wo_raw0", offset=13 * 1024, align_bytes=64),
+            loads.tile([P, PACK, P], F32, name="wo_raw1", offset=15 * 1024, align_bytes=64),
+            loads.tile([P, PACK, 2 * P], F32, name="wo_raw2", offset=17 * 1024, align_bytes=64),
+        ]
+        edge_w = [loads.tile([P, HALF], F32, name="edge_w%d" % h, offset=(21 + 2 * h) * 1024, align_bytes=64) for h in range(2)]
+
+        def load_scales(plane, first_row, scales):
             rows = scales[0].bitcast(I32)
-            for q in quadrants:
-                quadrant_rows = rows[4 * q : 4 * (q + 1), :].unsqueeze(0).broadcast_to([8, 4, rows.shape[1]])
-                queue.dma_start(plane[32 * q : 32 * (q + 1), :], quadrant_rows)
+            for q in range(4):
+                nc.sync.dma_start(plane[32 * q + first_row : 32 * q + first_row + 4, :], rows[4 * q : 4 * (q + 1), :])
 
         def load_words(tile_i32, words):
             nc.sync.dma_start(tile_i32, words[0].rearrange("p c i -> p (c i)").bitcast(I32))
 
         wo_rows = wo.rearrange("(p i) n -> p i n", i=PACK)
         nc.sync.dma_start(dst_list[:], offs2)
-        load_scales(table_scales, tab_scales, range(4), nc.sync)
         nc.sync.dma_start(src_list[:], offs)
-        load_scales(wa_plane, wa_scales, range(1), nc.sync)
+        load_scales(table_scales, 0, tab_scales)
         load_words(table_words[:], tab_words)
-        load_scales(wc_plane, wc_scales, range(4), nc.gpsimd)
         nc.sync.dma_start(wo_raw[0][:], wo_rows[:, :, 0:P])
-        load_scales(wa_plane, wa_scales, range(1, 4), nc.sync)
+        load_scales(w_planes, WC_ROW, wc_scales)
         nc.sync.dma_start(wc_codes[:].bitcast(I32), wc_words[0].bitcast(I32))
         load_words(wa_codes[:], wa_words)
+        load_scales(w_planes, WA_ROW, wa_scales)
         load_words(wb_codes[:], wb_words)
-        load_scales(wb_plane, wb_scales, range(4), nc.sync)
         nc.sync.dma_start(wo_raw[1][:], wo_rows[:, :, P : 2 * P])
+        load_scales(w_planes, WB_ROW, wb_scales)
         nc.sync.dma_start(edge_w[0][:], wgo[:, 0:HALF])
         nc.sync.dma_start(wo_raw[2][:], wo_rows[:, :, 2 * P : N])
         nc.sync.dma_start(edge_w[1][:], wgo[:, HALF:J])
-
-        make_identity(nc, identity[:])
-        nc.vector.memset(rows_out[0][:], 0.0)
 
         def list_cols(h):
             return slice(h * HALF // LANES, (h + 1) * HALF // LANES)
@@ -122,22 +127,22 @@ def tile_list_rgg_ownrelu_kernel(
         def gate_products(u, nt, h):
             cols = slice(nt * P, (nt + 1) * P)
             za = psum.tile([P, HALF], F32, name="za%d" % u, tag="sum_bank%d" % (u % 3), bufs=1)
-            ms = psum.tile([P, HALF], F32, name="ms", bufs=3)
+            ms = psum.tile([P, HALF], F32, name="ms%d" % u, tag="product_bank%d" % (u % 4), bufs=1)
             for e in range(E_TILES):
                 product(ms, e, src_words[h], src_scales[h], wc_codes[:, 2 * nt * P : 2 * (nt + 1) * P].bitcast(FP4X4),
-                        wc_plane[:].bitcast(U8)[:, cols], True, True)
+                        w_planes[:].bitcast(U8)[WC_ROW:, cols], True, True)
             for e in range(E_TILES):
                 product(za, e, dst_words[h], dst_scales[h], wa_codes[:, cols].bitcast(FP8X4),
-                        wa_plane[:].bitcast(U8)[:, cols], True, False)
+                        w_planes[:].bitcast(U8)[WA_ROW:, cols], True, False)
                 product(za, e, src_words[h], src_scales[h], wb_codes[:, cols].bitcast(FP8X4),
-                        wb_plane[:].bitcast(U8)[:, cols], False, True)
+                        w_planes[:].bitcast(U8)[WB_ROW:, cols], False, True)
             eta = keep.tile([P, HALF], F32, name="eta%d" % u, tag="eta%d" % u, align_bytes=64)
             nc.scalar.activation(eta[:], za[:], ACT.Sigmoid)
             return ms, eta
 
-        def own_product(nt, h):
+        def own_product(u, nt, h):
             cols = slice(nt * P, (nt + 1) * P)
-            ow = psum.tile([P, HALF], F32, name="ow")
+            ow = psum.tile([P, HALF], F32, name="ow%d" % u, tag="product_bank%d" % ((u - 1) % 4 if u else 4), bufs=1)
             for e in range(E_TILES):
                 product(ow, e, dst_words[h], dst_scales[h], wo_codes[:, cols].bitcast(FP8X4), wo_scales[:, cols], True, True)
             own = work.tile([P, HALF], F32, name="own")
@@ -199,10 +204,10 @@ def tile_list_rgg_ownrelu_kernel(
         gather_scales(src_scales, src_list, 1)
         rows_out.append(keep.tile([P, T], F32, name="rows_out1", tag="table_scales", align_bytes=64))
         nc.gpsimd.memset(rows_out[1][:], 0.0)
-        finish(0, own_product(*units[0]))
+        finish(0, own_product(0, *units[0]))
         for u in range(1, len(units) + 1):
             if u >= 2:
-                own = own_product(*units[u - 1])
+                own = own_product(u - 1, *units[u - 1])
             if u < len(units):
                 gated.append(gate(u, *gate_products(u, *units[u])))
             if u >= 2:

@@ -21,7 +21,8 @@ PACK = 4
 LANES = 16
 HALF = J // 2
 E_TILES = HALF // P
-OUT_TILES = 2
+OUT_TILES = 3
+VECTOR_GATES = 2
 WC_ROW, WA_ROW, WB_ROW = 0, 4, 8
 
 
@@ -38,25 +39,25 @@ def tile_list_rgg_ownrelu_kernel(
 
         src_list = keep.tile([P, J // LANES], U16, name="src_list")
         dst_list = keep.tile([P, J // LANES], U16, name="dst_list")
-        table_scales = keep.tile([P, T // 4], I32, name="table_scales", tag="table_scales", align_bytes=64)
-        w_planes = keep.tile([P, N // 4], I32, name="w_planes", align_bytes=64)
+        table_scales = keep.tile([P, T // 4], I32, name="table_scales", align_bytes=64)
         wo_codes = keep.tile([P, N], U32, name="wo_codes", align_bytes=64)
         wo_scales = keep.tile([P, N], U8, name="wo_scales", align_bytes=64)
         src_words = []
         dst_words = [keep.tile([P, HALF], U32, name="dst_words0", align_bytes=64)]
         src_scales = [keep.tile([P, HALF], U8, name="src_scales0", align_bytes=64)]
         dst_scales = [keep.tile([P, HALF], U8, name="dst_scales%d" % h, align_bytes=64) for h in range(2)]
-        rows_out = [keep.tile([P, T], F32, name="rows_out%d" % b) for b in range(OUT_TILES - 1)]
+        rows_out = [keep.tile([P, T], F32, name="rows_out0")]
         identity = keep.tile([P, P], F32, name="identity")
         warm = keep.tile([P, 2], F32, name="warm")
 
         nc.gpsimd.memset(table_scales[:], 0)
-        zeros = loads.tile([P, 25 * 256], F32, name="zeros", offset=0, align_bytes=64)
+        zeros = loads.tile([P, 35 * 256], F32, name="zeros", offset=0, align_bytes=64)
         nc.gpsimd.memset(zeros[:, 0:P], 0.0)
         nc.gpsimd.affine_select(
             out=identity[:], in_=zeros[:, 0:P], compare_op=ALU.not_equal, fill=1.0, base=0,
             pattern=[[-1, P]], channel_multiplier=1,
         )
+        w_planes = loads.tile([P, N // 4], I32, name="w_planes", offset=25 * 1024, align_bytes=64)
         nc.gpsimd.memset(w_planes[:], 0)
         nc.gpsimd.memset(warm[:, 0:1], 0.0)
         nc.scalar.activation(warm[:, 1:2], warm[:, 0:1], ACT.Sigmoid)
@@ -69,10 +70,13 @@ def tile_list_rgg_ownrelu_kernel(
         wc_codes = loads.tile([P, 2 * N], U8, name="wc_codes", offset=12 * 1024, align_bytes=64)
         wo_raw = [
             loads.tile([P, PACK, P], F32, name="wo_raw0", offset=13 * 1024, align_bytes=64),
-            loads.tile([P, PACK, P], F32, name="wo_raw1", offset=15 * 1024, align_bytes=64),
-            loads.tile([P, PACK, 2 * P], F32, name="wo_raw2", offset=17 * 1024, align_bytes=64),
+            loads.tile([P, PACK, 2 * P], F32, name="wo_raw1", offset=15 * 1024, align_bytes=64),
+            loads.tile([P, PACK, P], F32, name="wo_raw2", offset=19 * 1024, align_bytes=64),
         ]
         edge_w = [loads.tile([P, HALF], F32, name="edge_w%d" % h, offset=(21 + 2 * h) * 1024, align_bytes=64) for h in range(2)]
+        for b in range(1, OUT_TILES):
+            rows_out.append(loads.tile([P, T], F32, name="rows_out%d" % b, offset=(18 + 8 * b) * 1024, align_bytes=64))
+            nc.gpsimd.memset(rows_out[b][:], 0.0)
 
         def load_scales(plane, first_row, scales):
             rows = scales[0].bitcast(I32)
@@ -93,10 +97,10 @@ def tile_list_rgg_ownrelu_kernel(
         load_words(wa_codes[:], wa_words)
         load_scales(w_planes, WA_ROW, wa_scales)
         load_words(wb_codes[:], wb_words)
-        nc.sync.dma_start(wo_raw[1][:], wo_rows[:, :, P : 2 * P])
-        load_scales(w_planes, WB_ROW, wb_scales)
+        nc.sync.dma_start(wo_raw[1][:], wo_rows[:, :, P : 3 * P])
         nc.sync.dma_start(edge_w[0][:], wgo[:, 0:HALF])
-        nc.sync.dma_start(wo_raw[2][:], wo_rows[:, :, 2 * P : N])
+        load_scales(w_planes, WB_ROW, wb_scales)
+        nc.sync.dma_start(wo_raw[2][:], wo_rows[:, :, 3 * P : N])
         nc.sync.dma_start(edge_w[1][:], wgo[:, HALF:J])
 
         def list_cols(h):
@@ -124,13 +128,13 @@ def tile_list_rgg_ownrelu_kernel(
                 rhs=w_codes, rhs_scale=w_scales, start=start, stop=stop,
             )
 
+        def product_bank(kind, u):
+            first_tenant = u - {"ms": 0, "ow": 1, "za": 2}[kind]
+            return psum.tile([P, HALF], F32, name="%s%d" % (kind, u), tag="product_bank%d" % (first_tenant % 4), bufs=1)
+
         def gate_products(u, nt, h):
             cols = slice(nt * P, (nt + 1) * P)
-            za = psum.tile([P, HALF], F32, name="za%d" % u, tag="sum_bank%d" % (u % 3), bufs=1)
-            ms = psum.tile([P, HALF], F32, name="ms%d" % u, tag="product_bank%d" % (u % 4), bufs=1)
-            for e in range(E_TILES):
-                product(ms, e, src_words[h], src_scales[h], wc_codes[:, 2 * nt * P : 2 * (nt + 1) * P].bitcast(FP4X4),
-                        w_planes[:].bitcast(U8)[WC_ROW:, cols], True, True)
+            za = product_bank("za", u)
             for e in range(E_TILES):
                 product(za, e, dst_words[h], dst_scales[h], wa_codes[:, cols].bitcast(FP8X4),
                         w_planes[:].bitcast(U8)[WA_ROW:, cols], True, False)
@@ -138,42 +142,55 @@ def tile_list_rgg_ownrelu_kernel(
                         w_planes[:].bitcast(U8)[WB_ROW:, cols], False, True)
             eta = keep.tile([P, HALF], F32, name="eta%d" % u, tag="eta%d" % u, align_bytes=64)
             nc.scalar.activation(eta[:], za[:], ACT.Sigmoid)
-            return ms, eta
+            ms = product_bank("ms", u)
+            for e in range(E_TILES):
+                product(ms, e, src_words[h], src_scales[h], wc_codes[:, 2 * nt * P : 2 * (nt + 1) * P].bitcast(FP4X4),
+                        w_planes[:].bitcast(U8)[WC_ROW:, cols], True, True)
+            if u < VECTOR_GATES:
+                return ms, eta
+            message = work.tile([P, HALF], F32, name="message")
+            nc.scalar.copy(message[:], ms[:])
+            return message, eta
 
         def own_product(u, nt, h):
             cols = slice(nt * P, (nt + 1) * P)
-            ow = psum.tile([P, HALF], F32, name="ow%d" % u, tag="product_bank%d" % ((u - 1) % 4 if u else 4), bufs=1)
+            ow = product_bank("ow", u)
             for e in range(E_TILES):
                 product(ow, e, dst_words[h], dst_scales[h], wo_codes[:, cols].bitcast(FP8X4), wo_scales[:, cols], True, True)
             own = work.tile([P, HALF], F32, name="own")
             nc.scalar.copy(own[:], ow[:])
             return own
 
-        def gate(u, ms, eta):
-            gated = keep.tile([P, HALF], F32, name="gated%d" % u, tag="gated%d" % u, align_bytes=64)
-            nc.vector.tensor_tensor(gated[:], ms[:], eta[:], ALU.mult)
+        def chain_tile(kind, u):
+            slot = u + VECTOR_GATES if kind == "relu" else u
+            return keep.tile([P, HALF], F32, name="%s%d" % (kind, u), tag="chain%d" % slot, align_bytes=64)[:]
+
+        def gate(u, message, eta):
+            gated = chain_tile("gated", u)
+            engine = nc.vector if u < VECTOR_GATES else nc.gpsimd
+            engine.tensor_tensor(gated, message[:], eta[:], ALU.mult)
             return gated
 
-        def turn_own(u, own):
-            total = psum.tile([P, HALF], F32, name="total%d" % u, tag="sum_bank%d" % ((u + 1) % 3 if u else 0), bufs=1)
+        def finish(u, own, gated):
+            total = psum.tile([P, HALF], F32, name="total", bufs=4)
             for e in range(E_TILES):
                 edges = slice(e * P, (e + 1) * P)
                 nc.tensor.matmul(total[:, edges], own[:, edges], identity[:], start=e == 0, stop=False, is_transpose=True)
-            return total
-
-        def add_gated(total, gated):
             for e in range(E_TILES):
                 edges = slice(e * P, (e + 1) * P)
                 nc.tensor.matmul(total[:, edges], gated[:, edges], identity[:], start=False, stop=e == E_TILES - 1, is_transpose=True)
-            relu = work.tile([P, HALF], F32, name="relu")
-            nc.scalar.activation(relu[:], total[:], ACT.Relu)
+            relu = chain_tile("relu", u)
+            nc.scalar.activation(relu, total[:], ACT.Relu)
             return relu
 
-        def scatter(nt, h, relu):
+        def scatter(nt, h, relu, pieces):
             rows = rows_out[nt % OUT_TILES]
-            nc.vector.tensor_tensor(
-                rows[:].indirect(dst_list[:, list_cols(h)]), relu[:], edge_w[h][:], ALU.mult
-            )
+            width = HALF // pieces
+            for c in range(0, HALF, width):
+                weighted = work.tile([P, width], F32, name="weighted", bufs=9)
+                nc.gpsimd.tensor_tensor(weighted[:], relu[:, c : c + width], edge_w[h][:, c : c + width], ALU.mult)
+                j = h * HALF + c
+                nc.vector.tensor_copy(rows[:].indirect(dst_list[:, j // LANES : (j + width) // LANES]), weighted[:])
             if h == 1:
                 nc.sync.dma_start(out[nt * P : (nt + 1) * P, :], rows[:])
 
@@ -190,29 +207,27 @@ def tile_list_rgg_ownrelu_kernel(
         src_words.append(shared.tile([P, HALF], U32, name="src_words1", offset=2048, align_bytes=64))
         gather_words(src_words, src_list, 1)
 
-        units = [(0, 0), (1, 0), (0, 1), (1, 1), (2, 0), (2, 1), (3, 0), (3, 1)]
-        gated = []
-        relus = []
-
-        def finish(u, own):
-            relus.append(add_gated(turn_own(u, own), gated[u]))
-
-        gated.append(gate(0, *gate_products(0, *units[0])))
-        grouped_second = keep.tile([P, P, PACK], BF16, name="grouped_second", align_bytes=64)
+        units = [(0, 0), (1, 0), (2, 0), (0, 1), (1, 1), (2, 1), (3, 0), (3, 1)]
+        own = own_product(0, *units[0])
+        gated = [gate(0, *gate_products(0, *units[0]))]
+        grouped_second = keep.tile([P, 2 * P, PACK], BF16, name="grouped_second", align_bytes=64)
         quantize_wo(P, wo_raw[1], grouped_second[:])
         src_scales.append(keep.tile([P, HALF], U8, name="src_scales1", tag="eta0", align_bytes=64))
         gather_scales(src_scales, src_list, 1)
-        rows_out.append(keep.tile([P, T], F32, name="rows_out1", tag="table_scales", align_bytes=64))
-        nc.gpsimd.memset(rows_out[1][:], 0.0)
-        finish(0, own_product(0, *units[0]))
-        for u in range(1, len(units) + 1):
-            if u >= 2:
-                own = own_product(u - 1, *units[u - 1])
-            if u < len(units):
-                gated.append(gate(u, *gate_products(u, *units[u])))
-            if u >= 2:
-                finish(u - 1, own)
-            scatter(*units[u - 1], relus[u - 1])
-            if u == 2:
-                grouped_rest = keep.tile([P, 2 * P, PACK], BF16, name="grouped_rest", tag="gated1", align_bytes=64)
-                quantize_wo(2 * P, wo_raw[2], grouped_rest[:])
+        relu = finish(0, own, gated[0])
+        gated.append(gate(1, *gate_products(1, *units[1])))
+        own = own_product(1, *units[1])
+        for u in range(len(units)):
+            if u >= 1:
+                if u + 1 < len(units):
+                    next_own = own_product(u + 1, *units[u + 1])
+                relu = finish(u, own, gated[u])
+                own = next_own
+            if u + 2 < len(units):
+                products = gate_products(u + 2, *units[u + 2])
+            scatter(*units[u], relu, 1 if u else 2)
+            if u + 2 < len(units):
+                gated.append(gate(u + 2, *products))
+            if u == 0:
+                grouped_rest = keep.tile([P, P, PACK], BF16, name="grouped_rest", tag="chain0", align_bytes=64)
+                quantize_wo(3 * P, wo_raw[2], grouped_rest[:])

@@ -19,10 +19,14 @@ ALU = mybir.AluOpType
 P = 128
 PACK = 4
 LANES = 16
+KIB = 1024
 HALF = J // 2
-E_TILES = HALF // P
+EDGE_TILES = HALF // P
+UNITS = [(0, 0), (1, 0), (2, 0), (0, 1), (1, 1), (2, 1), (3, 0), (3, 1)]
 OUT_TILES = 3
-VECTOR_GATES = 2
+PRODUCT_BANKS = 4
+VECTOR_GATES = 3
+FUSED_UNITS = (0, 6, 7)
 WC_ROW, WA_ROW, WB_ROW = 0, 4, 8
 
 
@@ -32,202 +36,207 @@ def tile_list_rgg_ownrelu_kernel(
     nc = tc.nc
     with ExitStack() as ctx:
         keep = ctx.enter_context(tc.tile_pool(name="keep", bufs=1))
-        loads = ctx.enter_context(tc.tile_pool(name="loads", bufs=1))
-        shared = ctx.enter_context(tc.tile_pool(name="shared", bufs=1))
-        work = ctx.enter_context(tc.tile_pool(name="work", bufs=8))
-        psum = ctx.enter_context(tc.psum_pool(name="psum", bufs=2))
+        held = ctx.enter_context(tc.tile_pool(name="held", bufs=1))
+        picks = ctx.enter_context(tc.tile_pool(name="picks", bufs=1))
+        work = ctx.enter_context(tc.tile_pool(name="work", bufs=len(UNITS)))
+        psum = ctx.enter_context(tc.psum_pool(name="psum", bufs=1))
 
         src_list = keep.tile([P, J // LANES], U16, name="src_list")
         dst_list = keep.tile([P, J // LANES], U16, name="dst_list")
-        table_scales = keep.tile([P, T // 4], I32, name="table_scales", align_bytes=64)
+        table_plane = keep.tile([P, T // PACK], I32, name="table_plane", align_bytes=64)
         wo_codes = keep.tile([P, N], U32, name="wo_codes", align_bytes=64)
-        wo_scales = keep.tile([P, N], U8, name="wo_scales", align_bytes=64)
-        src_words = []
-        dst_words = [keep.tile([P, HALF], U32, name="dst_words0", align_bytes=64)]
-        src_scales = [keep.tile([P, HALF], U8, name="src_scales0", align_bytes=64)]
-        dst_scales = [keep.tile([P, HALF], U8, name="dst_scales%d" % h, align_bytes=64) for h in range(2)]
-        rows_out = [keep.tile([P, T], F32, name="rows_out0")]
+        wo_plane = keep.tile([P, N], U8, name="wo_plane", align_bytes=64)
         identity = keep.tile([P, P], F32, name="identity")
-        warm = keep.tile([P, 2], F32, name="warm")
 
-        nc.gpsimd.memset(table_scales[:], 0)
-        zeros = loads.tile([P, 35 * 256], F32, name="zeros", offset=0, align_bytes=64)
+        nc.gpsimd.memset(table_plane[:], 0)
+        zeros = held.tile([P, 35 * KIB // 4], F32, name="zeros", offset=0, align_bytes=64)
         nc.gpsimd.memset(zeros[:, 0:P], 0.0)
         nc.gpsimd.affine_select(
             out=identity[:], in_=zeros[:, 0:P], compare_op=ALU.not_equal, fill=1.0, base=0,
             pattern=[[-1, P]], channel_multiplier=1,
         )
-        w_planes = loads.tile([P, N // 4], I32, name="w_planes", offset=25 * 1024, align_bytes=64)
+
+        def held_tile(name, shape, dtype, kib):
+            return held.tile(shape, dtype, name=name, offset=kib * KIB, align_bytes=64)
+
+        table_words = held_tile("table_words", [P, T], I32, 0)
+        wa_codes = held_tile("wa_codes", [P, N], I32, 8)
+        wb_codes = held_tile("wb_codes", [P, N], I32, 10)
+        wc_codes = held_tile("wc_codes", [P, 2 * N], U8, 12)
+        wo_first = held_tile("wo_first", [P, PACK, P], F32, 13)
+        wo_middle = held_tile("wo_middle", [P, PACK, 2 * P], F32, 15)
+        wo_last = held_tile("wo_last", [P, PACK, P], F32, 19)
+        edge_w = [held_tile("edge_w%d" % h, [P, HALF], F32, 21 + 2 * h) for h in range(2)]
+        w_planes = held_tile("w_planes", [P, N // PACK], I32, 25)
         nc.gpsimd.memset(w_planes[:], 0)
-        nc.gpsimd.memset(warm[:, 0:1], 0.0)
-        nc.scalar.activation(warm[:, 1:2], warm[:, 0:1], ACT.Sigmoid)
+
+        rows_out = [keep.tile([P, T], F32, name="rows_out0")]
         nc.vector.memset(rows_out[0][:, 0 : T - 1], 0.0)
         nc.vector.memset(rows_out[0][:, T - 1 : T], 0.0)
-
-        table_words = loads.tile([P, T], I32, name="table_words", offset=0, align_bytes=64)
-        wa_codes = loads.tile([P, N], I32, name="wa_codes", offset=8 * 1024, align_bytes=64)
-        wb_codes = loads.tile([P, N], I32, name="wb_codes", offset=10 * 1024, align_bytes=64)
-        wc_codes = loads.tile([P, 2 * N], U8, name="wc_codes", offset=12 * 1024, align_bytes=64)
-        wo_raw = [
-            loads.tile([P, PACK, P], F32, name="wo_raw0", offset=13 * 1024, align_bytes=64),
-            loads.tile([P, PACK, 2 * P], F32, name="wo_raw1", offset=15 * 1024, align_bytes=64),
-            loads.tile([P, PACK, P], F32, name="wo_raw2", offset=19 * 1024, align_bytes=64),
-        ]
-        edge_w = [loads.tile([P, HALF], F32, name="edge_w%d" % h, offset=(21 + 2 * h) * 1024, align_bytes=64) for h in range(2)]
         for b in range(1, OUT_TILES):
-            rows_out.append(loads.tile([P, T], F32, name="rows_out%d" % b, offset=(18 + 8 * b) * 1024, align_bytes=64))
+            rows_out.append(held_tile("rows_out%d" % b, [P, T], F32, 18 + 8 * b))
             nc.gpsimd.memset(rows_out[b][:], 0.0)
 
-        def load_scales(plane, first_row, scales):
+        def load_plane(plane, first_row, scales):
             rows = scales[0].bitcast(I32)
             for q in range(4):
                 nc.sync.dma_start(plane[32 * q + first_row : 32 * q + first_row + 4, :], rows[4 * q : 4 * (q + 1), :])
 
-        def load_words(tile_i32, words):
-            nc.sync.dma_start(tile_i32, words[0].rearrange("p c i -> p (c i)").bitcast(I32))
+        def load_words(codes, words):
+            nc.sync.dma_start(codes[:], words[0].rearrange("p c i -> p (c i)").bitcast(I32))
 
         wo_rows = wo.rearrange("(p i) n -> p i n", i=PACK)
         nc.sync.dma_start(dst_list[:], offs2)
         nc.sync.dma_start(src_list[:], offs)
-        load_scales(table_scales, 0, tab_scales)
-        load_words(table_words[:], tab_words)
-        nc.sync.dma_start(wo_raw[0][:], wo_rows[:, :, 0:P])
-        load_scales(w_planes, WC_ROW, wc_scales)
+        load_plane(table_plane, 0, tab_scales)
+        load_words(table_words, tab_words)
+        nc.sync.dma_start(wo_first[:], wo_rows[:, :, 0:P])
+        load_plane(w_planes, WC_ROW, wc_scales)
         nc.sync.dma_start(wc_codes[:].bitcast(I32), wc_words[0].bitcast(I32))
-        load_words(wa_codes[:], wa_words)
-        load_scales(w_planes, WA_ROW, wa_scales)
-        load_words(wb_codes[:], wb_words)
-        nc.sync.dma_start(wo_raw[1][:], wo_rows[:, :, P : 3 * P])
+        load_words(wa_codes, wa_words)
+        load_plane(w_planes, WA_ROW, wa_scales)
+        load_words(wb_codes, wb_words)
+        nc.sync.dma_start(wo_middle[:], wo_rows[:, :, P : 3 * P])
+        load_plane(w_planes, WB_ROW, wb_scales)
         nc.sync.dma_start(edge_w[0][:], wgo[:, 0:HALF])
-        load_scales(w_planes, WB_ROW, wb_scales)
-        nc.sync.dma_start(wo_raw[2][:], wo_rows[:, :, 3 * P : N])
+        nc.sync.dma_start(wo_last[:], wo_rows[:, :, 3 * P : N])
         nc.sync.dma_start(edge_w[1][:], wgo[:, HALF:J])
 
-        def list_cols(h):
-            return slice(h * HALF // LANES, (h + 1) * HALF // LANES)
+        def entries(offsets, j0, j1):
+            return offsets[:, j0 // LANES : j1 // LANES]
 
-        def gather_scales(picked, lst, h):
-            nc.vector.tensor_copy(picked[h][:], table_scales[:].bitcast(U8).indirect(lst[:, list_cols(h)]))
+        def gather_scales(picked, offsets, j0, j1):
+            nc.vector.tensor_copy(picked[:], table_plane[:].bitcast(U8).indirect(entries(offsets, j0, j1)))
 
-        def gather_words(picked, lst, h):
-            nc.vector.tensor_copy(picked[h][:], table_words[:].bitcast(U32).indirect(lst[:, list_cols(h)]))
+        def gather_words(picked, offsets, h):
+            window = table_words[:].bitcast(U32)
+            nc.vector.tensor_copy(picked[:], window.indirect(entries(offsets, h * HALF, (h + 1) * HALF)))
 
         def quantize_wo(n0, raw, grouped):
             n1 = n0 + raw.shape[2]
             nc.scalar.copy(grouped, raw[:].rearrange("p i n -> p n i"))
             nc.vector.quantize_mx(
                 out=wo_codes[:, n0:n1].bitcast(FP8X4),
-                scales=wo_scales[:, n0:n1],
+                scales=wo_plane[:, n0:n1],
                 in_=grouped.rearrange("p n i -> p (n i)"),
             )
 
-        def product(bank, e, words, scales, w_codes, w_scales, start, stop):
+        def product(bank, e, picked, weight, start, stop):
             edges = slice(e * P, (e + 1) * P)
             nc.tensor.matmul_mx(
-                out=bank[:, edges], lhsT=words[:, edges].bitcast(FP8X4), lhsT_scale=scales[:, edges],
-                rhs=w_codes, rhs_scale=w_scales, start=start, stop=stop,
+                out=bank[:, edges], lhsT=picked[0][:, edges].bitcast(FP8X4), lhsT_scale=picked[1][:, edges],
+                rhs=weight[0], rhs_scale=weight[1], start=start, stop=stop,
             )
 
-        def product_bank(kind, u):
-            first_tenant = u - {"ms": 0, "ow": 1, "za": 2}[kind]
-            return psum.tile([P, HALF], F32, name="%s%d" % (kind, u), tag="product_bank%d" % (first_tenant % 4), bufs=1)
+        def product_bank(name, u, ahead):
+            tag = "product_bank%d" % ((u - ahead) % PRODUCT_BANKS)
+            return psum.tile([P, HALF], F32, name="%s%d" % (name, u), tag=tag)
 
-        def gate_products(u, nt, h):
+        def gate_products(u):
+            nt, h = UNITS[u]
             cols = slice(nt * P, (nt + 1) * P)
-            za = product_bank("za", u)
-            for e in range(E_TILES):
-                product(za, e, dst_words[h], dst_scales[h], wa_codes[:, cols].bitcast(FP8X4),
-                        w_planes[:].bitcast(U8)[WA_ROW:, cols], True, False)
-                product(za, e, src_words[h], src_scales[h], wb_codes[:, cols].bitcast(FP8X4),
-                        w_planes[:].bitcast(U8)[WB_ROW:, cols], False, True)
+            planes = w_planes[:].bitcast(U8)
+            za = product_bank("za", u, 2)
+            for e in range(EDGE_TILES):
+                product(za, e, dst[h], (wa_codes[:, cols].bitcast(FP8X4), planes[WA_ROW:, cols]), True, False)
+                product(za, e, src[h], (wb_codes[:, cols].bitcast(FP8X4), planes[WB_ROW:, cols]), False, True)
             eta = keep.tile([P, HALF], F32, name="eta%d" % u, tag="eta%d" % u, align_bytes=64)
             nc.scalar.activation(eta[:], za[:], ACT.Sigmoid)
-            ms = product_bank("ms", u)
-            for e in range(E_TILES):
-                product(ms, e, src_words[h], src_scales[h], wc_codes[:, 2 * nt * P : 2 * (nt + 1) * P].bitcast(FP4X4),
-                        w_planes[:].bitcast(U8)[WC_ROW:, cols], True, True)
+            ms = product_bank("ms", u, 0)
+            wc_cols = wc_codes[:, 2 * nt * P : 2 * (nt + 1) * P].bitcast(FP4X4)
+            for e in range(EDGE_TILES):
+                product(ms, e, src[h], (wc_cols, planes[WC_ROW:, cols]), True, True)
             if u < VECTOR_GATES:
                 return ms, eta
             message = work.tile([P, HALF], F32, name="message")
             nc.scalar.copy(message[:], ms[:])
             return message, eta
 
-        def own_product(u, nt, h):
+        def own_product(u):
+            nt, h = UNITS[u]
             cols = slice(nt * P, (nt + 1) * P)
-            ow = product_bank("ow", u)
-            for e in range(E_TILES):
-                product(ow, e, dst_words[h], dst_scales[h], wo_codes[:, cols].bitcast(FP8X4), wo_scales[:, cols], True, True)
+            ow = product_bank("ow", u, 1)
+            for e in range(EDGE_TILES):
+                product(ow, e, dst[h], (wo_codes[:, cols].bitcast(FP8X4), wo_plane[:, cols]), True, True)
             own = work.tile([P, HALF], F32, name="own")
             nc.scalar.copy(own[:], ow[:])
             return own
 
-        def chain_tile(kind, u):
-            slot = u + VECTOR_GATES if kind == "relu" else u
-            return keep.tile([P, HALF], F32, name="%s%d" % (kind, u), tag="chain%d" % slot, align_bytes=64)[:]
-
         def gate(u, message, eta):
-            gated = chain_tile("gated", u)
+            gated = keep.tile([P, HALF], F32, name="gated%d" % u, tag="chain%d" % u, align_bytes=64)
             engine = nc.vector if u < VECTOR_GATES else nc.gpsimd
-            engine.tensor_tensor(gated, message[:], eta[:], ALU.mult)
+            engine.tensor_tensor(gated[:], message[:], eta[:], ALU.mult)
             return gated
 
-        def finish(u, own, gated):
-            total = psum.tile([P, HALF], F32, name="total", bufs=4)
-            for e in range(E_TILES):
-                edges = slice(e * P, (e + 1) * P)
-                nc.tensor.matmul(total[:, edges], own[:, edges], identity[:], start=e == 0, stop=False, is_transpose=True)
-            for e in range(E_TILES):
-                edges = slice(e * P, (e + 1) * P)
-                nc.tensor.matmul(total[:, edges], gated[:, edges], identity[:], start=False, stop=e == E_TILES - 1, is_transpose=True)
-            relu = chain_tile("relu", u)
-            nc.scalar.activation(relu, total[:], ACT.Relu)
+        def add_and_relu(u, own, gated):
+            total = psum.tile([P, HALF], F32, name="total", bufs=8 - PRODUCT_BANKS)
+            for n, summand in enumerate((own, gated)):
+                for e in range(EDGE_TILES):
+                    edges = slice(e * P, (e + 1) * P)
+                    nc.tensor.matmul(
+                        total[:, edges], summand[:, edges], identity[:], is_transpose=True,
+                        start=(n, e) == (0, 0), stop=(n, e) == (1, EDGE_TILES - 1),
+                    )
+            relu = keep.tile([P, HALF], F32, name="relu%d" % u, tag="chain%d" % (u + 2), align_bytes=64)
+            nc.scalar.activation(relu[:], total[:], ACT.Relu)
             return relu
 
-        def scatter(nt, h, relu, pieces):
+        def scatter(u, relu):
+            nt, h = UNITS[u]
             rows = rows_out[nt % OUT_TILES]
-            width = HALF // pieces
-            for c in range(0, HALF, width):
-                weighted = work.tile([P, width], F32, name="weighted", bufs=9)
-                nc.gpsimd.tensor_tensor(weighted[:], relu[:, c : c + width], edge_w[h][:, c : c + width], ALU.mult)
-                j = h * HALF + c
-                nc.vector.tensor_copy(rows[:].indirect(dst_list[:, j // LANES : (j + width) // LANES]), weighted[:])
+            if u in FUSED_UNITS:
+                window = rows[:].indirect(entries(dst_list, h * HALF, (h + 1) * HALF))
+                nc.vector.tensor_tensor(window, relu[:], edge_w[h][:], ALU.mult)
+            else:
+                width = HALF // 2 if u - 1 in FUSED_UNITS else HALF
+                for c in range(0, HALF, width):
+                    weighted = work.tile([P, width], F32, name="weighted")
+                    nc.gpsimd.tensor_tensor(weighted[:], relu[:, c : c + width], edge_w[h][:, c : c + width], ALU.mult)
+                    window = rows[:].indirect(entries(dst_list, h * HALF + c, h * HALF + c + width))
+                    nc.vector.tensor_copy(window, weighted[:])
             if h == 1:
                 nc.sync.dma_start(out[nt * P : (nt + 1) * P, :], rows[:])
 
-        gather_scales(dst_scales, dst_list, 0)
-        gather_scales(src_scales, src_list, 0)
-        gather_scales(dst_scales, dst_list, 1)
-        gather_words(dst_words, dst_list, 0)
-        grouped_head = shared.tile([P, 2 * P + 32, PACK], BF16, name="grouped_head", offset=1920, align_bytes=64)
-        quantize_wo(0, wo_raw[0], grouped_head[:, 0:P, :])
-        src_words.append(shared.tile([P, HALF], U32, name="src_words0", offset=4096, align_bytes=64))
-        gather_words(src_words, src_list, 0)
-        dst_words.append(shared.tile([P, HALF], U32, name="dst_words1", offset=0, align_bytes=64))
-        gather_words(dst_words, dst_list, 1)
-        src_words.append(shared.tile([P, HALF], U32, name="src_words1", offset=2048, align_bytes=64))
-        gather_words(src_words, src_list, 1)
+        dst_plane = keep.tile([P, J], U8, name="dst_plane", align_bytes=64)
+        gather_scales(dst_plane, dst_list, 0, J)
+        src_plane0 = keep.tile([P, HALF], U8, name="src_plane0", align_bytes=64)
+        gather_scales(src_plane0, src_list, 0, HALF)
+        dst_words0 = keep.tile([P, HALF], U32, name="dst_words0", align_bytes=64)
+        gather_words(dst_words0, dst_list, 0)
 
-        units = [(0, 0), (1, 0), (2, 0), (0, 1), (1, 1), (2, 1), (3, 0), (3, 1)]
-        own = own_product(0, *units[0])
-        gated = [gate(0, *gate_products(0, *units[0]))]
-        grouped_second = keep.tile([P, 2 * P, PACK], BF16, name="grouped_second", align_bytes=64)
-        quantize_wo(P, wo_raw[1], grouped_second[:])
-        src_scales.append(keep.tile([P, HALF], U8, name="src_scales1", tag="eta0", align_bytes=64))
-        gather_scales(src_scales, src_list, 1)
-        relu = finish(0, own, gated[0])
-        gated.append(gate(1, *gate_products(1, *units[1])))
-        own = own_product(1, *units[1])
-        for u in range(len(units)):
-            if u >= 1:
-                if u + 1 < len(units):
-                    next_own = own_product(u + 1, *units[u + 1])
-                relu = finish(u, own, gated[u])
-                own = next_own
-            if u + 2 < len(units):
-                products = gate_products(u + 2, *units[u + 2])
-            scatter(*units[u], relu, 1 if u else 2)
-            if u + 2 < len(units):
+        grouped_first = picks.tile([P, 2 * P + 32, PACK], BF16, name="grouped_first", offset=2 * KIB - 128, align_bytes=64)
+        quantize_wo(0, wo_first, grouped_first[:, 0:P, :])
+        src_words0 = picks.tile([P, HALF], U32, name="src_words0", offset=4 * KIB, align_bytes=64)
+        gather_words(src_words0, src_list, 0)
+        dst_words1 = picks.tile([P, HALF], U32, name="dst_words1", offset=0, align_bytes=64)
+        gather_words(dst_words1, dst_list, 1)
+        src_words1 = picks.tile([P, HALF], U32, name="src_words1", offset=2 * KIB, align_bytes=64)
+        gather_words(src_words1, src_list, 1)
+        dst = [(dst_words0, dst_plane[:, 0:HALF]), (dst_words1, dst_plane[:, HALF:J])]
+        src = [(src_words0, src_plane0)]
+
+        own = own_product(0)
+        gated = [gate(0, *gate_products(0))]
+        grouped_middle = keep.tile([P, 2 * P, PACK], BF16, name="grouped_middle", align_bytes=64)
+        quantize_wo(P, wo_middle, grouped_middle[:])
+        src_plane1 = keep.tile([P, HALF], U8, name="src_plane1", tag="eta0", align_bytes=64)
+        gather_scales(src_plane1, src_list, HALF, J)
+        src.append((src_words1, src_plane1))
+        relu = add_and_relu(0, own, gated[0])
+        gated.append(gate(1, *gate_products(1)))
+        own = own_product(1)
+        scatter(0, relu)
+        gated.append(gate(2, *gate_products(2)))
+        grouped_last = keep.tile([P, P, PACK], BF16, name="grouped_last", tag="chain0", align_bytes=64)
+        quantize_wo(3 * P, wo_last, grouped_last[:])
+
+        for u in range(1, len(UNITS)):
+            if u + 1 < len(UNITS):
+                next_own = own_product(u + 1)
+            relu = add_and_relu(u, own, gated[u])
+            own = next_own
+            if u + 2 < len(UNITS):
+                products = gate_products(u + 2)
+            scatter(u, relu)
+            if u + 2 < len(UNITS):
                 gated.append(gate(u + 2, *products))
-            if u == 0:
-                grouped_rest = keep.tile([P, P, PACK], BF16, name="grouped_rest", tag="chain0", align_bytes=64)
-                quantize_wo(3 * P, wo_raw[2], grouped_rest[:])

@@ -43,13 +43,13 @@ def tile_list_rgg_ownrelu_kernel(
 
         src_list = keep.tile([P, J // LANES], U16, name="src_list")
         dst_list = keep.tile([P, J // LANES], U16, name="dst_list")
-        table_plane = keep.tile([P, T // PACK], I32, name="table_plane", align_bytes=64)
+        table_plane = keep.tile([P, T // PACK], I32, name="table_plane", tag="table_plane", align_bytes=64)
         wo_codes = keep.tile([P, N], U32, name="wo_codes", align_bytes=64)
         wo_plane = keep.tile([P, N], U8, name="wo_plane", align_bytes=64)
         identity = keep.tile([P, P], F32, name="identity")
 
         nc.gpsimd.memset(table_plane[:], 0)
-        zeros = held.tile([P, 35 * KIB // 4], F32, name="zeros", offset=0, align_bytes=64)
+        zeros = held.tile([P, 27 * KIB // 4], F32, name="zeros", offset=0, align_bytes=64)
         nc.gpsimd.memset(zeros[:, 0:P], 0.0)
         nc.gpsimd.affine_select(
             out=identity[:], in_=zeros[:, 0:P], compare_op=ALU.not_equal, fill=1.0, base=0,
@@ -70,12 +70,15 @@ def tile_list_rgg_ownrelu_kernel(
         w_planes = held_tile("w_planes", [P, N // PACK], I32, 25)
         nc.gpsimd.memset(w_planes[:], 0)
 
+        warm = keep.tile([P, 2], F32, name="warm")
+        nc.gpsimd.memset(warm[:, 0:1], 0.0)
+        nc.scalar.activation(warm[:, 1:2], warm[:, 0:1], ACT.Sigmoid)
+
         rows_out = [keep.tile([P, T], F32, name="rows_out0")]
         nc.vector.memset(rows_out[0][:, 0 : T - 1], 0.0)
         nc.vector.memset(rows_out[0][:, T - 1 : T], 0.0)
-        for b in range(1, OUT_TILES):
-            rows_out.append(held_tile("rows_out%d" % b, [P, T], F32, 18 + 8 * b))
-            nc.gpsimd.memset(rows_out[b][:], 0.0)
+        rows_out.append(held_tile("rows_out1", [P, T], F32, 26))
+        nc.gpsimd.memset(rows_out[1][:], 0.0)
 
         def load_plane(plane, first_row, scales):
             rows = scales[0].bitcast(I32)
@@ -222,6 +225,8 @@ def tile_list_rgg_ownrelu_kernel(
         src_plane1 = keep.tile([P, HALF], U8, name="src_plane1", tag="eta0", align_bytes=64)
         gather_scales(src_plane1, src_list, HALF, J)
         src.append((src_words1, src_plane1))
+        rows_out.append(keep.tile([P, T], F32, name="rows_out2", tag="table_plane", align_bytes=64))
+        nc.gpsimd.memset(rows_out[2][:], 0.0)
         relu = add_and_relu(0, own, gated[0])
         gated.append(gate(1, *gate_products(1)))
         own = own_product(1)

@@ -21,13 +21,16 @@ PACK = 4
 LANES = 16
 KIB = 1024
 HALF = J // 2
-EDGE_TILES = HALF // P
-UNITS = [(0, 0), (1, 0), (2, 0), (0, 1), (1, 1), (2, 1), (3, 0), (3, 1)]
+CUT_A, CUT_B = 2 * P, 5 * P
+PIECES = [
+    (0, 0, CUT_A), (1, 0, CUT_A), (0, CUT_A, CUT_B), (1, CUT_A, CUT_B), (0, CUT_B, J), (1, CUT_B, J),
+    (2, 0, HALF), (3, 0, HALF), (2, HALF, J), (3, HALF, J),
+]
+FILL_BANKS = {("ms", 0): 0, ("za", 0): 1, ("ow", 0): 1, ("ms", 1): 2, ("ow", 1): 1}
 OUT_TILES = 3
-PRODUCT_BANKS = 4
-VECTOR_GATES = 3
-FUSED_UNITS = (0, 6, 7)
-WC_ROW, WA_ROW, WB_ROW = 0, 4, 8
+WA_ROW, WB_ROW = 0, 4
+FUSED_FROM = len(PIECES) - 2
+GPSIMD_QUADRANTS = 2
 
 
 def tile_list_rgg_ownrelu_kernel(
@@ -37,20 +40,22 @@ def tile_list_rgg_ownrelu_kernel(
     with ExitStack() as ctx:
         keep = ctx.enter_context(tc.tile_pool(name="keep", bufs=1))
         held = ctx.enter_context(tc.tile_pool(name="held", bufs=1))
+        outs = ctx.enter_context(tc.tile_pool(name="outs", bufs=1))
         picks = ctx.enter_context(tc.tile_pool(name="picks", bufs=1))
-        work = ctx.enter_context(tc.tile_pool(name="work", bufs=len(UNITS)))
+        work = ctx.enter_context(tc.tile_pool(name="work", bufs=len(PIECES)))
+        chain = ctx.enter_context(tc.tile_pool(name="chain", bufs=1))
         psum = ctx.enter_context(tc.psum_pool(name="psum", bufs=1))
 
         src_list = keep.tile([P, J // LANES], U16, name="src_list")
         dst_list = keep.tile([P, J // LANES], U16, name="dst_list")
-        table_plane = keep.tile([P, T // PACK], I32, name="table_plane", tag="table_plane", align_bytes=64)
+        table_plane = keep.tile([P, T // PACK], I32, name="table_plane", align_bytes=64)
         wo_codes = keep.tile([P, N], U32, name="wo_codes", align_bytes=64)
         wo_plane = keep.tile([P, N], U8, name="wo_plane", align_bytes=64)
         identity = keep.tile([P, P], F32, name="identity")
 
-        nc.gpsimd.memset(table_plane[:], 0)
-        zeros = held.tile([P, 27 * KIB // 4], F32, name="zeros", offset=0, align_bytes=64)
+        zeros = held.tile([P, 25 * KIB // 4], F32, name="zeros", offset=0, align_bytes=64)
         nc.gpsimd.memset(zeros[:, 0:P], 0.0)
+        nc.gpsimd.memset(table_plane[:], 0)
         nc.gpsimd.affine_select(
             out=identity[:], in_=zeros[:, 0:P], compare_op=ALU.not_equal, fill=1.0, base=0,
             pattern=[[-1, P]], channel_multiplier=1,
@@ -63,185 +68,189 @@ def tile_list_rgg_ownrelu_kernel(
         wa_codes = held_tile("wa_codes", [P, N], I32, 8)
         wb_codes = held_tile("wb_codes", [P, N], I32, 10)
         wc_codes = held_tile("wc_codes", [P, 2 * N], U8, 12)
-        wo_first = held_tile("wo_first", [P, PACK, P], F32, 13)
-        wo_middle = held_tile("wo_middle", [P, PACK, 2 * P], F32, 15)
-        wo_last = held_tile("wo_last", [P, PACK, P], F32, 19)
-        edge_w = [held_tile("edge_w%d" % h, [P, HALF], F32, 21 + 2 * h) for h in range(2)]
-        w_planes = held_tile("w_planes", [P, N // PACK], I32, 25)
+        wo_raw = [held_tile("wo_raw%d" % h, [P, PACK, N // 2], F32, 13 + 4 * h) for h in range(2)]
+        edge_w = held_tile("edge_w", [P, J], F32, 21)
+        w_planes = keep.tile([P, N // PACK], I32, name="w_planes", align_bytes=64)
         nc.gpsimd.memset(w_planes[:], 0)
+        wc_plane = keep.tile([P, N // PACK], I32, name="wc_plane", align_bytes=64)
+        nc.vector.memset(wc_plane[0 : 32 * GPSIMD_QUADRANTS, :], 0)
+        nc.gpsimd.memset(wc_plane[32 * GPSIMD_QUADRANTS : P, :], 0)
 
-        warm = keep.tile([P, 2], F32, name="warm")
+        warm = outs.tile([P, 32], F32, name="warm", offset=8 * KIB - 64, align_bytes=64)
         nc.gpsimd.memset(warm[:, 0:1], 0.0)
         nc.scalar.activation(warm[:, 1:2], warm[:, 0:1], ACT.Sigmoid)
 
-        rows_out = [keep.tile([P, T], F32, name="rows_out0")]
-        nc.vector.memset(rows_out[0][:, 0 : T - 1], 0.0)
-        nc.vector.memset(rows_out[0][:, T - 1 : T], 0.0)
-        rows_out.append(held_tile("rows_out1", [P, T], F32, 26))
-        nc.gpsimd.memset(rows_out[1][:], 0.0)
-
-        def load_plane(plane, first_row, scales):
+        def load_quadrant(queue, plane, first_row, scales, q):
             rows = scales[0].bitcast(I32)
-            for q in range(4):
-                nc.sync.dma_start(plane[32 * q + first_row : 32 * q + first_row + 4, :], rows[4 * q : 4 * (q + 1), :])
+            queue.dma_start(plane[32 * q + first_row : 32 * q + first_row + 4, :], rows[4 * q : 4 * (q + 1), :])
 
         def load_words(codes, words):
             nc.sync.dma_start(codes[:], words[0].rearrange("p c i -> p (c i)").bitcast(I32))
 
+        for q in range(GPSIMD_QUADRANTS):
+            load_quadrant(nc.gpsimd, wc_plane, 0, wc_scales, q)
+
+        rows_out = [keep.tile([P, T], F32, name="rows_out0")]
+        nc.vector.memset(rows_out[0][:, 0 : T - 1], 0.0)
+        nc.vector.memset(rows_out[0][:, T - 1 : T], 0.0)
+        for b in range(1, OUT_TILES):
+            rows_out.append(outs.tile([P, T], F32, name="rows_out%d" % b, offset=8 * (b - 1) * KIB, align_bytes=64))
+            nc.gpsimd.memset(rows_out[b][:], 0.0)
+
         wo_rows = wo.rearrange("(p i) n -> p i n", i=PACK)
         nc.sync.dma_start(dst_list[:], offs2)
+        for q in range(4):
+            load_quadrant(nc.sync, table_plane, 0, tab_scales, q)
         nc.sync.dma_start(src_list[:], offs)
-        load_plane(table_plane, 0, tab_scales)
         load_words(table_words, tab_words)
-        nc.sync.dma_start(wo_first[:], wo_rows[:, :, 0:P])
-        load_plane(w_planes, WC_ROW, wc_scales)
-        nc.sync.dma_start(wc_codes[:].bitcast(I32), wc_words[0].bitcast(I32))
         load_words(wa_codes, wa_words)
-        load_plane(w_planes, WA_ROW, wa_scales)
+        for q in range(4):
+            load_quadrant(nc.sync, w_planes, WA_ROW, wa_scales, q)
+        load_quadrant(nc.sync, wc_plane, 0, wc_scales, 2)
+        nc.sync.dma_start(wo_raw[0][:], wo_rows[:, :, 0 : N // 2])
         load_words(wb_codes, wb_words)
-        nc.sync.dma_start(wo_middle[:], wo_rows[:, :, P : 3 * P])
-        load_plane(w_planes, WB_ROW, wb_scales)
-        nc.sync.dma_start(edge_w[0][:], wgo[:, 0:HALF])
-        nc.sync.dma_start(wo_last[:], wo_rows[:, :, 3 * P : N])
-        nc.sync.dma_start(edge_w[1][:], wgo[:, HALF:J])
+        nc.sync.dma_start(wc_codes[:].bitcast(I32), wc_words[0].bitcast(I32))
+        load_quadrant(nc.sync, wc_plane, 0, wc_scales, 3)
+        for q in range(4):
+            load_quadrant(nc.sync, w_planes, WB_ROW, wb_scales, q)
+        nc.sync.dma_start(edge_w[:, 0:CUT_A], wgo[:, 0:CUT_A])
+        nc.sync.dma_start(wo_raw[1][:], wo_rows[:, :, N // 2 : N])
+        nc.sync.dma_start(edge_w[:, CUT_A:J], wgo[:, CUT_A:J])
 
         def entries(offsets, j0, j1):
             return offsets[:, j0 // LANES : j1 // LANES]
 
-        def gather_scales(picked, offsets, j0, j1):
-            nc.vector.tensor_copy(picked[:], table_plane[:].bitcast(U8).indirect(entries(offsets, j0, j1)))
+        words_of = {"dst": {}, "src": {}}
+        scales_of = {"dst": {}, "src": {}}
+        lists = {"dst": dst_list, "src": src_list}
 
-        def gather_words(picked, offsets, h):
-            window = table_words[:].bitcast(U32)
-            nc.vector.tensor_copy(picked[:], window.indirect(entries(offsets, h * HALF, (h + 1) * HALF)))
+        def gather(found, window, picked, side, j0, j1):
+            nc.vector.tensor_copy(picked[:], window.indirect(entries(lists[side], j0, j1)))
+            for j in range(j0, j1, P):
+                found[side][j] = picked[:, j - j0 : j - j0 + P]
 
-        def quantize_wo(n0, raw, grouped):
-            n1 = n0 + raw.shape[2]
-            nc.scalar.copy(grouped, raw[:].rearrange("p i n -> p n i"))
+        def gather_scales(picked, side, j0, j1):
+            gather(scales_of, table_plane[:].bitcast(U8), picked, side, j0, j1)
+
+        def gather_words(picked, side, j0, j1):
+            gather(words_of, table_words[:].bitcast(U32), picked, side, j0, j1)
+
+        def quantize_wo(n0, n1, grouped):
+            raw = wo_raw[n0 // (N // 2)][:, :, n0 % (N // 2) : n0 % (N // 2) + n1 - n0]
+            nc.scalar.copy(grouped, raw.rearrange("p i n -> p n i"))
             nc.vector.quantize_mx(
                 out=wo_codes[:, n0:n1].bitcast(FP8X4),
                 scales=wo_plane[:, n0:n1],
                 in_=grouped.rearrange("p n i -> p (n i)"),
             )
 
-        def product(bank, e, picked, weight, start, stop):
-            edges = slice(e * P, (e + 1) * P)
-            nc.tensor.matmul_mx(
-                out=bank[:, edges], lhsT=picked[0][:, edges].bitcast(FP8X4), lhsT_scale=picked[1][:, edges],
-                rhs=weight[0], rhs_scale=weight[1], start=start, stop=stop,
-            )
+        def bank(role, u):
+            width = PIECES[u][2] - PIECES[u][1]
+            if role == "total":
+                place = 4 + u % 2 if u else 3
+            else:
+                place = FILL_BANKS.get((role, u), {"ms": 1, "za": 2, "ow": 3}[role])
+            return psum.tile([P, width], F32, name="%s%d" % (role, u), offset=place * 2 * KIB)
 
-        def product_bank(name, u, ahead):
-            tag = "product_bank%d" % ((u - ahead) % PRODUCT_BANKS)
-            return psum.tile([P, HALF], F32, name="%s%d" % (name, u), tag=tag)
+        def chained(name, shape, dtype, place):
+            return chain.tile(shape, dtype, name=name, offset=place * 2 * KIB, align_bytes=64)
+
+        def product(acc, u, passes):
+            nt, j0, j1 = PIECES[u]
+            for j in range(j0, j1, P):
+                for n, (side, codes, plane) in enumerate(passes):
+                    nc.tensor.matmul_mx(
+                        out=acc[:, j - j0 : j - j0 + P], lhsT=words_of[side][j].bitcast(FP8X4),
+                        lhsT_scale=scales_of[side][j], rhs=codes, rhs_scale=plane,
+                        start=n == 0, stop=n == len(passes) - 1,
+                    )
 
         def gate_products(u):
-            nt, h = UNITS[u]
+            nt, j0, j1 = PIECES[u]
             cols = slice(nt * P, (nt + 1) * P)
             planes = w_planes[:].bitcast(U8)
-            za = product_bank("za", u, 2)
-            for e in range(EDGE_TILES):
-                product(za, e, dst[h], (wa_codes[:, cols].bitcast(FP8X4), planes[WA_ROW:, cols]), True, False)
-                product(za, e, src[h], (wb_codes[:, cols].bitcast(FP8X4), planes[WB_ROW:, cols]), False, True)
-            eta = keep.tile([P, HALF], F32, name="eta%d" % u, tag="eta%d" % u, align_bytes=64)
+            za = bank("za", u)
+            product(za, u, [
+                ("dst", wa_codes[:, cols].bitcast(FP8X4), planes[WA_ROW:, cols]),
+                ("src", wb_codes[:, cols].bitcast(FP8X4), planes[WB_ROW:, cols]),
+            ])
+            eta = work.tile([P, j1 - j0], F32, name="eta")
             nc.scalar.activation(eta[:], za[:], ACT.Sigmoid)
-            ms = product_bank("ms", u, 0)
+            ms = bank("ms", u)
             wc_cols = wc_codes[:, 2 * nt * P : 2 * (nt + 1) * P].bitcast(FP4X4)
-            for e in range(EDGE_TILES):
-                product(ms, e, src[h], (wc_cols, planes[WC_ROW:, cols]), True, True)
-            if u < VECTOR_GATES:
-                return ms, eta
-            message = work.tile([P, HALF], F32, name="message")
+            product(ms, u, [("src", wc_cols, wc_plane[:].bitcast(U8)[:, cols])])
+            message = work.tile([P, j1 - j0], F32, name="message")
             nc.scalar.copy(message[:], ms[:])
             return message, eta
 
         def own_product(u):
-            nt, h = UNITS[u]
+            nt, j0, j1 = PIECES[u]
             cols = slice(nt * P, (nt + 1) * P)
-            ow = product_bank("ow", u, 1)
-            for e in range(EDGE_TILES):
-                product(ow, e, dst[h], (wo_codes[:, cols].bitcast(FP8X4), wo_plane[:, cols]), True, True)
-            own = work.tile([P, HALF], F32, name="own")
+            ow = bank("ow", u)
+            product(ow, u, [("dst", wo_codes[:, cols].bitcast(FP8X4), wo_plane[:, cols])])
+            own = work.tile([P, j1 - j0], F32, name="own")
             nc.scalar.copy(own[:], ow[:])
             return own
 
         def gate(u, message, eta):
-            gated = keep.tile([P, HALF], F32, name="gated%d" % u, tag="chain%d" % u, align_bytes=64)
-            engine = nc.vector if u < VECTOR_GATES else nc.gpsimd
-            engine.tensor_tensor(gated[:], message[:], eta[:], ALU.mult)
+            nt, j0, j1 = PIECES[u]
+            gated = chained("gated%d" % u, [P, j1 - j0], F32, u)
+            nc.gpsimd.tensor_tensor(gated[:], message[:], eta[:], ALU.mult)
             return gated
 
         def add_and_relu(u, own, gated):
-            total = psum.tile([P, HALF], F32, name="total", bufs=8 - PRODUCT_BANKS)
+            nt, j0, j1 = PIECES[u]
+            total = bank("total", u)
             for n, summand in enumerate((own, gated)):
-                for e in range(EDGE_TILES):
-                    edges = slice(e * P, (e + 1) * P)
+                for c in range(0, j1 - j0, P):
                     nc.tensor.matmul(
-                        total[:, edges], summand[:, edges], identity[:], is_transpose=True,
-                        start=(n, e) == (0, 0), stop=(n, e) == (1, EDGE_TILES - 1),
+                        total[:, c : c + P], summand[:, c : c + P], identity[:], is_transpose=True,
+                        start=(n, c) == (0, 0), stop=(n, c) == (1, j1 - j0 - P),
                     )
-            relu = keep.tile([P, HALF], F32, name="relu%d" % u, tag="chain%d" % (u + 2), align_bytes=64)
+            relu = chained("relu%d" % u, [P, j1 - j0], F32, u + 2)
             nc.scalar.activation(relu[:], total[:], ACT.Relu)
             return relu
 
         def scatter(u, relu):
-            nt, h = UNITS[u]
+            nt, j0, j1 = PIECES[u]
             rows = rows_out[nt % OUT_TILES]
-            if u in FUSED_UNITS:
-                window = rows[:].indirect(entries(dst_list, h * HALF, (h + 1) * HALF))
-                nc.vector.tensor_tensor(window, relu[:], edge_w[h][:], ALU.mult)
+            weights = edge_w[:, j0:j1]
+            window = rows[:].indirect(entries(dst_list, j0, j1))
+            if u >= FUSED_FROM:
+                nc.vector.tensor_tensor(window, relu[:], weights, ALU.mult)
             else:
-                width = HALF // 2 if u - 1 in FUSED_UNITS else HALF
-                for c in range(0, HALF, width):
-                    weighted = work.tile([P, width], F32, name="weighted")
-                    nc.gpsimd.tensor_tensor(weighted[:], relu[:, c : c + width], edge_w[h][:, c : c + width], ALU.mult)
-                    window = rows[:].indirect(entries(dst_list, h * HALF + c, h * HALF + c + width))
-                    nc.vector.tensor_copy(window, weighted[:])
-            if h == 1:
+                weighted = work.tile([P, j1 - j0], F32, name="weighted")
+                nc.gpsimd.tensor_tensor(weighted[:], relu[:], weights, ALU.mult)
+                nc.vector.tensor_copy(window, weighted[:])
+            if j1 == J:
                 nc.sync.dma_start(out[nt * P : (nt + 1) * P, :], rows[:])
 
-        dst_plane = keep.tile([P, J], U8, name="dst_plane", align_bytes=64)
-        gather_scales(dst_plane, dst_list, 0, J)
-        src_plane0 = keep.tile([P, HALF], U8, name="src_plane0", align_bytes=64)
-        gather_scales(src_plane0, src_list, 0, HALF)
-        dst_words0 = keep.tile([P, HALF], U32, name="dst_words0", align_bytes=64)
-        gather_words(dst_words0, dst_list, 0)
+        gather_scales(keep.tile([P, J], U8, name="dst_plane", align_bytes=64), "dst", 0, J)
+        gather_scales(keep.tile([P, CUT_B], U8, name="src_plane0", align_bytes=64), "src", 0, CUT_B)
+        for side in ("dst", "src"):
+            gather_words(keep.tile([P, CUT_A], U32, name=side + "_words0", align_bytes=64), side, 0, CUT_A)
+        grouped = picks.tile([P, N + N // 2 + 64, PACK], BF16, name="grouped0", offset=0, align_bytes=64)
+        quantize_wo(0, N // 2, grouped[:, 0 : N // 2, :])
+        rest = CUT_B - CUT_A
+        for n, side in enumerate(("dst", "src")):
+            picked = picks.tile([P, rest], U32, name=side + "_words1", offset=n * 4 * rest, align_bytes=64)
+            gather_words(picked, side, CUT_A, CUT_B)
+        gather_scales(picks.tile([P, rest], U8, name="src_plane1", offset=16 * rest, align_bytes=64), "src", CUT_B, J)
+        for n, side in enumerate(("dst", "src")):
+            picked = picks.tile([P, rest], U32, name=side + "_words2", offset=(n + 2) * 4 * rest, align_bytes=64)
+            gather_words(picked, side, CUT_B, J)
 
-        grouped_first = picks.tile([P, 2 * P + 32, PACK], BF16, name="grouped_first", offset=2 * KIB - 128, align_bytes=64)
-        quantize_wo(0, wo_first, grouped_first[:, 0:P, :])
-        src_words0 = picks.tile([P, HALF], U32, name="src_words0", offset=4 * KIB, align_bytes=64)
-        gather_words(src_words0, src_list, 0)
-        dst_words1 = picks.tile([P, HALF], U32, name="dst_words1", offset=0, align_bytes=64)
-        gather_words(dst_words1, dst_list, 1)
-        src_words1 = picks.tile([P, HALF], U32, name="src_words1", offset=2 * KIB, align_bytes=64)
-        gather_words(src_words1, src_list, 1)
-        dst = [(dst_words0, dst_plane[:, 0:HALF]), (dst_words1, dst_plane[:, HALF:J])]
-        src = [(src_words0, src_plane0)]
-
-        own = own_product(0)
         gated = [gate(0, *gate_products(0))]
-        grouped_middle = keep.tile([P, 2 * P, PACK], BF16, name="grouped_middle", align_bytes=64)
-        quantize_wo(P, wo_middle, grouped_middle[:])
-        src_plane1 = keep.tile([P, HALF], U8, name="src_plane1", tag="eta0", align_bytes=64)
-        gather_scales(src_plane1, src_list, HALF, J)
-        src.append((src_words1, src_plane1))
-        rows_out.append(keep.tile([P, T], F32, name="rows_out2", tag="table_plane", align_bytes=64))
-        nc.gpsimd.memset(rows_out[2][:], 0.0)
-        relu = add_and_relu(0, own, gated[0])
+        own = own_product(0)
         gated.append(gate(1, *gate_products(1)))
-        own = own_product(1)
-        scatter(0, relu)
-        gated.append(gate(2, *gate_products(2)))
-        grouped_last = keep.tile([P, P, PACK], BF16, name="grouped_last", tag="chain0", align_bytes=64)
-        quantize_wo(3 * P, wo_last, grouped_last[:])
-
-        for u in range(1, len(UNITS)):
-            if u + 1 < len(UNITS):
-                next_own = own_product(u + 1)
+        for u in range(len(PIECES)):
             relu = add_and_relu(u, own, gated[u])
-            own = next_own
-            if u + 2 < len(UNITS):
+            if u in (3, 4):
+                quantize_wo((u - 1) * P, u * P, chained("grouped%d" % u, [P, P, PACK], BF16, u)[:])
+            if u + 1 < len(PIECES):
+                own = own_product(u + 1)
+            if u + 2 < len(PIECES):
                 products = gate_products(u + 2)
             scatter(u, relu)
-            if u + 2 < len(UNITS):
+            if u + 2 < len(PIECES):
                 gated.append(gate(u + 2, *products))

@@ -21,16 +21,19 @@ PACK = 4
 LANES = 16
 KIB = 1024
 HALF = J // 2
-CUT_A, CUT_B = 2 * P, 5 * P
 PIECES = [
-    (0, 0, CUT_A), (1, 0, CUT_A), (0, CUT_A, CUT_B), (1, CUT_A, CUT_B), (0, CUT_B, J), (1, CUT_B, J),
-    (2, 0, HALF), (3, 0, HALF), (2, HALF, J), (3, HALF, J),
+    (0, 0, HALF), (1, 0, HALF), (2, 0, HALF), (0, HALF, J), (1, HALF, J), (2, HALF, J), (3, 0, HALF), (3, HALF, J),
 ]
-FILL_BANKS = {("ms", 0): 0, ("za", 0): 1, ("ow", 0): 1, ("ms", 1): 2, ("ow", 1): 1}
 OUT_TILES = 3
-WA_ROW, WB_ROW = 0, 4
-FUSED_FROM = len(PIECES) - 2
-GPSIMD_QUADRANTS = 2
+WC_ROW, WA_ROW, WB_ROW = 0, 4, 8
+VECTOR_GATES = 3
+FUSED = (0, 5, 6, 7)
+BANKS = {
+    "za": [3, 7, 3, 5, 3, 5, 3, 5],
+    "ms": [0, 1, 2, 1, 2, 1, 2, 1],
+    "ow": [4, 0, 4, 0, 4, 0, 4, 0],
+    "total": [7, 6, 7, 6, 7, 6, 7, 6],
+}
 
 
 def tile_list_rgg_ownrelu_kernel(
@@ -40,7 +43,6 @@ def tile_list_rgg_ownrelu_kernel(
     with ExitStack() as ctx:
         keep = ctx.enter_context(tc.tile_pool(name="keep", bufs=1))
         held = ctx.enter_context(tc.tile_pool(name="held", bufs=1))
-        outs = ctx.enter_context(tc.tile_pool(name="outs", bufs=1))
         picks = ctx.enter_context(tc.tile_pool(name="picks", bufs=1))
         work = ctx.enter_context(tc.tile_pool(name="work", bufs=len(PIECES)))
         chain = ctx.enter_context(tc.tile_pool(name="chain", bufs=1))
@@ -53,16 +55,16 @@ def tile_list_rgg_ownrelu_kernel(
         wo_plane = keep.tile([P, N], U8, name="wo_plane", align_bytes=64)
         identity = keep.tile([P, P], F32, name="identity")
 
-        zeros = held.tile([P, 25 * KIB // 4], F32, name="zeros", offset=0, align_bytes=64)
-        nc.gpsimd.memset(zeros[:, 0:P], 0.0)
         nc.gpsimd.memset(table_plane[:], 0)
+        zeros = held.tile([P, 26 * KIB // 4], F32, name="zeros", offset=0, align_bytes=64)
+        nc.gpsimd.memset(zeros[:, 0:P], 0.0)
         nc.gpsimd.affine_select(
             out=identity[:], in_=zeros[:, 0:P], compare_op=ALU.not_equal, fill=1.0, base=0,
             pattern=[[-1, P]], channel_multiplier=1,
         )
 
         def held_tile(name, shape, dtype, kib):
-            return held.tile(shape, dtype, name=name, offset=kib * KIB, align_bytes=64)
+            return held.tile(shape, dtype, name=name, offset=int(kib * KIB), align_bytes=64)
 
         table_words = held_tile("table_words", [P, T], I32, 0)
         wa_codes = held_tile("wa_codes", [P, N], I32, 8)
@@ -70,52 +72,46 @@ def tile_list_rgg_ownrelu_kernel(
         wc_codes = held_tile("wc_codes", [P, 2 * N], U8, 12)
         wo_raw = [held_tile("wo_raw%d" % h, [P, PACK, N // 2], F32, 13 + 4 * h) for h in range(2)]
         edge_w = held_tile("edge_w", [P, J], F32, 21)
-        w_planes = keep.tile([P, N // PACK], I32, name="w_planes", align_bytes=64)
+        last_relu = keep.tile([P, J], F32, name="last_relu")
+        w_planes = held_tile("w_planes", [P, N // PACK], I32, 25)
         nc.gpsimd.memset(w_planes[:], 0)
-        wc_plane = keep.tile([P, N // PACK], I32, name="wc_plane", align_bytes=64)
-        nc.vector.memset(wc_plane[0 : 32 * GPSIMD_QUADRANTS, :], 0)
-        nc.gpsimd.memset(wc_plane[32 * GPSIMD_QUADRANTS : P, :], 0)
 
-        warm = outs.tile([P, 32], F32, name="warm", offset=8 * KIB - 64, align_bytes=64)
+        def load_rows(first_row, scales, quadrants, plane, queue=nc.sync):
+            rows = scales[0].bitcast(I32)
+            for q in quadrants:
+                queue.dma_start(plane[32 * q + first_row : 32 * q + first_row + 4, :], rows[4 * q : 4 * (q + 1), :])
+
+        load_rows(0, tab_scales, range(2, 4), table_plane, nc.scalar)
+        warm = keep.tile([P, 2], F32, name="warm")
         nc.gpsimd.memset(warm[:, 0:1], 0.0)
         nc.scalar.activation(warm[:, 1:2], warm[:, 0:1], ACT.Sigmoid)
-
-        def load_quadrant(queue, plane, first_row, scales, q):
-            rows = scales[0].bitcast(I32)
-            queue.dma_start(plane[32 * q + first_row : 32 * q + first_row + 4, :], rows[4 * q : 4 * (q + 1), :])
-
-        def load_words(codes, words):
-            nc.sync.dma_start(codes[:], words[0].rearrange("p c i -> p (c i)").bitcast(I32))
-
-        for q in range(GPSIMD_QUADRANTS):
-            load_quadrant(nc.gpsimd, wc_plane, 0, wc_scales, q)
 
         rows_out = [keep.tile([P, T], F32, name="rows_out0")]
         nc.vector.memset(rows_out[0][:, 0 : T - 1], 0.0)
         nc.vector.memset(rows_out[0][:, T - 1 : T], 0.0)
-        for b in range(1, OUT_TILES):
-            rows_out.append(outs.tile([P, T], F32, name="rows_out%d" % b, offset=8 * (b - 1) * KIB, align_bytes=64))
-            nc.gpsimd.memset(rows_out[b][:], 0.0)
+        rows_out.append(held_tile("rows_out1", [P, T], F32, 25.5))
+        nc.gpsimd.memset(rows_out[1][:], 0.0)
+
+        def load_words(codes, words):
+            nc.sync.dma_start(codes[:], words[0].rearrange("p c i -> p (c i)").bitcast(I32))
 
         wo_rows = wo.rearrange("(p i) n -> p i n", i=PACK)
         nc.sync.dma_start(dst_list[:], offs2)
-        for q in range(4):
-            load_quadrant(nc.sync, table_plane, 0, tab_scales, q)
+        load_rows(0, tab_scales, range(2), table_plane)
         nc.sync.dma_start(src_list[:], offs)
-        load_words(table_words, tab_words)
         load_words(wa_codes, wa_words)
-        for q in range(4):
-            load_quadrant(nc.sync, w_planes, WA_ROW, wa_scales, q)
-        load_quadrant(nc.sync, wc_plane, 0, wc_scales, 2)
+        load_words(table_words, tab_words)
+        load_rows(WA_ROW, wa_scales, range(4), w_planes)
+        load_rows(WC_ROW, wc_scales, range(1), w_planes)
         nc.sync.dma_start(wo_raw[0][:], wo_rows[:, :, 0 : N // 2])
+        load_rows(WC_ROW, wc_scales, range(1, 2), w_planes)
         load_words(wb_codes, wb_words)
         nc.sync.dma_start(wc_codes[:].bitcast(I32), wc_words[0].bitcast(I32))
-        load_quadrant(nc.sync, wc_plane, 0, wc_scales, 3)
-        for q in range(4):
-            load_quadrant(nc.sync, w_planes, WB_ROW, wb_scales, q)
-        nc.sync.dma_start(edge_w[:, 0:CUT_A], wgo[:, 0:CUT_A])
+        load_rows(WC_ROW, wc_scales, range(2, 4), w_planes)
+        load_rows(WB_ROW, wb_scales, range(4), w_planes)
         nc.sync.dma_start(wo_raw[1][:], wo_rows[:, :, N // 2 : N])
-        nc.sync.dma_start(edge_w[:, CUT_A:J], wgo[:, CUT_A:J])
+        for h in range(2):
+            nc.sync.dma_start(edge_w[:, h * HALF : (h + 1) * HALF], wgo[:, h * HALF : (h + 1) * HALF])
 
         def entries(offsets, j0, j1):
             return offsets[:, j0 // LANES : j1 // LANES]
@@ -146,10 +142,7 @@ def tile_list_rgg_ownrelu_kernel(
 
         def bank(role, u):
             width = PIECES[u][2] - PIECES[u][1]
-            if role == "total":
-                place = 4 + u % 2 if u else 3
-            else:
-                place = FILL_BANKS.get((role, u), {"ms": 1, "za": 2, "ow": 3}[role])
+            place = BANKS[role][u]
             return psum.tile([P, width], F32, name="%s%d" % (role, u), offset=place * 2 * KIB)
 
         def chained(name, shape, dtype, place):
@@ -174,11 +167,16 @@ def tile_list_rgg_ownrelu_kernel(
                 ("dst", wa_codes[:, cols].bitcast(FP8X4), planes[WA_ROW:, cols]),
                 ("src", wb_codes[:, cols].bitcast(FP8X4), planes[WB_ROW:, cols]),
             ])
-            eta = work.tile([P, j1 - j0], F32, name="eta")
-            nc.scalar.activation(eta[:], za[:], ACT.Sigmoid)
+            if u == 0:
+                eta = picks.tile([P, 3 * HALF // 2], F32, name="eta0", offset=5 * KIB, align_bytes=64)[:, 0:HALF]
+            else:
+                eta = work.tile([P, j1 - j0], F32, name="eta")[:]
+            nc.scalar.activation(eta, za[:], ACT.Sigmoid)
             ms = bank("ms", u)
             wc_cols = wc_codes[:, 2 * nt * P : 2 * (nt + 1) * P].bitcast(FP4X4)
-            product(ms, u, [("src", wc_cols, wc_plane[:].bitcast(U8)[:, cols])])
+            product(ms, u, [("src", wc_cols, planes[WC_ROW:, cols])])
+            if u < VECTOR_GATES:
+                return ms, eta
             message = work.tile([P, j1 - j0], F32, name="message")
             nc.scalar.copy(message[:], ms[:])
             return message, eta
@@ -195,7 +193,8 @@ def tile_list_rgg_ownrelu_kernel(
         def gate(u, message, eta):
             nt, j0, j1 = PIECES[u]
             gated = chained("gated%d" % u, [P, j1 - j0], F32, u)
-            nc.gpsimd.tensor_tensor(gated[:], message[:], eta[:], ALU.mult)
+            engine = nc.vector if u < VECTOR_GATES else nc.gpsimd
+            engine.tensor_tensor(gated[:], message[:], eta, ALU.mult)
             return gated
 
         def add_and_relu(u, own, gated):
@@ -207,50 +206,59 @@ def tile_list_rgg_ownrelu_kernel(
                         total[:, c : c + P], summand[:, c : c + P], identity[:], is_transpose=True,
                         start=(n, c) == (0, 0), stop=(n, c) == (1, j1 - j0 - P),
                     )
-            relu = chained("relu%d" % u, [P, j1 - j0], F32, u + 2)
-            nc.scalar.activation(relu[:], total[:], ACT.Relu)
+            if nt == 3:
+                relu = last_relu[:, j0:j1]
+            else:
+                relu = chained("relu%d" % u, [P, j1 - j0], F32, u + 8 if u in FUSED else u + 2)[:]
+            nc.scalar.activation(relu, total[:], ACT.Relu)
             return relu
 
         def scatter(u, relu):
             nt, j0, j1 = PIECES[u]
             rows = rows_out[nt % OUT_TILES]
+            if nt == 3:
+                if j1 < J:
+                    return
+                j0, relu = 0, last_relu[:]
             weights = edge_w[:, j0:j1]
             window = rows[:].indirect(entries(dst_list, j0, j1))
-            if u >= FUSED_FROM:
-                nc.vector.tensor_tensor(window, relu[:], weights, ALU.mult)
+            if u in FUSED:
+                nc.vector.tensor_tensor(window, relu, weights, ALU.mult)
             else:
                 weighted = work.tile([P, j1 - j0], F32, name="weighted")
-                nc.gpsimd.tensor_tensor(weighted[:], relu[:], weights, ALU.mult)
+                engine = nc.vector if u - 1 in FUSED else nc.gpsimd
+                engine.tensor_tensor(weighted[:], relu, weights, ALU.mult)
                 nc.vector.tensor_copy(window, weighted[:])
             if j1 == J:
                 nc.sync.dma_start(out[nt * P : (nt + 1) * P, :], rows[:])
 
         gather_scales(keep.tile([P, J], U8, name="dst_plane", align_bytes=64), "dst", 0, J)
-        gather_scales(keep.tile([P, CUT_B], U8, name="src_plane0", align_bytes=64), "src", 0, CUT_B)
+        gather_scales(keep.tile([P, HALF], U8, name="src_plane0", align_bytes=64), "src", 0, HALF)
         for side in ("dst", "src"):
-            gather_words(keep.tile([P, CUT_A], U32, name=side + "_words0", align_bytes=64), side, 0, CUT_A)
-        grouped = picks.tile([P, N + N // 2 + 64, PACK], BF16, name="grouped0", offset=0, align_bytes=64)
-        quantize_wo(0, N // 2, grouped[:, 0 : N // 2, :])
-        rest = CUT_B - CUT_A
-        for n, side in enumerate(("dst", "src")):
-            picked = picks.tile([P, rest], U32, name=side + "_words1", offset=n * 4 * rest, align_bytes=64)
-            gather_words(picked, side, CUT_A, CUT_B)
-        gather_scales(picks.tile([P, rest], U8, name="src_plane1", offset=16 * rest, align_bytes=64), "src", CUT_B, J)
-        for n, side in enumerate(("dst", "src")):
-            picked = picks.tile([P, rest], U32, name=side + "_words2", offset=(n + 2) * 4 * rest, align_bytes=64)
-            gather_words(picked, side, CUT_B, J)
+            gather_words(keep.tile([P, HALF], U32, name=side + "_words0", align_bytes=64), side, 0, HALF)
+        grouped = picks.tile([P, N // 2, PACK], BF16, name="grouped0", offset=KIB, align_bytes=64)
+        quantize_wo(0, N // 2, grouped[:])
+        gather_words(picks.tile([P, HALF], U32, name="dst_words1", offset=0, align_bytes=64), "dst", HALF, J)
+        gather_scales(picks.tile([P, HALF], U8, name="src_plane1", offset=2 * KIB, align_bytes=64), "src", HALF, J)
 
-        gated = [gate(0, *gate_products(0))]
         own = own_product(0)
+        gated = [gate(0, *gate_products(0))]
+        gather_words(picks.tile([P, HALF], U32, name="src_words1", offset=5 * KIB, align_bytes=64), "src", HALF, J)
         gated.append(gate(1, *gate_products(1)))
+        grouped = picks.tile([P, P, PACK], BF16, name="grouped2", offset=7 * KIB, align_bytes=64)
+        quantize_wo(2 * P, 3 * P, grouped[:])
+        rows_out.append(picks.tile([P, T], F32, name="rows_out2", offset=7 * KIB, align_bytes=64))
+        nc.gpsimd.memset(rows_out[2][:], 0.0)
+        gated.append(gate(2, *gate_products(2)))
         for u in range(len(PIECES)):
             relu = add_and_relu(u, own, gated[u])
-            if u in (3, 4):
-                quantize_wo((u - 1) * P, u * P, chained("grouped%d" % u, [P, P, PACK], BF16, u)[:])
+            if u == 0:
+                quantize_wo(3 * P, N, chained("grouped3", [P, P, PACK], BF16, 0)[:])
             if u + 1 < len(PIECES):
                 own = own_product(u + 1)
-            if u + 2 < len(PIECES):
+            ahead = u + 2 in range(VECTOR_GATES, len(PIECES))
+            if ahead:
                 products = gate_products(u + 2)
             scatter(u, relu)
-            if u + 2 < len(PIECES):
+            if ahead:
                 gated.append(gate(u + 2, *products))

@@ -27,7 +27,7 @@ PIECES = [
 OUT_TILES = 3
 WC_ROW, WA_ROW, WB_ROW = 0, 4, 8
 VECTOR_GATES = 3
-FUSED = (0, 5, 6, 7)
+FUSED = (0, 6, 7)
 BANKS = {
     "za": [3, 7, 3, 5, 3, 5, 3, 5],
     "ms": [0, 1, 2, 1, 2, 1, 2, 1],
@@ -72,16 +72,14 @@ def tile_list_rgg_ownrelu_kernel(
         wc_codes = held_tile("wc_codes", [P, 2 * N], U8, 12)
         wo_raw = [held_tile("wo_raw%d" % h, [P, PACK, N // 2], F32, 13 + 4 * h) for h in range(2)]
         edge_w = held_tile("edge_w", [P, J], F32, 21)
-        last_relu = keep.tile([P, J], F32, name="last_relu")
         w_planes = held_tile("w_planes", [P, N // PACK], I32, 25)
         nc.gpsimd.memset(w_planes[:], 0)
 
-        def load_rows(first_row, scales, quadrants, plane, queue=nc.sync):
+        def load_rows(first_row, scales, quadrants, plane):
             rows = scales[0].bitcast(I32)
             for q in quadrants:
-                queue.dma_start(plane[32 * q + first_row : 32 * q + first_row + 4, :], rows[4 * q : 4 * (q + 1), :])
+                nc.sync.dma_start(plane[32 * q + first_row : 32 * q + first_row + 4, :], rows[4 * q : 4 * (q + 1), :])
 
-        load_rows(0, tab_scales, range(2, 4), table_plane, nc.scalar)
         warm = keep.tile([P, 2], F32, name="warm")
         nc.gpsimd.memset(warm[:, 0:1], 0.0)
         nc.scalar.activation(warm[:, 1:2], warm[:, 0:1], ACT.Sigmoid)
@@ -97,7 +95,7 @@ def tile_list_rgg_ownrelu_kernel(
 
         wo_rows = wo.rearrange("(p i) n -> p i n", i=PACK)
         nc.sync.dma_start(dst_list[:], offs2)
-        load_rows(0, tab_scales, range(2), table_plane)
+        load_rows(0, tab_scales, range(4), table_plane)
         nc.sync.dma_start(src_list[:], offs)
         load_words(wa_codes, wa_words)
         load_words(table_words, tab_words)
@@ -206,20 +204,13 @@ def tile_list_rgg_ownrelu_kernel(
                         total[:, c : c + P], summand[:, c : c + P], identity[:], is_transpose=True,
                         start=(n, c) == (0, 0), stop=(n, c) == (1, j1 - j0 - P),
                     )
-            if nt == 3:
-                relu = last_relu[:, j0:j1]
-            else:
-                relu = chained("relu%d" % u, [P, j1 - j0], F32, u + 8 if u in FUSED else u + 2)[:]
+            relu = chained("relu%d" % u, [P, j1 - j0], F32, u + 8 if u in FUSED else u + 2)[:]
             nc.scalar.activation(relu, total[:], ACT.Relu)
             return relu
 
         def scatter(u, relu):
             nt, j0, j1 = PIECES[u]
             rows = rows_out[nt % OUT_TILES]
-            if nt == 3:
-                if j1 < J:
-                    return
-                j0, relu = 0, last_relu[:]
             weights = edge_w[:, j0:j1]
             window = rows[:].indirect(entries(dst_list, j0, j1))
             if u in FUSED:

@@ -26,13 +26,13 @@ PIECES = [
 ]
 OUT_TILES = 3
 WC_ROW, WA_ROW, WB_ROW = 0, 4, 8
-VECTOR_GATES = 3
-FUSED = (0, 6, 7)
+VECTOR_GATES = 2
+LAST = len(PIECES) - 2
 BANKS = {
-    "za": [3, 7, 3, 5, 3, 5, 3, 5],
-    "ms": [0, 1, 2, 1, 2, 1, 2, 1],
-    "ow": [4, 0, 4, 0, 4, 0, 4, 0],
-    "total": [7, 6, 7, 6, 7, 6, 7, 6],
+    "za": [3, 7, 0, 7, 0, 7, 0, 7],
+    "ms": [0, 1, 1, 5, 1, 5, 1, 5],
+    "ow": [4, 3, 4, 3, 4, 3, 4, 3],
+    "total": [7, 0, 7, 0, 7, 0, 7, 0],
 }
 
 
@@ -56,7 +56,7 @@ def tile_list_rgg_ownrelu_kernel(
         identity = keep.tile([P, P], F32, name="identity")
 
         nc.gpsimd.memset(table_plane[:], 0)
-        zeros = held.tile([P, 26 * KIB // 4], F32, name="zeros", offset=0, align_bytes=64)
+        zeros = held.tile([P, 34 * KIB // 4], F32, name="zeros", offset=0, align_bytes=64)
         nc.gpsimd.memset(zeros[:, 0:P], 0.0)
         nc.gpsimd.affine_select(
             out=identity[:], in_=zeros[:, 0:P], compare_op=ALU.not_equal, fill=1.0, base=0,
@@ -87,8 +87,9 @@ def tile_list_rgg_ownrelu_kernel(
         rows_out = [keep.tile([P, T], F32, name="rows_out0")]
         nc.vector.memset(rows_out[0][:, 0 : T - 1], 0.0)
         nc.vector.memset(rows_out[0][:, T - 1 : T], 0.0)
-        rows_out.append(held_tile("rows_out1", [P, T], F32, 25.5))
-        nc.gpsimd.memset(rows_out[1][:], 0.0)
+        for n in range(1, OUT_TILES):
+            rows_out.append(held_tile("rows_out%d" % n, [P, T], F32, 17.5 + 8 * n))
+            nc.gpsimd.memset(rows_out[n][:], 0.0)
 
         def load_words(codes, words):
             nc.sync.dma_start(codes[:], words[0].rearrange("p c i -> p (c i)").bitcast(I32))
@@ -105,8 +106,9 @@ def tile_list_rgg_ownrelu_kernel(
         load_rows(WC_ROW, wc_scales, range(1, 2), w_planes)
         load_words(wb_codes, wb_words)
         nc.sync.dma_start(wc_codes[:].bitcast(I32), wc_words[0].bitcast(I32))
-        load_rows(WC_ROW, wc_scales, range(2, 4), w_planes)
+        load_rows(WC_ROW, wc_scales, range(2, 3), w_planes)
         load_rows(WB_ROW, wb_scales, range(4), w_planes)
+        load_rows(WC_ROW, wc_scales, range(3, 4), w_planes)
         nc.sync.dma_start(wo_raw[1][:], wo_rows[:, :, N // 2 : N])
         for h in range(2):
             nc.sync.dma_start(edge_w[:, h * HALF : (h + 1) * HALF], wgo[:, h * HALF : (h + 1) * HALF])
@@ -166,7 +168,7 @@ def tile_list_rgg_ownrelu_kernel(
                 ("src", wb_codes[:, cols].bitcast(FP8X4), planes[WB_ROW:, cols]),
             ])
             if u == 0:
-                eta = picks.tile([P, 3 * HALF // 2], F32, name="eta0", offset=5 * KIB, align_bytes=64)[:, 0:HALF]
+                eta = picks.tile([P, HALF], F32, name="eta0", offset=4 * KIB, align_bytes=64)[:]
             else:
                 eta = work.tile([P, j1 - j0], F32, name="eta")[:]
             nc.scalar.activation(eta, za[:], ACT.Sigmoid)
@@ -190,36 +192,30 @@ def tile_list_rgg_ownrelu_kernel(
 
         def gate(u, message, eta):
             nt, j0, j1 = PIECES[u]
-            gated = chained("gated%d" % u, [P, j1 - j0], F32, u)
+            gated = chained("gated%d" % u, [P, j1 - j0], F32, u if u != 1 else 10)
             engine = nc.vector if u < VECTOR_GATES else nc.gpsimd
             engine.tensor_tensor(gated[:], message[:], eta, ALU.mult)
             return gated
 
-        def add_and_relu(u, own, gated):
+        def add(u, own, gated):
             nt, j0, j1 = PIECES[u]
             total = bank("total", u)
-            for n, summand in enumerate((own, gated)):
+            for n, summand in enumerate((gated, own)):
                 for c in range(0, j1 - j0, P):
                     nc.tensor.matmul(
                         total[:, c : c + P], summand[:, c : c + P], identity[:], is_transpose=True,
                         start=(n, c) == (0, 0), stop=(n, c) == (1, j1 - j0 - P),
                     )
-            relu = chained("relu%d" % u, [P, j1 - j0], F32, u + 8 if u in FUSED else u + 2)[:]
-            nc.scalar.activation(relu, total[:], ACT.Relu)
-            return relu
+            return total
 
-        def scatter(u, relu):
-            nt, j0, j1 = PIECES[u]
+        def place_rows(u, j0, j1, values, weights):
+            nt = PIECES[u][0]
             rows = rows_out[nt % OUT_TILES]
-            weights = edge_w[:, j0:j1]
             window = rows[:].indirect(entries(dst_list, j0, j1))
-            if u in FUSED:
-                nc.vector.tensor_tensor(window, relu, weights, ALU.mult)
+            if weights is None:
+                nc.vector.tensor_copy(window, values)
             else:
-                weighted = work.tile([P, j1 - j0], F32, name="weighted")
-                engine = nc.vector if u - 1 in FUSED else nc.gpsimd
-                engine.tensor_tensor(weighted[:], relu, weights, ALU.mult)
-                nc.vector.tensor_copy(window, weighted[:])
+                nc.vector.tensor_tensor(window, values, weights, ALU.mult)
             if j1 == J:
                 nc.sync.dma_start(out[nt * P : (nt + 1) * P, :], rows[:])
 
@@ -234,22 +230,28 @@ def tile_list_rgg_ownrelu_kernel(
 
         own = own_product(0)
         gated = [gate(0, *gate_products(0))]
-        gather_words(picks.tile([P, HALF], U32, name="src_words1", offset=5 * KIB, align_bytes=64), "src", HALF, J)
+        gather_words(picks.tile([P, HALF], U32, name="src_words1", offset=4 * KIB, align_bytes=64), "src", HALF, J)
         gated.append(gate(1, *gate_products(1)))
-        grouped = picks.tile([P, P, PACK], BF16, name="grouped2", offset=7 * KIB, align_bytes=64)
-        quantize_wo(2 * P, 3 * P, grouped[:])
-        rows_out.append(picks.tile([P, T], F32, name="rows_out2", offset=7 * KIB, align_bytes=64))
-        nc.gpsimd.memset(rows_out[2][:], 0.0)
-        gated.append(gate(2, *gate_products(2)))
+        quantize_wo(N // 2, N, chained("grouped1", [P, N, PACK], BF16, 1)[:, 0 : N // 2, :])
+        last_relu = chained("last_relu", [P, J], F32, 8)
         for u in range(len(PIECES)):
-            relu = add_and_relu(u, own, gated[u])
+            nt, j0, j1 = PIECES[u]
+            total = add(u, own, gated[u])
             if u == 0:
-                quantize_wo(3 * P, N, chained("grouped3", [P, P, PACK], BF16, 0)[:])
+                weighted = chained("weighted0", [P, HALF], F32, 1)
+                nc.vector.scalar_tensor_tensor(weighted[:], total[:], 0.0, edge_w[:, j0:j1], ALU.max, ALU.mult)
+            else:
+                relu = last_relu[:, j0:j1] if u >= LAST else chained("relu%d" % u, [P, HALF], F32, u + 2)[:]
+                nc.scalar.activation(relu, total[:], ACT.Relu)
             if u + 1 < len(PIECES):
                 own = own_product(u + 1)
-            ahead = u + 2 in range(VECTOR_GATES, len(PIECES))
-            if ahead:
+            if u + 2 < len(PIECES):
                 products = gate_products(u + 2)
-            scatter(u, relu)
-            if ahead:
+            if 0 < u < LAST:
+                weighted = work.tile([P, HALF], F32, name="weighted")
+                nc.gpsimd.tensor_tensor(weighted[:], relu, edge_w[:, j0:j1], ALU.mult)
+            if u < LAST:
+                place_rows(u, j0, j1, weighted[:], None)
+            if u + 2 < len(PIECES):
                 gated.append(gate(u + 2, *products))
+        place_rows(LAST + 1, 0, J, last_relu[:], edge_w[:])

@@ -25,14 +25,14 @@ PIECES = [
     (0, 0, HALF), (1, 0, HALF), (2, 0, HALF), (0, HALF, J), (1, HALF, J), (2, HALF, J), (3, 0, HALF), (3, HALF, J),
 ]
 OUT_TILES = 3
-WC_ROW, WA_ROW, WB_ROW = 0, 4, 8
+WC_ROW, WB_ROW = 0, 4
 VECTOR_GATES = 2
 LAST = len(PIECES) - 2
 BANKS = {
-    "za": [3, 7, 0, 7, 0, 7, 0, 7],
-    "ms": [0, 1, 1, 5, 1, 5, 1, 5],
-    "ow": [4, 3, 4, 3, 4, 3, 4, 3],
-    "total": [7, 0, 7, 0, 7, 0, 7, 0],
+    "za": [3, 7, 2, 7, 2, 7, 2, 7],
+    "ms": [0, 1, 5, 3, 4, 3, 4, 3],
+    "ow": [3, 3, 4, 3, 4, 3, 4, 3],
+    "total": [7, 2, 7, 2, 7, 2, 7, 2],
 }
 
 
@@ -56,7 +56,7 @@ def tile_list_rgg_ownrelu_kernel(
         identity = keep.tile([P, P], F32, name="identity")
 
         nc.gpsimd.memset(table_plane[:], 0)
-        zeros = held.tile([P, 34 * KIB // 4], F32, name="zeros", offset=0, align_bytes=64)
+        zeros = held.tile([P, 35 * KIB // 4], F32, name="zeros", offset=0, align_bytes=64)
         nc.gpsimd.memset(zeros[:, 0:P], 0.0)
         nc.gpsimd.affine_select(
             out=identity[:], in_=zeros[:, 0:P], compare_op=ALU.not_equal, fill=1.0, base=0,
@@ -72,8 +72,9 @@ def tile_list_rgg_ownrelu_kernel(
         wc_codes = held_tile("wc_codes", [P, 2 * N], U8, 12)
         wo_raw = [held_tile("wo_raw%d" % h, [P, PACK, N // 2], F32, 13 + 4 * h) for h in range(2)]
         edge_w = held_tile("edge_w", [P, J], F32, 21)
-        w_planes = held_tile("w_planes", [P, N // PACK], I32, 25)
+        w_planes = held_tile("w_planes", [P, 2 * N // PACK], I32, 25)
         nc.gpsimd.memset(w_planes[:], 0)
+        wa_plane, src_planes = w_planes[:, 0 : N // PACK], w_planes[:, N // PACK :]
 
         def load_rows(first_row, scales, quadrants, plane):
             rows = scales[0].bitcast(I32)
@@ -88,7 +89,7 @@ def tile_list_rgg_ownrelu_kernel(
         nc.vector.memset(rows_out[0][:, 0 : T - 1], 0.0)
         nc.vector.memset(rows_out[0][:, T - 1 : T], 0.0)
         for n in range(1, OUT_TILES):
-            rows_out.append(held_tile("rows_out%d" % n, [P, T], F32, 17.5 + 8 * n))
+            rows_out.append(held_tile("rows_out%d" % n, [P, T], F32, 18 + 8 * n))
             nc.gpsimd.memset(rows_out[n][:], 0.0)
 
         def load_words(codes, words):
@@ -97,18 +98,16 @@ def tile_list_rgg_ownrelu_kernel(
         wo_rows = wo.rearrange("(p i) n -> p i n", i=PACK)
         nc.sync.dma_start(dst_list[:], offs2)
         load_rows(0, tab_scales, range(4), table_plane)
-        nc.sync.dma_start(src_list[:], offs)
         load_words(wa_codes, wa_words)
         load_words(table_words, tab_words)
-        load_rows(WA_ROW, wa_scales, range(4), w_planes)
-        load_rows(WC_ROW, wc_scales, range(1), w_planes)
+        nc.sync.dma_start(src_list[:], offs)
+        load_rows(0, wa_scales, range(4), wa_plane)
+        load_rows(WC_ROW, wc_scales, range(1), src_planes)
         nc.sync.dma_start(wo_raw[0][:], wo_rows[:, :, 0 : N // 2])
-        load_rows(WC_ROW, wc_scales, range(1, 2), w_planes)
         load_words(wb_codes, wb_words)
+        load_rows(WC_ROW, wc_scales, range(1, 4), src_planes)
+        load_rows(WB_ROW, wb_scales, range(4), src_planes)
         nc.sync.dma_start(wc_codes[:].bitcast(I32), wc_words[0].bitcast(I32))
-        load_rows(WC_ROW, wc_scales, range(2, 3), w_planes)
-        load_rows(WB_ROW, wb_scales, range(4), w_planes)
-        load_rows(WC_ROW, wc_scales, range(3, 4), w_planes)
         nc.sync.dma_start(wo_raw[1][:], wo_rows[:, :, N // 2 : N])
         for h in range(2):
             nc.sync.dma_start(edge_w[:, h * HALF : (h + 1) * HALF], wgo[:, h * HALF : (h + 1) * HALF])
@@ -150,21 +149,21 @@ def tile_list_rgg_ownrelu_kernel(
 
         def product(acc, u, passes):
             nt, j0, j1 = PIECES[u]
-            for j in range(j0, j1, P):
-                for n, (side, codes, plane) in enumerate(passes):
+            for n, (side, codes, plane) in enumerate(passes):
+                for j in range(j0, j1, P):
                     nc.tensor.matmul_mx(
                         out=acc[:, j - j0 : j - j0 + P], lhsT=words_of[side][j].bitcast(FP8X4),
                         lhsT_scale=scales_of[side][j], rhs=codes, rhs_scale=plane,
-                        start=n == 0, stop=n == len(passes) - 1,
+                        start=(n, j) == (0, j0), stop=(n, j) == (len(passes) - 1, j1 - P),
                     )
 
         def gate_products(u):
             nt, j0, j1 = PIECES[u]
             cols = slice(nt * P, (nt + 1) * P)
-            planes = w_planes[:].bitcast(U8)
+            planes = src_planes.bitcast(U8)
             za = bank("za", u)
             product(za, u, [
-                ("dst", wa_codes[:, cols].bitcast(FP8X4), planes[WA_ROW:, cols]),
+                ("dst", wa_codes[:, cols].bitcast(FP8X4), wa_plane.bitcast(U8)[:, cols]),
                 ("src", wb_codes[:, cols].bitcast(FP8X4), planes[WB_ROW:, cols]),
             ])
             if u == 0:
@@ -220,16 +219,15 @@ def tile_list_rgg_ownrelu_kernel(
                 nc.sync.dma_start(out[nt * P : (nt + 1) * P, :], rows[:])
 
         gather_scales(keep.tile([P, J], U8, name="dst_plane", align_bytes=64), "dst", 0, J)
+        gather_words(keep.tile([P, HALF], U32, name="dst_words0", align_bytes=64), "dst", 0, HALF)
         gather_scales(keep.tile([P, HALF], U8, name="src_plane0", align_bytes=64), "src", 0, HALF)
-        for side in ("dst", "src"):
-            gather_words(keep.tile([P, HALF], U32, name=side + "_words0", align_bytes=64), side, 0, HALF)
-        grouped = picks.tile([P, N // 2, PACK], BF16, name="grouped0", offset=KIB, align_bytes=64)
-        quantize_wo(0, N // 2, grouped[:])
-        gather_words(picks.tile([P, HALF], U32, name="dst_words1", offset=0, align_bytes=64), "dst", HALF, J)
-        gather_scales(picks.tile([P, HALF], U8, name="src_plane1", offset=2 * KIB, align_bytes=64), "src", HALF, J)
+        gather_words(keep.tile([P, HALF], U32, name="src_words0", align_bytes=64), "src", 0, HALF)
+        quantize_wo(0, N // 2, keep.tile([P, N // 2, PACK], BF16, name="grouped0", align_bytes=64)[:])
+        gather_words(held_tile("dst_words1", [P, HALF], U32, 13), "dst", HALF, J)
+        gather_scales(held_tile("src_plane1", [P, HALF], U8, 15), "src", HALF, J)
 
-        own = own_product(0)
         gated = [gate(0, *gate_products(0))]
+        own = own_product(0)
         gather_words(picks.tile([P, HALF], U32, name="src_words1", offset=4 * KIB, align_bytes=64), "src", HALF, J)
         gated.append(gate(1, *gate_products(1)))
         quantize_wo(N // 2, N, chained("grouped1", [P, N, PACK], BF16, 1)[:, 0 : N // 2, :])

@@ -25,13 +25,12 @@ PIECES = [
     (0, 0, HALF), (1, 0, HALF), (2, 0, HALF), (0, HALF, J), (1, HALF, J), (2, HALF, J), (3, 0, HALF), (3, HALF, J),
 ]
 OUT_TILES = 3
-WC_ROW, WB_ROW = 0, 4
-VECTOR_GATES = 2
+VECTOR_GATES = 1
 LAST = len(PIECES) - 2
 BANKS = {
     "za": [3, 7, 2, 7, 2, 7, 2, 7],
-    "ms": [0, 1, 5, 3, 4, 3, 4, 3],
-    "ow": [3, 3, 4, 3, 4, 3, 4, 3],
+    "ms": [0, 1, 5, 0, 3, 0, 3, 0],
+    "ow": [3, 0, 3, 0, 3, 0, 3, 0],
     "total": [7, 2, 7, 2, 7, 2, 7, 2],
 }
 
@@ -70,16 +69,16 @@ def tile_list_rgg_ownrelu_kernel(
         wa_codes = held_tile("wa_codes", [P, N], I32, 8)
         wb_codes = held_tile("wb_codes", [P, N], I32, 10)
         wc_codes = held_tile("wc_codes", [P, 2 * N], U8, 12)
-        wo_raw = [held_tile("wo_raw%d" % h, [P, PACK, N // 2], F32, 13 + 4 * h) for h in range(2)]
+        wo_raw = held_tile("wo_raw", [P, PACK, N], F32, 13)
         edge_w = held_tile("edge_w", [P, J], F32, 21)
-        w_planes = held_tile("w_planes", [P, 2 * N // PACK], I32, 25)
+        w_planes = held_tile("w_planes", [P, 3 * N // PACK], I32, 25)
         nc.gpsimd.memset(w_planes[:], 0)
-        wa_plane, src_planes = w_planes[:, 0 : N // PACK], w_planes[:, N // PACK :]
+        wa_plane, wb_plane, wc_plane = (w_planes[:, n * N // PACK : (n + 1) * N // PACK] for n in range(3))
 
-        def load_rows(first_row, scales, quadrants, plane):
+        def load_rows(scales, quadrants, plane):
             rows = scales[0].bitcast(I32)
             for q in quadrants:
-                nc.sync.dma_start(plane[32 * q + first_row : 32 * q + first_row + 4, :], rows[4 * q : 4 * (q + 1), :])
+                nc.sync.dma_start(plane[32 * q : 32 * q + 4, :], rows[4 * q : 4 * (q + 1), :])
 
         warm = keep.tile([P, 2], F32, name="warm")
         nc.gpsimd.memset(warm[:, 0:1], 0.0)
@@ -89,7 +88,7 @@ def tile_list_rgg_ownrelu_kernel(
         nc.vector.memset(rows_out[0][:, 0 : T - 1], 0.0)
         nc.vector.memset(rows_out[0][:, T - 1 : T], 0.0)
         for n in range(1, OUT_TILES):
-            rows_out.append(held_tile("rows_out%d" % n, [P, T], F32, 18 + 8 * n))
+            rows_out.append(held_tile("rows_out%d" % n, [P, T], F32, 18.5 + 8 * n))
             nc.gpsimd.memset(rows_out[n][:], 0.0)
 
         def load_words(codes, words):
@@ -97,18 +96,18 @@ def tile_list_rgg_ownrelu_kernel(
 
         wo_rows = wo.rearrange("(p i) n -> p i n", i=PACK)
         nc.sync.dma_start(dst_list[:], offs2)
-        load_rows(0, tab_scales, range(4), table_plane)
+        nc.sync.dma_start(src_list[:], offs)
+        load_rows(tab_scales, range(4), table_plane)
         load_words(wa_codes, wa_words)
         load_words(table_words, tab_words)
-        nc.sync.dma_start(src_list[:], offs)
-        load_rows(0, wa_scales, range(4), wa_plane)
-        load_rows(WC_ROW, wc_scales, range(1), src_planes)
-        nc.sync.dma_start(wo_raw[0][:], wo_rows[:, :, 0 : N // 2])
-        load_words(wb_codes, wb_words)
-        load_rows(WC_ROW, wc_scales, range(1, 4), src_planes)
-        load_rows(WB_ROW, wb_scales, range(4), src_planes)
         nc.sync.dma_start(wc_codes[:].bitcast(I32), wc_words[0].bitcast(I32))
-        nc.sync.dma_start(wo_raw[1][:], wo_rows[:, :, N // 2 : N])
+        load_rows(wa_scales, range(4), wa_plane)
+        load_rows(wc_scales, range(1), wc_plane)
+        nc.sync.dma_start(wo_raw[:], wo_rows)
+        load_words(wb_codes, wb_words)
+        load_rows(wc_scales, range(1, 3), wc_plane)
+        load_rows(wb_scales, range(4), wb_plane)
+        load_rows(wc_scales, range(3, 4), wc_plane)
         for h in range(2):
             nc.sync.dma_start(edge_w[:, h * HALF : (h + 1) * HALF], wgo[:, h * HALF : (h + 1) * HALF])
 
@@ -131,8 +130,10 @@ def tile_list_rgg_ownrelu_kernel(
             gather(words_of, table_words[:].bitcast(U32), picked, side, j0, j1)
 
         def quantize_wo(n0, n1, grouped):
-            raw = wo_raw[n0 // (N // 2)][:, :, n0 % (N // 2) : n0 % (N // 2) + n1 - n0]
-            nc.scalar.copy(grouped, raw.rearrange("p i n -> p n i"))
+            raw = wo_raw[:, :, n0:n1]
+            nc.scalar.copy(
+                grouped.rearrange("p (c m) i -> p c i m", m=4), raw.rearrange("p i (c m) -> p c i m", m=4)
+            )
             nc.vector.quantize_mx(
                 out=wo_codes[:, n0:n1].bitcast(FP8X4),
                 scales=wo_plane[:, n0:n1],
@@ -160,11 +161,10 @@ def tile_list_rgg_ownrelu_kernel(
         def gate_products(u):
             nt, j0, j1 = PIECES[u]
             cols = slice(nt * P, (nt + 1) * P)
-            planes = src_planes.bitcast(U8)
             za = bank("za", u)
             product(za, u, [
                 ("dst", wa_codes[:, cols].bitcast(FP8X4), wa_plane.bitcast(U8)[:, cols]),
-                ("src", wb_codes[:, cols].bitcast(FP8X4), planes[WB_ROW:, cols]),
+                ("src", wb_codes[:, cols].bitcast(FP8X4), wb_plane.bitcast(U8)[:, cols]),
             ])
             if u == 0:
                 eta = picks.tile([P, HALF], F32, name="eta0", offset=4 * KIB, align_bytes=64)[:]
@@ -173,7 +173,7 @@ def tile_list_rgg_ownrelu_kernel(
             nc.scalar.activation(eta, za[:], ACT.Sigmoid)
             ms = bank("ms", u)
             wc_cols = wc_codes[:, 2 * nt * P : 2 * (nt + 1) * P].bitcast(FP4X4)
-            product(ms, u, [("src", wc_cols, planes[WC_ROW:, cols])])
+            product(ms, u, [("src", wc_cols, wc_plane.bitcast(U8)[:, cols])])
             if u < VECTOR_GATES:
                 return ms, eta
             message = work.tile([P, j1 - j0], F32, name="message")
@@ -191,7 +191,7 @@ def tile_list_rgg_ownrelu_kernel(
 
         def gate(u, message, eta):
             nt, j0, j1 = PIECES[u]
-            gated = chained("gated%d" % u, [P, j1 - j0], F32, u if u != 1 else 10)
+            gated = chained("gated%d" % u, [P, j1 - j0], F32, u)
             engine = nc.vector if u < VECTOR_GATES else nc.gpsimd
             engine.tensor_tensor(gated[:], message[:], eta, ALU.mult)
             return gated
@@ -222,28 +222,30 @@ def tile_list_rgg_ownrelu_kernel(
         gather_words(keep.tile([P, HALF], U32, name="dst_words0", align_bytes=64), "dst", 0, HALF)
         gather_scales(keep.tile([P, HALF], U8, name="src_plane0", align_bytes=64), "src", 0, HALF)
         gather_words(keep.tile([P, HALF], U32, name="src_words0", align_bytes=64), "src", 0, HALF)
-        quantize_wo(0, N // 2, keep.tile([P, N // 2, PACK], BF16, name="grouped0", align_bytes=64)[:])
-        gather_words(held_tile("dst_words1", [P, HALF], U32, 13), "dst", HALF, J)
-        gather_scales(held_tile("src_plane1", [P, HALF], U8, 15), "src", HALF, J)
+        gather_words(keep.tile([P, HALF], U32, name="dst_words1", align_bytes=64), "dst", HALF, J)
+        gather_words(keep.tile([P, HALF], U32, name="src_words1", align_bytes=64), "src", HALF, J)
+        for h in range(2):
+            grouped = chained("grouped%d" % h, [P, N // 2, PACK], BF16, h)
+            quantize_wo(h * N // 2, (h + 1) * N // 2, grouped[:])
 
         gated = [gate(0, *gate_products(0))]
         own = own_product(0)
-        gather_words(picks.tile([P, HALF], U32, name="src_words1", offset=4 * KIB, align_bytes=64), "src", HALF, J)
+        gather_scales(picks.tile([P, HALF], U8, name="src_plane1", offset=4 * KIB, align_bytes=64), "src", HALF, J)
         gated.append(gate(1, *gate_products(1)))
-        quantize_wo(N // 2, N, chained("grouped1", [P, N, PACK], BF16, 1)[:, 0 : N // 2, :])
+        products = gate_products(2)
         last_relu = chained("last_relu", [P, J], F32, 8)
         for u in range(len(PIECES)):
             nt, j0, j1 = PIECES[u]
             total = add(u, own, gated[u])
             if u == 0:
-                weighted = chained("weighted0", [P, HALF], F32, 1)
+                weighted = work.tile([P, HALF], F32, name="weighted")
                 nc.vector.scalar_tensor_tensor(weighted[:], total[:], 0.0, edge_w[:, j0:j1], ALU.max, ALU.mult)
             else:
                 relu = last_relu[:, j0:j1] if u >= LAST else chained("relu%d" % u, [P, HALF], F32, u + 2)[:]
                 nc.scalar.activation(relu, total[:], ACT.Relu)
             if u + 1 < len(PIECES):
                 own = own_product(u + 1)
-            if u + 2 < len(PIECES):
+            if 0 < u < LAST:
                 products = gate_products(u + 2)
             if 0 < u < LAST:
                 weighted = work.tile([P, HALF], F32, name="weighted")

@@ -19,20 +19,18 @@ ALU = mybir.AluOpType
 P = 128
 PACK = 4
 LANES = 16
+LINE = 4
 KIB = 1024
 HALF = J // 2
-PIECES = [
-    (0, 0, HALF), (1, 0, HALF), (2, 0, HALF), (0, HALF, J), (1, HALF, J), (2, HALF, J), (3, 0, HALF), (3, HALF, J),
-]
-OUT_TILES = 3
-VECTOR_GATES = 1
+PLACE = 2 * KIB
+PIECES = [(0, 0), (1, 0), (2, 0), (0, HALF), (1, HALF), (2, HALF), (3, 0), (3, HALF)]
 LAST = len(PIECES) - 2
-BANKS = {
-    "za": [3, 7, 2, 7, 2, 7, 2, 7],
-    "ms": [0, 1, 5, 0, 3, 0, 3, 0],
-    "ow": [3, 0, 3, 0, 3, 0, 3, 0],
-    "total": [7, 2, 7, 2, 7, 2, 7, 2],
-}
+OUT_TILES = 3
+SUM_BANKS = (7, 2)
+PRODUCT_BANKS = (3, 0)
+FIRST_ZA_BANK = PRODUCT_BANKS[0]
+FIRST_MS_BANKS = (PRODUCT_BANKS[1], 1, 5)
+LAST_GATHER_AT = 4 * KIB
 
 
 def tile_list_rgg_ownrelu_kernel(
@@ -56,7 +54,8 @@ def tile_list_rgg_ownrelu_kernel(
 
         nc.gpsimd.memset(table_plane[:], 0)
         zeros = held.tile([P, 35 * KIB // 4], F32, name="zeros", offset=0, align_bytes=64)
-        nc.gpsimd.memset(zeros[:, 0:P], 0.0)
+        nc.vector.memset(zeros[:, 0 : P - 1], 0.0)
+        nc.vector.memset(zeros[:, P - 1 : P], 0.0)
         nc.gpsimd.affine_select(
             out=identity[:], in_=zeros[:, 0:P], compare_op=ALU.not_equal, fill=1.0, base=0,
             pattern=[[-1, P]], channel_multiplier=1,
@@ -88,13 +87,12 @@ def tile_list_rgg_ownrelu_kernel(
         nc.vector.memset(rows_out[0][:, 0 : T - 1], 0.0)
         nc.vector.memset(rows_out[0][:, T - 1 : T], 0.0)
         for n in range(1, OUT_TILES):
-            rows_out.append(held_tile("rows_out%d" % n, [P, T], F32, 18.5 + 8 * n))
+            rows_out.append(held_tile("rows_out%d" % n, [P, T], F32, 26.5 + 8 * (n - 1)))
             nc.gpsimd.memset(rows_out[n][:], 0.0)
 
         def load_words(codes, words):
             nc.sync.dma_start(codes[:], words[0].rearrange("p c i -> p (c i)").bitcast(I32))
 
-        wo_rows = wo.rearrange("(p i) n -> p i n", i=PACK)
         nc.sync.dma_start(dst_list[:], offs2)
         nc.sync.dma_start(src_list[:], offs)
         load_rows(tab_scales, range(4), table_plane)
@@ -103,7 +101,7 @@ def tile_list_rgg_ownrelu_kernel(
         nc.sync.dma_start(wc_codes[:].bitcast(I32), wc_words[0].bitcast(I32))
         load_rows(wa_scales, range(4), wa_plane)
         load_rows(wc_scales, range(1), wc_plane)
-        nc.sync.dma_start(wo_raw[:], wo_rows)
+        nc.sync.dma_start(wo_raw[:], wo.rearrange("(p i) n -> p i n", i=PACK))
         load_words(wb_codes, wb_words)
         load_rows(wc_scales, range(1, 3), wc_plane)
         load_rows(wb_scales, range(4), wb_plane)
@@ -129,94 +127,87 @@ def tile_list_rgg_ownrelu_kernel(
         def gather_words(picked, side, j0, j1):
             gather(words_of, table_words[:].bitcast(U32), picked, side, j0, j1)
 
-        def quantize_wo(n0, n1, grouped):
-            raw = wo_raw[:, :, n0:n1]
+        def chained(name, shape, dtype, place):
+            return chain.tile(shape, dtype, name=name, offset=place * PLACE, align_bytes=64)
+
+        def quantize_wo(h):
+            cols = slice(h * N // 2, (h + 1) * N // 2)
+            grouped = chained("grouped%d" % h, [P, N // 2, PACK], BF16, h)[:]
             nc.scalar.copy(
-                grouped.rearrange("p (c m) i -> p c i m", m=4), raw.rearrange("p i (c m) -> p c i m", m=4)
+                grouped.rearrange("p (c m) i -> p c i m", m=LINE),
+                wo_raw[:, :, cols].rearrange("p i (c m) -> p c i m", m=LINE),
             )
             nc.vector.quantize_mx(
-                out=wo_codes[:, n0:n1].bitcast(FP8X4),
-                scales=wo_plane[:, n0:n1],
+                out=wo_codes[:, cols].bitcast(FP8X4),
+                scales=wo_plane[:, cols],
                 in_=grouped.rearrange("p n i -> p (n i)"),
             )
 
-        def bank(role, u):
-            width = PIECES[u][2] - PIECES[u][1]
-            place = BANKS[role][u]
-            return psum.tile([P, width], F32, name="%s%d" % (role, u), offset=place * 2 * KIB)
-
-        def chained(name, shape, dtype, place):
-            return chain.tile(shape, dtype, name=name, offset=place * 2 * KIB, align_bytes=64)
+        def bank(name, u, number):
+            return psum.tile([P, HALF], F32, name="%s%d" % (name, u), offset=number * PLACE)
 
         def product(acc, u, passes):
-            nt, j0, j1 = PIECES[u]
+            j0 = PIECES[u][1]
             for n, (side, codes, plane) in enumerate(passes):
-                for j in range(j0, j1, P):
+                for c in range(0, HALF, P):
                     nc.tensor.matmul_mx(
-                        out=acc[:, j - j0 : j - j0 + P], lhsT=words_of[side][j].bitcast(FP8X4),
-                        lhsT_scale=scales_of[side][j], rhs=codes, rhs_scale=plane,
-                        start=(n, j) == (0, j0), stop=(n, j) == (len(passes) - 1, j1 - P),
+                        out=acc[:, c : c + P], lhsT=words_of[side][j0 + c].bitcast(FP8X4),
+                        lhsT_scale=scales_of[side][j0 + c], rhs=codes, rhs_scale=plane,
+                        start=(n, c) == (0, 0), stop=(n, c) == (len(passes) - 1, HALF - P),
                     )
 
         def gate_products(u):
-            nt, j0, j1 = PIECES[u]
+            nt = PIECES[u][0]
             cols = slice(nt * P, (nt + 1) * P)
-            za = bank("za", u)
+            za = bank("za", u, SUM_BANKS[(u - 1) % 2] if u > 0 else FIRST_ZA_BANK)
             product(za, u, [
                 ("dst", wa_codes[:, cols].bitcast(FP8X4), wa_plane.bitcast(U8)[:, cols]),
                 ("src", wb_codes[:, cols].bitcast(FP8X4), wb_plane.bitcast(U8)[:, cols]),
             ])
             if u == 0:
-                eta = picks.tile([P, HALF], F32, name="eta0", offset=4 * KIB, align_bytes=64)[:]
+                eta = picks.tile([P, HALF], F32, name="eta0", offset=LAST_GATHER_AT, align_bytes=64)
             else:
-                eta = work.tile([P, j1 - j0], F32, name="eta")[:]
-            nc.scalar.activation(eta, za[:], ACT.Sigmoid)
-            ms = bank("ms", u)
+                eta = work.tile([P, HALF], F32, name="eta")
+            nc.scalar.activation(eta[:], za[:], ACT.Sigmoid)
+            ms = bank("ms", u, FIRST_MS_BANKS[u] if u < len(FIRST_MS_BANKS) else PRODUCT_BANKS[u % 2])
             wc_cols = wc_codes[:, 2 * nt * P : 2 * (nt + 1) * P].bitcast(FP4X4)
             product(ms, u, [("src", wc_cols, wc_plane.bitcast(U8)[:, cols])])
-            if u < VECTOR_GATES:
+            if u == 0:
                 return ms, eta
-            message = work.tile([P, j1 - j0], F32, name="message")
+            message = work.tile([P, HALF], F32, name="message")
             nc.scalar.copy(message[:], ms[:])
             return message, eta
 
         def own_product(u):
-            nt, j0, j1 = PIECES[u]
+            nt = PIECES[u][0]
             cols = slice(nt * P, (nt + 1) * P)
-            ow = bank("ow", u)
+            ow = bank("ow", u, PRODUCT_BANKS[u % 2])
             product(ow, u, [("dst", wo_codes[:, cols].bitcast(FP8X4), wo_plane[:, cols])])
-            own = work.tile([P, j1 - j0], F32, name="own")
+            own = work.tile([P, HALF], F32, name="own")
             nc.scalar.copy(own[:], ow[:])
             return own
 
         def gate(u, message, eta):
-            nt, j0, j1 = PIECES[u]
-            gated = chained("gated%d" % u, [P, j1 - j0], F32, u)
-            engine = nc.vector if u < VECTOR_GATES else nc.gpsimd
-            engine.tensor_tensor(gated[:], message[:], eta, ALU.mult)
+            gated = chained("gated%d" % u, [P, HALF], F32, u)
+            engine = nc.vector if u == 0 else nc.gpsimd
+            engine.tensor_tensor(gated[:], message[:], eta[:], ALU.mult)
             return gated
 
         def add(u, own, gated):
-            nt, j0, j1 = PIECES[u]
-            total = bank("total", u)
+            total = bank("total", u, SUM_BANKS[u % 2])
             for n, summand in enumerate((gated, own)):
-                for c in range(0, j1 - j0, P):
+                for c in range(0, HALF, P):
                     nc.tensor.matmul(
                         total[:, c : c + P], summand[:, c : c + P], identity[:], is_transpose=True,
-                        start=(n, c) == (0, 0), stop=(n, c) == (1, j1 - j0 - P),
+                        start=(n, c) == (0, 0), stop=(n, c) == (1, HALF - P),
                     )
             return total
 
-        def place_rows(u, j0, j1, values, weights):
-            nt = PIECES[u][0]
-            rows = rows_out[nt % OUT_TILES]
-            window = rows[:].indirect(entries(dst_list, j0, j1))
-            if weights is None:
-                nc.vector.tensor_copy(window, values)
-            else:
-                nc.vector.tensor_tensor(window, values, weights, ALU.mult)
-            if j1 == J:
-                nc.sync.dma_start(out[nt * P : (nt + 1) * P, :], rows[:])
+        def window(nt, j0, j1):
+            return rows_out[nt % OUT_TILES][:].indirect(entries(dst_list, j0, j1))
+
+        def store(nt):
+            nc.sync.dma_start(out[nt * P : (nt + 1) * P, :], rows_out[nt % OUT_TILES][:])
 
         gather_scales(keep.tile([P, J], U8, name="dst_plane", align_bytes=64), "dst", 0, J)
         gather_words(keep.tile([P, HALF], U32, name="dst_words0", align_bytes=64), "dst", 0, HALF)
@@ -225,33 +216,36 @@ def tile_list_rgg_ownrelu_kernel(
         gather_words(keep.tile([P, HALF], U32, name="dst_words1", align_bytes=64), "dst", HALF, J)
         gather_words(keep.tile([P, HALF], U32, name="src_words1", align_bytes=64), "src", HALF, J)
         for h in range(2):
-            grouped = chained("grouped%d" % h, [P, N // 2, PACK], BF16, h)
-            quantize_wo(h * N // 2, (h + 1) * N // 2, grouped[:])
+            quantize_wo(h)
 
         gated = [gate(0, *gate_products(0))]
         own = own_product(0)
-        gather_scales(picks.tile([P, HALF], U8, name="src_plane1", offset=4 * KIB, align_bytes=64), "src", HALF, J)
+        src_plane1 = picks.tile([P, HALF], U8, name="src_plane1", offset=LAST_GATHER_AT, align_bytes=64)
+        gather_scales(src_plane1, "src", HALF, J)
         gated.append(gate(1, *gate_products(1)))
         products = gate_products(2)
-        last_relu = chained("last_relu", [P, J], F32, 8)
-        for u in range(len(PIECES)):
-            nt, j0, j1 = PIECES[u]
+
+        last_relu = chained("last_relu", [P, J], F32, len(PIECES))
+        for u, (nt, j0) in enumerate(PIECES):
+            edges = slice(j0, j0 + HALF)
             total = add(u, own, gated[u])
             if u == 0:
                 weighted = work.tile([P, HALF], F32, name="weighted")
-                nc.vector.scalar_tensor_tensor(weighted[:], total[:], 0.0, edge_w[:, j0:j1], ALU.max, ALU.mult)
+                nc.vector.scalar_tensor_tensor(weighted[:], total[:], 0.0, edge_w[:, edges], ALU.max, ALU.mult)
             else:
-                relu = last_relu[:, j0:j1] if u >= LAST else chained("relu%d" % u, [P, HALF], F32, u + 2)[:]
+                relu = last_relu[:, edges] if u >= LAST else chained("relu%d" % u, [P, HALF], F32, u + 2)[:]
                 nc.scalar.activation(relu, total[:], ACT.Relu)
             if u + 1 < len(PIECES):
                 own = own_product(u + 1)
-            if 0 < u < LAST:
+            if u >= LAST:
+                continue
+            if u > 0:
                 products = gate_products(u + 2)
-            if 0 < u < LAST:
                 weighted = work.tile([P, HALF], F32, name="weighted")
-                nc.gpsimd.tensor_tensor(weighted[:], relu, edge_w[:, j0:j1], ALU.mult)
-            if u < LAST:
-                place_rows(u, j0, j1, weighted[:], None)
-            if u + 2 < len(PIECES):
-                gated.append(gate(u + 2, *products))
-        place_rows(LAST + 1, 0, J, last_relu[:], edge_w[:])
+                nc.gpsimd.tensor_tensor(weighted[:], relu, edge_w[:, edges], ALU.mult)
+            nc.vector.tensor_copy(window(nt, j0, j0 + HALF), weighted[:])
+            if j0 + HALF == J:
+                store(nt)
+            gated.append(gate(u + 2, *products))
+        nc.vector.tensor_tensor(window(PIECES[LAST][0], 0, J), last_relu[:], edge_w[:], ALU.mult)
+        store(PIECES[LAST][0])

@@ -52,8 +52,8 @@ def tile_list_rgg_ownrelu_kernel(
         wo_plane = keep.tile([P, N], U8, name="wo_plane", align_bytes=64)
         identity = keep.tile([P, P], F32, name="identity")
 
-        nc.gpsimd.memset(table_plane[:], 0)
-        zeros = held.tile([P, 35 * KIB // 4], F32, name="zeros", offset=0, align_bytes=64)
+        nc.vector.memset(table_plane[:], 0)
+        zeros = held.tile([P, 43 * KIB // 4], F32, name="zeros", offset=0, align_bytes=64)
         nc.vector.memset(zeros[:, 0 : P - 1], 0.0)
         nc.vector.memset(zeros[:, P - 1 : P], 0.0)
         nc.gpsimd.affine_select(
@@ -74,20 +74,16 @@ def tile_list_rgg_ownrelu_kernel(
         nc.gpsimd.memset(w_planes[:], 0)
         wa_plane, wb_plane, wc_plane = (w_planes[:, n * N // PACK : (n + 1) * N // PACK] for n in range(3))
 
-        def load_rows(scales, quadrants, plane):
+        def load_rows(scales, places, plane, queue=nc.sync):
             rows = scales[0].bitcast(I32)
-            for q in quadrants:
-                nc.sync.dma_start(plane[32 * q : 32 * q + 4, :], rows[4 * q : 4 * (q + 1), :])
+            for r in places:
+                queue.dma_start(plane[r:P:32, :], rows[r:16:4, :])
 
-        warm = keep.tile([P, 2], F32, name="warm")
-        nc.gpsimd.memset(warm[:, 0:1], 0.0)
-        nc.scalar.activation(warm[:, 1:2], warm[:, 0:1], ACT.Sigmoid)
+        warm = keep.tile([P, 1], F32, name="warm")
+        nc.scalar.activation(warm[:], identity[:, 0:1], ACT.Sigmoid)
 
-        rows_out = [keep.tile([P, T], F32, name="rows_out0")]
-        nc.vector.memset(rows_out[0][:, 0 : T - 1], 0.0)
-        nc.vector.memset(rows_out[0][:, T - 1 : T], 0.0)
-        for n in range(1, OUT_TILES):
-            rows_out.append(held_tile("rows_out%d" % n, [P, T], F32, 26.5 + 8 * (n - 1)))
+        rows_out = [held_tile("rows_out%d" % n, [P, T], F32, 26.5 + 8 * n) for n in range(OUT_TILES)]
+        for n in range(OUT_TILES):
             nc.gpsimd.memset(rows_out[n][:], 0.0)
 
         def load_words(codes, words):
@@ -95,7 +91,8 @@ def tile_list_rgg_ownrelu_kernel(
 
         nc.sync.dma_start(dst_list[:], offs2)
         nc.sync.dma_start(src_list[:], offs)
-        load_rows(tab_scales, range(4), table_plane)
+        load_rows(tab_scales, range(2), table_plane)
+        load_rows(tab_scales, range(2, 4), table_plane, nc.scalar)
         load_words(wa_codes, wa_words)
         load_words(table_words, tab_words)
         nc.sync.dma_start(wc_codes[:].bitcast(I32), wc_words[0].bitcast(I32))

@@ -74,10 +74,10 @@ def tile_list_rgg_ownrelu_kernel(
         nc.gpsimd.memset(w_planes[:], 0)
         wa_plane, wb_plane, wc_plane = (w_planes[:, n * N // PACK : (n + 1) * N // PACK] for n in range(3))
 
-        def load_rows(scales, places, plane, queue=nc.sync):
+        def load_rows(scales, places, plane):
             rows = scales[0].bitcast(I32)
             for r in places:
-                queue.dma_start(plane[r:P:32, :], rows[r:16:4, :])
+                nc.sync.dma_start(plane[r:P:32, :], rows[r:16:4, :])
 
         warm = keep.tile([P, 1], F32, name="warm")
         nc.scalar.activation(warm[:], identity[:, 0:1], ACT.Sigmoid)
@@ -90,9 +90,8 @@ def tile_list_rgg_ownrelu_kernel(
             nc.sync.dma_start(codes[:], words[0].rearrange("p c i -> p (c i)").bitcast(I32))
 
         nc.sync.dma_start(dst_list[:], offs2)
+        load_rows(tab_scales, range(4), table_plane)
         nc.sync.dma_start(src_list[:], offs)
-        load_rows(tab_scales, range(2), table_plane)
-        load_rows(tab_scales, range(2, 4), table_plane, nc.scalar)
         load_words(wa_codes, wa_words)
         load_words(table_words, tab_words)
         nc.sync.dma_start(wc_codes[:].bitcast(I32), wc_words[0].bitcast(I32))

@@ -30,6 +30,7 @@ SUM_BANKS = (7, 2)
 PRODUCT_BANKS = (3, 0)
 FIRST_ZA_BANK = PRODUCT_BANKS[0]
 FIRST_MS_BANKS = (PRODUCT_BANKS[1], 1, 5)
+SHARE = P
 LAST_GATHER_AT = 4 * KIB
 
 
@@ -129,10 +130,14 @@ def tile_list_rgg_ownrelu_kernel(
         def quantize_wo(h):
             cols = slice(h * N // 2, (h + 1) * N // 2)
             grouped = chained("grouped%d" % h, [P, N // 2, PACK], BF16, h)[:]
+            mine = N // 2 - h * SHARE
             nc.scalar.copy(
-                grouped.rearrange("p (c m) i -> p c i m", m=LINE),
-                wo_raw[:, :, cols].rearrange("p i (c m) -> p c i m", m=LINE),
+                grouped[:, 0:mine, :].rearrange("p (c m) i -> p c i m", m=LINE),
+                wo_raw[:, :, cols.start : cols.start + mine].rearrange("p i (c m) -> p c i m", m=LINE),
             )
+            if h == 1:
+                rows = wo_raw[:, :, N - SHARE : N].rearrange("p i n -> p n i")
+                nc.gpsimd.tensor_scalar(grouped[:, mine:, :], rows, 1.0, 0.0, ALU.mult, ALU.add)
             nc.vector.quantize_mx(
                 out=wo_codes[:, cols].bitcast(FP8X4),
                 scales=wo_plane[:, cols],

@@ -184,7 +184,10 @@ def tile_list_rgg_ownrelu_kernel(
             cols = slice(nt * P, (nt + 1) * P)
             ow = bank("ow", u, PRODUCT_BANKS[u % 2])
             product(ow, u, [("dst", wo_codes[:, cols].bitcast(FP8X4), wo_plane[:, cols])])
-            own = work.tile([P, HALF], F32, name="own")
+            if u == 0:
+                own = picks.tile([P, HALF], F32, name="own0", offset=0, align_bytes=64)
+            else:
+                own = work.tile([P, HALF], F32, name="own")
             nc.scalar.copy(own[:], ow[:])
             return own
 
@@ -215,7 +218,7 @@ def tile_list_rgg_ownrelu_kernel(
         gather_scales(keep.tile([P, HALF], U8, name="src_plane0", align_bytes=64), "src", 0, HALF)
         gather_words(keep.tile([P, HALF], U32, name="src_words0", align_bytes=64), "src", 0, HALF)
         gather_words(keep.tile([P, HALF], U32, name="dst_words1", align_bytes=64), "dst", HALF, J)
-        gather_words(keep.tile([P, HALF], U32, name="src_words1", align_bytes=64), "src", HALF, J)
+        gather_words(keep.tile([P, HALF - P], U32, name="src_words1", align_bytes=64), "src", HALF, J - P)
         for h in range(2):
             quantize_wo(h)
 
@@ -233,6 +236,7 @@ def tile_list_rgg_ownrelu_kernel(
             if u == 0:
                 weighted = work.tile([P, HALF], F32, name="weighted")
                 nc.vector.scalar_tensor_tensor(weighted[:], total[:], 0.0, edge_w[:, edges], ALU.max, ALU.mult)
+                gather_words(picks.tile([P, P], U32, name="src_words2", offset=0, align_bytes=64), "src", J - P, J)
             else:
                 relu = last_relu[:, edges] if u >= LAST else chained("relu%d" % u, [P, HALF], F32, u + 2)[:]
                 nc.scalar.activation(relu, total[:], ACT.Relu)

@@ -31,6 +31,7 @@ PRODUCT_BANKS = (3, 0)
 FIRST_ZA_BANK = PRODUCT_BANKS[0]
 FIRST_MS_BANKS = (PRODUCT_BANKS[1], 1, 5)
 SHARE = P
+EARLY = 3 * J // 4
 LAST_GATHER_AT = 4 * KIB
 
 
@@ -49,7 +50,7 @@ def tile_list_rgg_ownrelu_kernel(
         src_list = keep.tile([P, J // LANES], U16, name="src_list")
         dst_list = keep.tile([P, J // LANES], U16, name="dst_list")
         table_plane = keep.tile([P, T // PACK], I32, name="table_plane", align_bytes=64)
-        wo_codes = keep.tile([P, N], U32, name="wo_codes", align_bytes=64)
+        wo_codes = keep.tile([P, N - P], U32, name="wo_codes", align_bytes=64)
         wo_plane = keep.tile([P, N], U8, name="wo_plane", align_bytes=64)
         identity = keep.tile([P, P], F32, name="identity")
 
@@ -62,6 +63,9 @@ def tile_list_rgg_ownrelu_kernel(
             pattern=[[-1, P]], channel_multiplier=1,
         )
 
+        no_bias = picks.tile([P, KIB // 4], F32, name="no_bias", offset=LAST_GATHER_AT, align_bytes=64)
+        nc.vector.memset(no_bias[:, 0:1], 0.0)
+
         def held_tile(name, shape, dtype, kib):
             return held.tile(shape, dtype, name=name, offset=int(kib * KIB), align_bytes=64)
 
@@ -69,7 +73,8 @@ def tile_list_rgg_ownrelu_kernel(
         wa_codes = held_tile("wa_codes", [P, N], I32, 8)
         wb_codes = held_tile("wb_codes", [P, N], I32, 10)
         wc_codes = held_tile("wc_codes", [P, 2 * N], U8, 12)
-        wo_raw = held_tile("wo_raw", [P, PACK, N], F32, 13)
+        wo_raw = held_tile("wo_raw", [P, PACK, N - P], F32, 13)
+        wo_late = held_tile("wo_late", [P, PACK, P], F32, 19)
         edge_w = held_tile("edge_w", [P, J], F32, 21)
         w_planes = held_tile("w_planes", [P, 3 * N // PACK], I32, 25)
         nc.gpsimd.memset(w_planes[:], 0)
@@ -87,24 +92,30 @@ def tile_list_rgg_ownrelu_kernel(
         for n in range(OUT_TILES):
             nc.gpsimd.memset(rows_out[n][:], 0.0)
 
-        def load_words(codes, words):
-            nc.sync.dma_start(codes[:], words[0].rearrange("p c i -> p (c i)").bitcast(I32))
+        def load_words(codes, words, cols=slice(0, T)):
+            nc.sync.dma_start(codes[:, cols], words[0].rearrange("p c i -> p (c i)").bitcast(I32)[:, cols])
+
+        early, late = slice(0, N - P), slice(N - P, N)
 
         nc.sync.dma_start(dst_list[:], offs2)
         load_rows(tab_scales, range(4), table_plane)
         nc.sync.dma_start(src_list[:], offs)
-        load_words(wa_codes, wa_words)
+        load_words(wa_codes, wa_words, early)
         load_words(table_words, tab_words)
         nc.sync.dma_start(wc_codes[:].bitcast(I32), wc_words[0].bitcast(I32))
         load_rows(wa_scales, range(4), wa_plane)
         load_rows(wc_scales, range(1), wc_plane)
-        nc.sync.dma_start(wo_raw[:], wo.rearrange("(p i) n -> p i n", i=PACK))
-        load_words(wb_codes, wb_words)
+        wo_rows = wo.rearrange("(p i) n -> p i n", i=PACK)
+        nc.sync.dma_start(wo_raw[:], wo_rows[:, :, early])
+        load_words(wb_codes, wb_words, early)
         load_rows(wc_scales, range(1, 3), wc_plane)
         load_rows(wb_scales, range(4), wb_plane)
         load_rows(wc_scales, range(3, 4), wc_plane)
         for h in range(2):
             nc.sync.dma_start(edge_w[:, h * HALF : (h + 1) * HALF], wgo[:, h * HALF : (h + 1) * HALF])
+        nc.sync.dma_start(wo_late[:], wo_rows[:, :, late])
+        load_words(wa_codes, wa_words, late)
+        load_words(wb_codes, wb_words, late)
 
         def entries(offsets, j0, j1):
             return offsets[:, j0 // LANES : j1 // LANES]
@@ -125,23 +136,16 @@ def tile_list_rgg_ownrelu_kernel(
             gather(words_of, table_words[:].bitcast(U32), picked, side, j0, j1)
 
         def chained(name, shape, dtype, place):
-            return chain.tile(shape, dtype, name=name, offset=place * PLACE, align_bytes=64)
+            return chain.tile(shape, dtype, name=name, offset=int(place * PLACE), align_bytes=64)
 
-        def quantize_wo(h):
-            cols = slice(h * N // 2, (h + 1) * N // 2)
-            grouped = chained("grouped%d" % h, [P, N // 2, PACK], BF16, h)[:]
-            mine = N // 2 - h * SHARE
+        def interleave(grouped, raw):
             nc.scalar.copy(
-                grouped[:, 0:mine, :].rearrange("p (c m) i -> p c i m", m=LINE),
-                wo_raw[:, :, cols.start : cols.start + mine].rearrange("p i (c m) -> p c i m", m=LINE),
+                grouped.rearrange("p (c m) i -> p c i m", m=LINE), raw.rearrange("p i (c m) -> p c i m", m=LINE)
             )
-            if h == 1:
-                rows = wo_raw[:, :, N - SHARE : N].rearrange("p i n -> p n i")
-                nc.gpsimd.tensor_scalar(grouped[:, mine:, :], rows, 1.0, 0.0, ALU.mult, ALU.add)
+
+        def quantize(codes, cols, grouped):
             nc.vector.quantize_mx(
-                out=wo_codes[:, cols].bitcast(FP8X4),
-                scales=wo_plane[:, cols],
-                in_=grouped.rearrange("p n i -> p (n i)"),
+                out=codes.bitcast(FP8X4), scales=wo_plane[:, cols], in_=grouped.rearrange("p n i -> p (n i)")
             )
 
         def bank(name, u, number):
@@ -166,10 +170,11 @@ def tile_list_rgg_ownrelu_kernel(
                 ("src", wb_codes[:, cols].bitcast(FP8X4), wb_plane.bitcast(U8)[:, cols]),
             ])
             if u == 0:
-                eta = picks.tile([P, HALF], F32, name="eta0", offset=LAST_GATHER_AT, align_bytes=64)
+                eta = work.tile([P, HALF], F32, name="eta")
+                nc.scalar.activation(eta[:], za[:], ACT.Sigmoid, bias=no_bias[:, 0:1])
             else:
                 eta = work.tile([P, HALF], F32, name="eta")
-            nc.scalar.activation(eta[:], za[:], ACT.Sigmoid)
+                nc.scalar.activation(eta[:], za[:], ACT.Sigmoid)
             ms = bank("ms", u, FIRST_MS_BANKS[u] if u < len(FIRST_MS_BANKS) else PRODUCT_BANKS[u % 2])
             wc_cols = wc_codes[:, 2 * nt * P : 2 * (nt + 1) * P].bitcast(FP4X4)
             product(ms, u, [("src", wc_cols, wc_plane.bitcast(U8)[:, cols])])
@@ -183,16 +188,18 @@ def tile_list_rgg_ownrelu_kernel(
             nt = PIECES[u][0]
             cols = slice(nt * P, (nt + 1) * P)
             ow = bank("ow", u, PRODUCT_BANKS[u % 2])
-            product(ow, u, [("dst", wo_codes[:, cols].bitcast(FP8X4), wo_plane[:, cols])])
+            product(ow, u, [("dst", wo_of[nt].bitcast(FP8X4), wo_plane[:, cols])])
             if u == 0:
                 own = picks.tile([P, HALF], F32, name="own0", offset=0, align_bytes=64)
+            elif u == 1:
+                own = chained("own1", [P, HALF], F32, 11.5)
             else:
                 own = work.tile([P, HALF], F32, name="own")
             nc.scalar.copy(own[:], ow[:])
             return own
 
         def gate(u, message, eta):
-            gated = chained("gated%d" % u, [P, HALF], F32, u)
+            gated = chained("gated%d" % u, [P, HALF], F32, 11 if u == 4 else u)
             engine = nc.vector if u == 0 else nc.gpsimd
             engine.tensor_tensor(gated[:], message[:], eta[:], ALU.mult)
             return gated
@@ -213,22 +220,32 @@ def tile_list_rgg_ownrelu_kernel(
         def store(nt):
             nc.sync.dma_start(out[nt * P : (nt + 1) * P, :], rows_out[nt % OUT_TILES][:])
 
-        gather_scales(keep.tile([P, J], U8, name="dst_plane", align_bytes=64), "dst", 0, J)
+        gather_scales(keep.tile([P, EARLY], U8, name="dst_plane0", align_bytes=64), "dst", 0, EARLY)
         gather_words(keep.tile([P, HALF], U32, name="dst_words0", align_bytes=64), "dst", 0, HALF)
         gather_scales(keep.tile([P, HALF], U8, name="src_plane0", align_bytes=64), "src", 0, HALF)
         gather_words(keep.tile([P, HALF], U32, name="src_words0", align_bytes=64), "src", 0, HALF)
         gather_words(keep.tile([P, HALF], U32, name="dst_words1", align_bytes=64), "dst", HALF, J)
         gather_words(keep.tile([P, HALF - P], U32, name="src_words1", align_bytes=64), "src", HALF, J - P)
-        for h in range(2):
-            quantize_wo(h)
+        mine = N - P - SHARE
+        grouped = chained("grouped0", [P, mine, PACK], BF16, 0)[:]
+        interleave(grouped, wo_raw[:, :, 0:mine])
+        quantize(wo_codes[:, 0:mine], slice(0, mine), grouped)
+        grouped = chained("grouped1", [P, SHARE, PACK], BF16, 1)[:]
+        rows = wo_raw[:, :, mine:].rearrange("p i n -> p n i")
+        nc.gpsimd.tensor_scalar(grouped, rows, 1.0, 0.0, ALU.mult, ALU.add)
+        quantize(wo_codes[:, mine:], slice(mine, N - P), grouped)
+        wo_of = {nt: wo_codes[:, nt * P : (nt + 1) * P] for nt in range(N // P - 1)}
 
         gated = [gate(0, *gate_products(0))]
         own = own_product(0)
         src_plane1 = picks.tile([P, HALF], U8, name="src_plane1", offset=LAST_GATHER_AT, align_bytes=64)
         gather_scales(src_plane1, "src", HALF, J)
+        dst_plane1 = picks.tile([P, J - EARLY], U8, name="dst_plane1", offset=LAST_GATHER_AT + HALF, align_bytes=64)
+        gather_scales(dst_plane1, "dst", EARLY, J)
         gated.append(gate(1, *gate_products(1)))
         products = gate_products(2)
 
+        waiting = []
         last_relu = chained("last_relu", [P, J], F32, len(PIECES))
         for u, (nt, j0) in enumerate(PIECES):
             edges = slice(j0, j0 + HALF)
@@ -246,11 +263,24 @@ def tile_list_rgg_ownrelu_kernel(
                 continue
             if u > 0:
                 products = gate_products(u + 2)
-                weighted = work.tile([P, HALF], F32, name="weighted")
+                if u == 3:
+                    weighted = chained("weighted3", [P, HALF], F32, 12)
+                else:
+                    weighted = work.tile([P, HALF], F32, name="weighted")
                 nc.gpsimd.tensor_tensor(weighted[:], relu, edge_w[:, edges], ALU.mult)
+            if u == 2:
+                wo_of[N // P - 1] = chained("wo_codes_late", [P, P], U32, u + 2)[:]
+                quantize(wo_of[N // P - 1], late, grouped)
             nc.vector.tensor_copy(window(nt, j0, j0 + HALF), weighted[:])
             if j0 + HALF == J:
                 store(nt)
-            gated.append(gate(u + 2, *products))
+            waiting.append(products)
+            if u != 2:
+                for products in waiting:
+                    gated.append(gate(len(gated), *products))
+                waiting.clear()
+            if u == 1:
+                grouped = chained("grouped_late", [P, P, PACK], BF16, 11.75)[:]
+                interleave(grouped, wo_late[:])
         nc.vector.tensor_tensor(window(PIECES[LAST][0], 0, J), last_relu[:], edge_w[:], ALU.mult)
         store(PIECES[LAST][0])

@@ -165,10 +165,11 @@ def tile_list_rgg_ownrelu_kernel(
             nt = PIECES[u][0]
             cols = slice(nt * P, (nt + 1) * P)
             za = bank("za", u, SUM_BANKS[(u - 1) % 2] if u > 0 else FIRST_ZA_BANK)
-            product(za, u, [
+            passes = [
                 ("dst", wa_codes[:, cols].bitcast(FP8X4), wa_plane.bitcast(U8)[:, cols]),
                 ("src", wb_codes[:, cols].bitcast(FP8X4), wb_plane.bitcast(U8)[:, cols]),
-            ])
+            ]
+            product(za, u, passes[::-1] if u == 2 else passes)
             if u == 0:
                 eta = work.tile([P, HALF], F32, name="eta")
                 nc.scalar.activation(eta[:], za[:], ACT.Sigmoid, bias=no_bias[:, 0:1])
@@ -245,7 +246,6 @@ def tile_list_rgg_ownrelu_kernel(
         gated.append(gate(1, *gate_products(1)))
         products = gate_products(2)
 
-        waiting = []
         last_relu = chained("last_relu", [P, J], F32, len(PIECES))
         for u, (nt, j0) in enumerate(PIECES):
             edges = slice(j0, j0 + HALF)
@@ -274,11 +274,7 @@ def tile_list_rgg_ownrelu_kernel(
             nc.vector.tensor_copy(window(nt, j0, j0 + HALF), weighted[:])
             if j0 + HALF == J:
                 store(nt)
-            waiting.append(products)
-            if u != 2:
-                for products in waiting:
-                    gated.append(gate(len(gated), *products))
-                waiting.clear()
+            gated.append(gate(u + 2, *products))
             if u == 1:
                 grouped = chained("grouped_late", [P, P, PACK], BF16, 11.75)[:]
                 interleave(grouped, wo_late[:])

@@ -32,6 +32,7 @@ FIRST_ZA_BANK = PRODUCT_BANKS[0]
 FIRST_MS_BANKS = (PRODUCT_BANKS[1], 1, 5)
 SHARE = P
 EARLY = 3 * J // 4
+FIRST_GATE = HALF - P
 LAST_GATHER_AT = 4 * KIB
 
 
@@ -65,6 +66,8 @@ def tile_list_rgg_ownrelu_kernel(
 
         no_bias = picks.tile([P, KIB // 4], F32, name="no_bias", offset=LAST_GATHER_AT, align_bytes=64)
         nc.vector.memset(no_bias[:, 0:1], 0.0)
+        unit = picks.tile([P, 8], F32, name="unit", offset=6 * KIB, align_bytes=64)
+        nc.vector.memset(unit[:, 0:1], 1.0)
 
         def held_tile(name, shape, dtype, kib):
             return held.tile(shape, dtype, name=name, offset=int(kib * KIB), align_bytes=64)
@@ -138,10 +141,12 @@ def tile_list_rgg_ownrelu_kernel(
         def chained(name, shape, dtype, place):
             return chain.tile(shape, dtype, name=name, offset=int(place * PLACE), align_bytes=64)
 
-        def interleave(grouped, raw):
-            nc.scalar.copy(
-                grouped.rearrange("p (c m) i -> p c i m", m=LINE), raw.rearrange("p i (c m) -> p c i m", m=LINE)
-            )
+        def interleave(grouped, raw, scale=None):
+            sides = grouped.rearrange("p (c m) i -> p c i m", m=LINE), raw.rearrange("p i (c m) -> p c i m", m=LINE)
+            if scale is None:
+                nc.scalar.copy(*sides)
+            else:
+                nc.scalar.activation(*sides, ACT.Copy, scale=scale)
 
         def quantize(codes, cols, grouped):
             nc.vector.quantize_mx(
@@ -151,14 +156,14 @@ def tile_list_rgg_ownrelu_kernel(
         def bank(name, u, number):
             return psum.tile([P, HALF], F32, name="%s%d" % (name, u), offset=number * PLACE)
 
-        def product(acc, u, passes):
+        def product(acc, u, passes, c0=0, c1=HALF):
             j0 = PIECES[u][1]
             for n, (side, codes, plane) in enumerate(passes):
-                for c in range(0, HALF, P):
+                for c in range(c0, c1, P):
                     nc.tensor.matmul_mx(
                         out=acc[:, c : c + P], lhsT=words_of[side][j0 + c].bitcast(FP8X4),
                         lhsT_scale=scales_of[side][j0 + c], rhs=codes, rhs_scale=plane,
-                        start=(n, c) == (0, 0), stop=(n, c) == (len(passes) - 1, HALF - P),
+                        start=(n, c) == (0, c0), stop=(n, c) == (len(passes) - 1, c1 - P),
                     )
 
         def gate_products(u):
@@ -178,9 +183,15 @@ def tile_list_rgg_ownrelu_kernel(
                 nc.scalar.activation(eta[:], za[:], ACT.Sigmoid)
             ms = bank("ms", u, FIRST_MS_BANKS[u] if u < len(FIRST_MS_BANKS) else PRODUCT_BANKS[u % 2])
             wc_cols = wc_codes[:, 2 * nt * P : 2 * (nt + 1) * P].bitcast(FP4X4)
-            product(ms, u, [("src", wc_cols, wc_plane.bitcast(U8)[:, cols])])
+            passes = [("src", wc_cols, wc_plane.bitcast(U8)[:, cols])]
             if u == 0:
-                return ms, eta
+                product(ms, u, passes, 0, FIRST_GATE)
+                rest = bank("ms_rest", u, 6)
+                product(rest, u, passes, FIRST_GATE, HALF)
+                message = keep.tile([P, HALF - FIRST_GATE], F32, name="message_rest")
+                nc.scalar.copy(message[:], rest[:, FIRST_GATE:])
+                return (ms, message), eta
+            product(ms, u, passes)
             message = work.tile([P, HALF], F32, name="message")
             nc.scalar.copy(message[:], ms[:])
             return message, eta
@@ -200,19 +211,28 @@ def tile_list_rgg_ownrelu_kernel(
             return own
 
         def gate(u, message, eta):
-            gated = chained("gated%d" % u, [P, HALF], F32, 11 if u == 4 else u)
-            engine = nc.vector if u == 0 else nc.gpsimd
-            engine.tensor_tensor(gated[:], message[:], eta[:], ALU.mult)
+            if u == 0:
+                mine = chained("gated0", [P, FIRST_GATE], F32, 0)
+                nc.vector.tensor_tensor(mine[:], message[0][:, 0:FIRST_GATE], eta[:, 0:FIRST_GATE], ALU.mult)
+                rest = chained("gated_rest", [P, HALF - FIRST_GATE], F32, 13.25 - (HALF - FIRST_GATE) / HALF)
+                nc.gpsimd.tensor_tensor(rest[:], message[1][:], eta[:, FIRST_GATE:], ALU.mult)
+                return mine, rest
+            gated = chained("gated%d" % u, [P, HALF], F32, {1: 13.25, 4: 11}.get(u, u))
+            nc.gpsimd.tensor_tensor(gated[:], message[:], eta[:], ALU.mult)
             return gated
 
         def add(u, own, gated):
             total = bank("total", u, SUM_BANKS[u % 2])
-            for n, summand in enumerate((gated, own)):
-                for c in range(0, HALF, P):
-                    nc.tensor.matmul(
-                        total[:, c : c + P], summand[:, c : c + P], identity[:], is_transpose=True,
-                        start=(n, c) == (0, 0), stop=(n, c) == (1, HALF - P),
-                    )
+            if u == 0:
+                blocks = [(c, gated[0][:, c : c + P]) for c in range(0, FIRST_GATE, P)]
+                blocks += [(c, gated[1][:, c - FIRST_GATE : c - FIRST_GATE + P]) for c in range(FIRST_GATE, HALF, P)]
+                blocks += [(c, own[:, c : c + P]) for c in range(0, HALF, P)]
+            else:
+                blocks = [(c, summand[:, c : c + P]) for summand in (gated, own) for c in range(0, HALF, P)]
+            for n, (c, block) in enumerate(blocks):
+                nc.tensor.matmul(
+                    total[:, c : c + P], block, identity[:], is_transpose=True, start=n == 0, stop=n == len(blocks) - 1
+                )
             return total
 
         def window(nt, j0, j1):
@@ -226,15 +246,17 @@ def tile_list_rgg_ownrelu_kernel(
         gather_scales(keep.tile([P, HALF], U8, name="src_plane0", align_bytes=64), "src", 0, HALF)
         gather_words(keep.tile([P, HALF], U32, name="src_words0", align_bytes=64), "src", 0, HALF)
         gather_words(keep.tile([P, HALF], U32, name="dst_words1", align_bytes=64), "dst", HALF, J)
-        gather_words(keep.tile([P, HALF - P], U32, name="src_words1", align_bytes=64), "src", HALF, J - P)
+        grouped = chained("grouped0", [P, P, PACK], BF16, 0)[:]
+        interleave(grouped, wo_raw[:, :, 0:P])
+        quantize(wo_codes[:, 0:P], slice(0, P), grouped)
+        grouped = chained("grouped1", [P, N - 2 * P, PACK], BF16, 13)[:]
         mine = N - P - SHARE
-        grouped = chained("grouped0", [P, mine, PACK], BF16, 0)[:]
-        interleave(grouped, wo_raw[:, :, 0:mine])
-        quantize(wo_codes[:, 0:mine], slice(0, mine), grouped)
-        grouped = chained("grouped1", [P, SHARE, PACK], BF16, 1)[:]
+        interleave(grouped[:, 0 : mine - P, :], wo_raw[:, :, P:mine], unit[:, 0:1])
         rows = wo_raw[:, :, mine:].rearrange("p i n -> p n i")
-        nc.gpsimd.tensor_scalar(grouped, rows, 1.0, 0.0, ALU.mult, ALU.add)
-        quantize(wo_codes[:, mine:], slice(mine, N - P), grouped)
+        nc.gpsimd.tensor_scalar(grouped[:, mine - P :, :], rows, 1.0, 0.0, ALU.mult, ALU.add)
+        src_words1 = picks.tile([P, HALF - P], U32, name="src_words1", offset=6 * KIB, align_bytes=64)
+        gather_words(src_words1, "src", HALF, J - P)
+        quantize(wo_codes[:, P:], slice(P, N - P), grouped)
         wo_of = {nt: wo_codes[:, nt * P : (nt + 1) * P] for nt in range(N // P - 1)}
 
         gated = [gate(0, *gate_products(0))]

@@ -210,6 +210,9 @@ def tile_list_rgg_ownrelu_kernel(
             nc.scalar.copy(own[:], ow[:])
             return own
 
+        def parts(u):
+            return [slice(0, HALF // 2), slice(HALF // 2, HALF)] if u == 1 else [slice(0, HALF)]
+
         def gate(u, message, eta):
             if u == 0:
                 mine = chained("gated0", [P, FIRST_GATE], F32, 0)
@@ -218,17 +221,18 @@ def tile_list_rgg_ownrelu_kernel(
                 nc.gpsimd.tensor_tensor(rest[:], message[1][:], eta[:, FIRST_GATE:], ALU.mult)
                 return mine, rest
             gated = chained("gated%d" % u, [P, HALF], F32, {1: 13.25, 4: 11}.get(u, u))
-            nc.gpsimd.tensor_tensor(gated[:], message[:], eta[:], ALU.mult)
+            for part in parts(u):
+                nc.gpsimd.tensor_tensor(gated[:, part], message[:, part], eta[:, part], ALU.mult)
             return gated
 
-        def add(u, own, gated):
-            total = bank("total", u, SUM_BANKS[u % 2])
+        def add(u, own, gated, part, number):
+            total = bank("total%d_" % part.start, u, number)
             if u == 0:
                 blocks = [(c, gated[0][:, c : c + P]) for c in range(0, FIRST_GATE, P)]
                 blocks += [(c, gated[1][:, c - FIRST_GATE : c - FIRST_GATE + P]) for c in range(FIRST_GATE, HALF, P)]
                 blocks += [(c, own[:, c : c + P]) for c in range(0, HALF, P)]
             else:
-                blocks = [(c, summand[:, c : c + P]) for summand in (gated, own) for c in range(0, HALF, P)]
+                blocks = [(c, summand[:, c : c + P]) for summand in (gated, own) for c in range(part.start, part.stop, P)]
             for n, (c, block) in enumerate(blocks):
                 nc.tensor.matmul(
                     total[:, c : c + P], block, identity[:], is_transpose=True, start=n == 0, stop=n == len(blocks) - 1
@@ -271,14 +275,17 @@ def tile_list_rgg_ownrelu_kernel(
         last_relu = chained("last_relu", [P, J], F32, len(PIECES))
         for u, (nt, j0) in enumerate(PIECES):
             edges = slice(j0, j0 + HALF)
-            total = add(u, own, gated[u])
+            numbers = [4, SUM_BANKS[1]] if u == 1 else [SUM_BANKS[u % 2]]
             if u == 0:
+                total = add(u, own, gated[u], parts(u)[0], numbers[0])
                 weighted = work.tile([P, HALF], F32, name="weighted")
                 nc.vector.scalar_tensor_tensor(weighted[:], total[:], 0.0, edge_w[:, edges], ALU.max, ALU.mult)
                 gather_words(picks.tile([P, P], U32, name="src_words2", offset=0, align_bytes=64), "src", J - P, J)
             else:
                 relu = last_relu[:, edges] if u >= LAST else chained("relu%d" % u, [P, HALF], F32, u + 2)[:]
-                nc.scalar.activation(relu, total[:], ACT.Relu)
+                for part, number in zip(parts(u), numbers):
+                    total = add(u, own, gated[u], part, number)
+                    nc.scalar.activation(relu[:, part], total[:, part], ACT.Relu)
             if u + 1 < len(PIECES):
                 own = own_product(u + 1)
             if u >= LAST:
@@ -289,7 +296,8 @@ def tile_list_rgg_ownrelu_kernel(
                     weighted = chained("weighted3", [P, HALF], F32, 12)
                 else:
                     weighted = work.tile([P, HALF], F32, name="weighted")
-                nc.gpsimd.tensor_tensor(weighted[:], relu, edge_w[:, edges], ALU.mult)
+                for part in parts(u):
+                    nc.gpsimd.tensor_tensor(weighted[:, part], relu[:, part], edge_w[:, edges][:, part], ALU.mult)
             if u == 2:
                 wo_of[N // P - 1] = chained("wo_codes_late", [P, P], U32, u + 2)[:]
                 quantize(wo_of[N // P - 1], late, grouped)

@@ -174,7 +174,7 @@ def tile_list_rgg_ownrelu_kernel(
                 ("dst", wa_codes[:, cols].bitcast(FP8X4), wa_plane.bitcast(U8)[:, cols]),
                 ("src", wb_codes[:, cols].bitcast(FP8X4), wb_plane.bitcast(U8)[:, cols]),
             ]
-            product(za, u, passes[::-1] if u == 2 else passes)
+            product(za, u, passes)
             if u == 0:
                 eta = work.tile([P, HALF], F32, name="eta")
                 nc.scalar.activation(eta[:], za[:], ACT.Sigmoid, bias=no_bias[:, 0:1])
@@ -193,7 +193,8 @@ def tile_list_rgg_ownrelu_kernel(
                 return (ms, message), eta
             product(ms, u, passes)
             message = work.tile([P, HALF], F32, name="message")
-            nc.scalar.copy(message[:], ms[:])
+            for part in parts(u):
+                nc.scalar.copy(message[:, part], ms[:, part])
             return message, eta
 
         def own_product(u):
@@ -246,7 +247,9 @@ def tile_list_rgg_ownrelu_kernel(
             nc.sync.dma_start(out[nt * P : (nt + 1) * P, :], rows_out[nt % OUT_TILES][:])
 
         gather_scales(keep.tile([P, EARLY], U8, name="dst_plane0", align_bytes=64), "dst", 0, EARLY)
-        gather_words(keep.tile([P, HALF], U32, name="dst_words0", align_bytes=64), "dst", 0, HALF)
+        for j0 in (0, HALF // 2):
+            picked = keep.tile([P, HALF // 2], U32, name="dst_words0_%d" % j0, align_bytes=64)
+            gather_words(picked, "dst", j0, j0 + HALF // 2)
         gather_scales(keep.tile([P, HALF], U8, name="src_plane0", align_bytes=64), "src", 0, HALF)
         gather_words(keep.tile([P, HALF], U32, name="src_words0", align_bytes=64), "src", 0, HALF)
         gather_words(keep.tile([P, HALF], U32, name="dst_words1", align_bytes=64), "dst", HALF, J)

@@ -103,9 +103,10 @@ def tile_list_rgg_ownrelu_kernel(
         nc.sync.dma_start(dst_list[:], offs2)
         load_rows(tab_scales, range(4), table_plane)
         nc.sync.dma_start(src_list[:], offs)
-        load_words(wa_codes, wa_words, early)
+        wc_late = (N - P) // 2
+        nc.sync.dma_start(wc_codes[:].bitcast(I32)[:, :wc_late], wc_words[0].bitcast(I32)[:, :wc_late])
         load_words(table_words, tab_words)
-        nc.sync.dma_start(wc_codes[:].bitcast(I32), wc_words[0].bitcast(I32))
+        load_words(wa_codes, wa_words, early)
         load_rows(wa_scales, range(4), wa_plane)
         load_rows(wc_scales, range(1), wc_plane)
         wo_rows = wo.rearrange("(p i) n -> p i n", i=PACK)
@@ -114,11 +115,11 @@ def tile_list_rgg_ownrelu_kernel(
         load_rows(wc_scales, range(1, 3), wc_plane)
         load_rows(wb_scales, range(4), wb_plane)
         load_rows(wc_scales, range(3, 4), wc_plane)
-        for h in range(2):
-            nc.sync.dma_start(edge_w[:, h * HALF : (h + 1) * HALF], wgo[:, h * HALF : (h + 1) * HALF])
+        nc.sync.dma_start(edge_w[:], wgo)
         nc.sync.dma_start(wo_late[:], wo_rows[:, :, late])
         load_words(wa_codes, wa_words, late)
         load_words(wb_codes, wb_words, late)
+        nc.sync.dma_start(wc_codes[:].bitcast(I32)[:, wc_late:], wc_words[0].bitcast(I32)[:, wc_late:])
 
         def entries(offsets, j0, j1):
             return offsets[:, j0 // LANES : j1 // LANES]

@@ -56,7 +56,7 @@ def tile_list_rgg_ownrelu_kernel(
         identity = keep.tile([P, P], F32, name="identity")
 
         nc.vector.memset(table_plane[:], 0)
-        zeros = held.tile([P, 43 * KIB // 4], F32, name="zeros", offset=0, align_bytes=64)
+        zeros = held.tile([P, 43 * KIB // 4], F32, name="zeros", offset=0, align_bytes=256)
         nc.vector.memset(zeros[:, 0 : P - 1], 0.0)
         nc.vector.memset(zeros[:, P - 1 : P], 0.0)
         nc.gpsimd.affine_select(
@@ -70,7 +70,7 @@ def tile_list_rgg_ownrelu_kernel(
         nc.vector.memset(unit[:, 0:1], 1.0)
 
         def held_tile(name, shape, dtype, kib):
-            return held.tile(shape, dtype, name=name, offset=int(kib * KIB), align_bytes=64)
+            return held.tile(shape, dtype, name=name, offset=int(kib * KIB), align_bytes=256)
 
         table_words = held_tile("table_words", [P, T], I32, 0)
         wa_codes = held_tile("wa_codes", [P, N], I32, 8)

from contextlib import ExitStack

import concourse.mybir as mybir

K, N, T, J = 512, 512, 2048, 1024
FLOPS = 4 * 2 * K * N * J

F32 = mybir.dt.float32
BF16 = mybir.dt.bfloat16
I32 = mybir.dt.int32
U32 = mybir.dt.uint32
U16 = mybir.dt.uint16
U8 = mybir.dt.uint8
FP8X4 = mybir.dt.float8_e4m3fn_x4
FP4X4 = mybir.dt.float4_e2m1fn_x4
ACT = mybir.ActivationFunctionType
ALU = mybir.AluOpType

P = 128
PACK = 4
LANES = 16
LINE = 4
KIB = 1024
HALF = J // 2
PLACE = 2 * KIB
PIECES = [(0, 0), (1, 0), (2, 0), (0, HALF), (1, HALF), (2, HALF), (3, 0), (3, HALF)]
LAST = len(PIECES) - 2
OUT_TILES = 3
SUM_BANKS = (7, 2)
PRODUCT_BANKS = (3, 0)
FIRST_ZA_BANK = PRODUCT_BANKS[0]
FIRST_MS_BANKS = (PRODUCT_BANKS[1], 1, 5)
SHARE = P
EARLY = 3 * J // 4
FIRST_GATE = HALF - P
LAST_GATHER_AT = 4 * KIB


def tile_list_rgg_ownrelu_kernel(
    tc, tab_words, tab_scales, wa_words, wa_scales, wb_words, wb_scales, wc_words, wc_scales, wo, wgo, offs, offs2, out
):
    nc = tc.nc
    with ExitStack() as ctx:
        keep = ctx.enter_context(tc.tile_pool(name="keep", bufs=1))
        held = ctx.enter_context(tc.tile_pool(name="held", bufs=1))
        picks = ctx.enter_context(tc.tile_pool(name="picks", bufs=1))
        work = ctx.enter_context(tc.tile_pool(name="work", bufs=len(PIECES)))
        chain = ctx.enter_context(tc.tile_pool(name="chain", bufs=1))
        psum = ctx.enter_context(tc.psum_pool(name="psum", bufs=1))

        src_list = keep.tile([P, J // LANES], U16, name="src_list")
        dst_list = keep.tile([P, J // LANES], U16, name="dst_list")
        table_plane = keep.tile([P, T // PACK], I32, name="table_plane", align_bytes=64)
        wo_codes = keep.tile([P, N - P], U32, name="wo_codes", align_bytes=64)
        wo_plane = keep.tile([P, N], U8, name="wo_plane", align_bytes=64)
        identity = keep.tile([P, P], F32, name="identity")

        nc.vector.memset(table_plane[:], 0)
        zeros = held.tile([P, 43 * KIB // 4], F32, name="zeros", offset=0, align_bytes=256)
        nc.vector.memset(zeros[:, 0 : P - 1], 0.0)
        nc.vector.memset(zeros[:, P - 1 : P], 0.0)
        nc.gpsimd.affine_select(
            out=identity[:], in_=zeros[:, 0:P], compare_op=ALU.not_equal, fill=1.0, base=0,
            pattern=[[-1, P]], channel_multiplier=1,
        )

        no_bias = picks.tile([P, KIB // 4], F32, name="no_bias", offset=LAST_GATHER_AT, align_bytes=64)
        nc.vector.memset(no_bias[:, 0:1], 0.0)
        unit = picks.tile([P, 8], F32, name="unit", offset=6 * KIB, align_bytes=64)
        nc.vector.memset(unit[:, 0:1], 1.0)

        def held_tile(name, shape, dtype, kib):
            return held.tile(shape, dtype, name=name, offset=int(kib * KIB), align_bytes=256)

        table_words = held_tile("table_words", [P, T], I32, 0)
        wa_codes = held_tile("wa_codes", [P, N], I32, 8)
        wb_codes = held_tile("wb_codes", [P, N], I32, 10)
        wc_codes = held_tile("wc_codes", [P, 2 * N], U8, 12)
        wo_raw = held_tile("wo_raw", [P, PACK, N - P], F32, 13)
        wo_late = held_tile("wo_late", [P, PACK, P], F32, 19)
        edge_w = held_tile("edge_w", [P, J], F32, 21)
        w_planes = held_tile("w_planes", [P, 3 * N // PACK], I32, 25)
        nc.gpsimd.memset(w_planes[:], 0)
        wa_plane, wb_plane, wc_plane = (w_planes[:, n * N // PACK : (n + 1) * N // PACK] for n in range(3))

        def load_rows(scales, places, plane):
            rows = scales[0].bitcast(I32)
            for r in places:
                nc.sync.dma_start(plane[r:P:32, :], rows[r:16:4, :])

        warm = keep.tile([P, 1], F32, name="warm")
        nc.scalar.activation(warm[:], identity[:, 0:1], ACT.Sigmoid)

        rows_out = [held_tile("rows_out%d" % n, [P, T], F32, 26.5 + 8 * n) for n in range(OUT_TILES)]
        for n in range(OUT_TILES):
            nc.gpsimd.memset(rows_out[n][:], 0.0)

        def load_words(codes, words, cols=slice(0, T)):
            nc.sync.dma_start(codes[:, cols], words[0].rearrange("p c i -> p (c i)").bitcast(I32)[:, cols])

        early, late = slice(0, N - P), slice(N - P, N)

        nc.sync.dma_start(dst_list[:], offs2)
        load_rows(tab_scales, range(4), table_plane)
        nc.sync.dma_start(src_list[:], offs)
        wc_late = (N - P) // 2
        nc.sync.dma_start(wc_codes[:].bitcast(I32)[:, :wc_late], wc_words[0].bitcast(I32)[:, :wc_late])
        load_words(table_words, tab_words)
        load_words(wa_codes, wa_words, early)
        load_rows(wa_scales, range(4), wa_plane)
        load_rows(wc_scales, range(1), wc_plane)
        wo_rows = wo.rearrange("(p i) n -> p i n", i=PACK)
        nc.sync.dma_start(wo_raw[:], wo_rows[:, :, early])
        load_words(wb_codes, wb_words, early)
        load_rows(wc_scales, range(1, 3), wc_plane)
        load_rows(wb_scales, range(4), wb_plane)
        load_rows(wc_scales, range(3, 4), wc_plane)
        nc.sync.dma_start(edge_w[:], wgo)
        nc.sync.dma_start(wo_late[:], wo_rows[:, :, late])
        load_words(wa_codes, wa_words, late)
        load_words(wb_codes, wb_words, late)
        nc.sync.dma_start(wc_codes[:].bitcast(I32)[:, wc_late:], wc_words[0].bitcast(I32)[:, wc_late:])

        def entries(offsets, j0, j1):
            return offsets[:, j0 // LANES : j1 // LANES]

        words_of = {"dst": {}, "src": {}}
        scales_of = {"dst": {}, "src": {}}
        lists = {"dst": dst_list, "src": src_list}

        def gather(found, window, picked, side, j0, j1):
            nc.vector.tensor_copy(picked[:], window.indirect(entries(lists[side], j0, j1)))
            for j in range(j0, j1, P):
                found[side][j] = picked[:, j - j0 : j - j0 + P]

        def gather_scales(picked, side, j0, j1):
            gather(scales_of, table_plane[:].bitcast(U8), picked, side, j0, j1)

        def gather_words(picked, side, j0, j1):
            gather(words_of, table_words[:].bitcast(U32), picked, side, j0, j1)

        def chained(name, shape, dtype, place):
            return chain.tile(shape, dtype, name=name, offset=int(place * PLACE), align_bytes=64)

        def interleave(grouped, raw, scale=None):
            sides = grouped.rearrange("p (c m) i -> p c i m", m=LINE), raw.rearrange("p i (c m) -> p c i m", m=LINE)
            if scale is None:
                nc.scalar.copy(*sides)
            else:
                nc.scalar.activation(*sides, ACT.Copy, scale=scale)

        def quantize(codes, cols, grouped):
            nc.vector.quantize_mx(
                out=codes.bitcast(FP8X4), scales=wo_plane[:, cols], in_=grouped.rearrange("p n i -> p (n i)")
            )

        def bank(name, u, number):
            return psum.tile([P, HALF], F32, name="%s%d" % (name, u), offset=number * PLACE)

        def product(acc, u, passes, c0=0, c1=HALF):
            j0 = PIECES[u][1]
            for n, (side, codes, plane) in enumerate(passes):
                for c in range(c0, c1, P):
                    nc.tensor.matmul_mx(
                        out=acc[:, c : c + P], lhsT=words_of[side][j0 + c].bitcast(FP8X4),
                        lhsT_scale=scales_of[side][j0 + c], rhs=codes, rhs_scale=plane,
                        start=(n, c) == (0, c0), stop=(n, c) == (len(passes) - 1, c1 - P),
                    )

        def gate_products(u):
            nt = PIECES[u][0]
            cols = slice(nt * P, (nt + 1) * P)
            za = bank("za", u, SUM_BANKS[(u - 1) % 2] if u > 0 else FIRST_ZA_BANK)
            passes = [
                ("dst", wa_codes[:, cols].bitcast(FP8X4), wa_plane.bitcast(U8)[:, cols]),
                ("src", wb_codes[:, cols].bitcast(FP8X4), wb_plane.bitcast(U8)[:, cols]),
            ]
            product(za, u, passes)
            if u == 0:
                eta = work.tile([P, HALF], F32, name="eta")
                nc.scalar.activation(eta[:], za[:], ACT.Sigmoid, bias=no_bias[:, 0:1])
            else:
                eta = work.tile([P, HALF], F32, name="eta")
                nc.scalar.activation(eta[:], za[:], ACT.Sigmoid)
            ms = bank("ms", u, FIRST_MS_BANKS[u] if u < len(FIRST_MS_BANKS) else PRODUCT_BANKS[u % 2])
            wc_cols = wc_codes[:, 2 * nt * P : 2 * (nt + 1) * P].bitcast(FP4X4)
            passes = [("src", wc_cols, wc_plane.bitcast(U8)[:, cols])]
            if u == 0:
                product(ms, u, passes, 0, FIRST_GATE)
                rest = bank("ms_rest", u, 6)
                product(rest, u, passes, FIRST_GATE, HALF)
                message = keep.tile([P, HALF - FIRST_GATE], F32, name="message_rest")
                nc.scalar.copy(message[:], rest[:, FIRST_GATE:])
                return (ms, message), eta
            product(ms, u, passes)
            message = work.tile([P, HALF], F32, name="message")
            for part in parts(u):
                nc.scalar.copy(message[:, part], ms[:, part])
            return message, eta

        def own_product(u):
            nt = PIECES[u][0]
            cols = slice(nt * P, (nt + 1) * P)
            ow = bank("ow", u, PRODUCT_BANKS[u % 2])
            product(ow, u, [("dst", wo_of[nt].bitcast(FP8X4), wo_plane[:, cols])])
            if u == 0:
                own = picks.tile([P, HALF], F32, name="own0", offset=0, align_bytes=64)
            elif u == 1:
                own = chained("own1", [P, HALF], F32, 11.5)
            else:
                own = work.tile([P, HALF], F32, name="own")
            nc.scalar.copy(own[:], ow[:])
            return own

        def parts(u):
            return [slice(0, HALF // 2), slice(HALF // 2, HALF)] if u == 1 else [slice(0, HALF)]

        def gate(u, message, eta):
            if u == 0:
                mine = chained("gated0", [P, FIRST_GATE], F32, 0)
                nc.vector.tensor_tensor(mine[:], message[0][:, 0:FIRST_GATE], eta[:, 0:FIRST_GATE], ALU.mult)
                rest = chained("gated_rest", [P, HALF - FIRST_GATE], F32, 13.25 - (HALF - FIRST_GATE) / HALF)
                nc.gpsimd.tensor_tensor(rest[:], message[1][:], eta[:, FIRST_GATE:], ALU.mult)
                return mine, rest
            gated = chained("gated%d" % u, [P, HALF], F32, {1: 13.25, 4: 11}.get(u, u))
            for part in parts(u):
                nc.gpsimd.tensor_tensor(gated[:, part], message[:, part], eta[:, part], ALU.mult)
            return gated

        def add(u, own, gated, part, number):
            total = bank("total%d_" % part.start, u, number)
            if u == 0:
                blocks = [(c, gated[0][:, c : c + P]) for c in range(0, FIRST_GATE, P)]
                blocks += [(c, gated[1][:, c - FIRST_GATE : c - FIRST_GATE + P]) for c in range(FIRST_GATE, HALF, P)]
                blocks += [(c, own[:, c : c + P]) for c in range(0, HALF, P)]
            else:
                blocks = [(c, summand[:, c : c + P]) for summand in (gated, own) for c in range(part.start, part.stop, P)]
            for n, (c, block) in enumerate(blocks):
                nc.tensor.matmul(
                    total[:, c : c + P], block, identity[:], is_transpose=True, start=n == 0, stop=n == len(blocks) - 1
                )
            return total

        def window(nt, j0, j1):
            return rows_out[nt % OUT_TILES][:].indirect(entries(dst_list, j0, j1))

        def store(nt):
            nc.sync.dma_start(out[nt * P : (nt + 1) * P, :], rows_out[nt % OUT_TILES][:])

        gather_scales(keep.tile([P, EARLY], U8, name="dst_plane0", align_bytes=64), "dst", 0, EARLY)
        for j0 in (0, HALF // 2):
            picked = keep.tile([P, HALF // 2], U32, name="dst_words0_%d" % j0, align_bytes=64)
            gather_words(picked, "dst", j0, j0 + HALF // 2)
        gather_scales(keep.tile([P, HALF], U8, name="src_plane0", align_bytes=64), "src", 0, HALF)
        gather_words(keep.tile([P, HALF], U32, name="src_words0", align_bytes=64), "src", 0, HALF)
        gather_words(keep.tile([P, HALF], U32, name="dst_words1", align_bytes=64), "dst", HALF, J)
        grouped = chained("grouped0", [P, P, PACK], BF16, 0)[:]
        interleave(grouped, wo_raw[:, :, 0:P])
        quantize(wo_codes[:, 0:P], slice(0, P), grouped)
        grouped = chained("grouped1", [P, N - 2 * P, PACK], BF16, 13)[:]
        mine = N - P - SHARE
        interleave(grouped[:, 0 : mine - P, :], wo_raw[:, :, P:mine], unit[:, 0:1])
        rows = wo_raw[:, :, mine:].rearrange("p i n -> p n i")
        nc.gpsimd.tensor_scalar(grouped[:, mine - P :, :], rows, 1.0, 0.0, ALU.mult, ALU.add)
        src_words1 = picks.tile([P, HALF - P], U32, name="src_words1", offset=6 * KIB, align_bytes=64)
        gather_words(src_words1, "src", HALF, J - P)
        quantize(wo_codes[:, P:], slice(P, N - P), grouped)
        wo_of = {nt: wo_codes[:, nt * P : (nt + 1) * P] for nt in range(N // P - 1)}

        gated = [gate(0, *gate_products(0))]
        own = own_product(0)
        src_plane1 = picks.tile([P, HALF], U8, name="src_plane1", offset=LAST_GATHER_AT, align_bytes=64)
        gather_scales(src_plane1, "src", HALF, J)
        dst_plane1 = picks.tile([P, J - EARLY], U8, name="dst_plane1", offset=LAST_GATHER_AT + HALF, align_bytes=64)
        gather_scales(dst_plane1, "dst", EARLY, J)
        gated.append(gate(1, *gate_products(1)))
        products = gate_products(2)

        last_relu = chained("last_relu", [P, J], F32, len(PIECES))
        for u, (nt, j0) in enumerate(PIECES):
            edges = slice(j0, j0 + HALF)
            numbers = [4, SUM_BANKS[1]] if u == 1 else [SUM_BANKS[u % 2]]
            if u == 0:
                total = add(u, own, gated[u], parts(u)[0], numbers[0])
                weighted = work.tile([P, HALF], F32, name="weighted")
                nc.vector.scalar_tensor_tensor(weighted[:], total[:], 0.0, edge_w[:, edges], ALU.max, ALU.mult)
                gather_words(picks.tile([P, P], U32, name="src_words2", offset=0, align_bytes=64), "src", J - P, J)
            else:
                relu = last_relu[:, edges] if u >= LAST else chained("relu%d" % u, [P, HALF], F32, u + 2)[:]
                for part, number in zip(parts(u), numbers):
                    total = add(u, own, gated[u], part, number)
                    nc.scalar.activation(relu[:, part], total[:, part], ACT.Relu)
            if u + 1 < len(PIECES):
                own = own_product(u + 1)
            if u >= LAST:
                continue
            if u > 0:
                products = gate_products(u + 2)
                if u == 3:
                    weighted = chained("weighted3", [P, HALF], F32, 12)
                else:
                    weighted = work.tile([P, HALF], F32, name="weighted")
                for part in parts(u):
                    nc.gpsimd.tensor_tensor(weighted[:, part], relu[:, part], edge_w[:, edges][:, part], ALU.mult)
            if u == 2:
                wo_of[N // P - 1] = chained("wo_codes_late", [P, P], U32, u + 2)[:]
                quantize(wo_of[N // P - 1], late, grouped)
            nc.vector.tensor_copy(window(nt, j0, j0 + HALF), weighted[:])
            if j0 + HALF == J:
                store(nt)
            gated.append(gate(u + 2, *products))
            if u == 1:
                grouped = chained("grouped_late", [P, P, PACK], BF16, 11.75)[:]
                interleave(grouped, wo_late[:])
        nc.vector.tensor_tensor(window(PIECES[LAST][0], 0, J), last_relu[:], edge_w[:], ALU.mult)
        store(PIECES[LAST][0])
